import numpy as np
import ml_dtypes


def mxq(x, axis, fmt="e4m3"):
    dtype, down = {"e4m3": (ml_dtypes.float8_e4m3fn, 7), "e5m2": (ml_dtypes.float8_e5m2, 14)}[fmt]
    v = np.moveaxis(np.asarray(x, np.float32).astype(ml_dtypes.bfloat16).astype(np.float64), axis, -1)
    blocks = v.reshape(v.shape[:-1] + (-1, 32))
    amax = np.abs(blocks).max(-1, keepdims=True)
    byte = np.maximum(np.where(amax > 0, np.frexp(amax)[1] - 1 + 127, 0) - down, 1)
    scale = np.exp2(byte - 127.0)
    codes = (blocks / scale).astype(np.float32).astype(dtype).astype(np.float64)
    return np.moveaxis((codes * scale).reshape(v.shape), -1, axis)


WIDE = False


def mx_kscale(k):
    if not WIDE:
        return np.ones(k)
    levels = np.array([30, -30])
    if k % 512:
        return np.exp2(np.random.permutation(np.resize(levels, k // 32))).repeat(32)
    a = np.empty((k // 512, 16))
    for p in range(k // 512):
        a[p, :8] = np.random.permutation(np.resize(levels, 8))
        for g in range(8):
            far = levels[np.abs(levels - a[p, g]) >= 10]
            a[p, g + 8] = far[np.random.randint(len(far))]
    return np.exp2(a.ravel()).repeat(32)


def f64(x):
    return np.asarray(x).astype(np.float64)


def striped(idx):
    return np.tile(idx.reshape(-1, 16).T, (8, 1)).astype(np.uint16)


def unstriped(offs):
    return offs[:16].T.reshape(-1).astype(np.int64)


E2M1 = np.array([0.0, 0.5, 1.0, 1.5, 2.0, 3.0, 4.0, 6.0, -0.0, -0.5, -1.0, -1.5, -2.0, -3.0, -4.0, -6.0])


def pack_weight(w, fmt):
    k, n = w.shape
    w = f64(np.asarray(w, np.float32).astype(ml_dtypes.bfloat16)).reshape(k // 32, 32, n)
    amax = np.abs(w).max(1)
    if fmt == "e4m3":
        byte = np.frexp(amax)[1] - 1 + 127 - 7
    elif fmt == "e5m2":
        byte = np.frexp(amax)[1] - 1 + 127 - 14
    else:
        mant, ex = np.frexp(amax / 6.0)
        byte = np.where(mant > 0.5, ex, ex - 1) + 127
    byte = np.clip(np.where(amax > 0, byte, 1), 1, 254)
    scaled = (w * np.exp2(127.0 - byte)[:, None, :]).reshape(k, n).astype(np.float32)
    by_word = np.ascontiguousarray(scaled.reshape(k // 512, 128, 4, n).transpose(0, 1, 3, 2))
    if fmt == "e4m3":
        words = by_word.astype(ml_dtypes.float8_e4m3fn).view(np.uint8)
    elif fmt == "e5m2":
        words = by_word.astype(ml_dtypes.float8_e5m2).view(np.uint8)
    else:
        c = by_word.astype(ml_dtypes.float4_e2m1fn).view(np.uint8) & 0xF
        words = (c[..., 0::2] | (c[..., 1::2] << 4)).reshape(k // 512, 128, 2 * n)
    return np.ascontiguousarray(words), np.ascontiguousarray(byte.astype(np.uint8).reshape(k // 512, 16, n))


def unpack_weight(words, scales, fmt):
    g, _, n = scales.shape
    words = np.ascontiguousarray(words).reshape(g, 128, n, -1)
    if fmt == "e4m3":
        vals = words.view(ml_dtypes.float8_e4m3fn).astype(np.float64)
    elif fmt == "e5m2":
        vals = words.view(ml_dtypes.float8_e5m2).astype(np.float64)
    else:
        nib = np.empty((g, 128, n, 4), np.uint8)
        nib[..., 0::2] = words & 0xF
        nib[..., 1::2] = words >> 4
        vals = E2M1[nib]
    vals = vals * np.repeat(np.exp2(scales.astype(np.float64) - 127.0), 8, axis=1)[..., None]
    return vals.transpose(0, 1, 3, 2).reshape(g * 512, n)


K, T, E, C, N = 128, 1024, 4, 512, 1536


def by_expert(wq, xq):
    return np.concatenate([wq[e].T @ xq[:, e * C:(e + 1) * C] for e in range(E)], axis=1)


def setup_inputs():
    n = np.random.standard_normal
    s = mx_kscale(N)[:, None]
    first = np.random.permutation(np.repeat(np.arange(E), T // E))
    second = (first + 1 + np.random.permutation(np.repeat(np.arange(E - 1), -(-T // (E - 1)))[:T])) % E
    while np.bincount(second, minlength=E).max() != T // E:
        load = np.bincount(second, minlength=E); hi, lo = int(load.argmax()), int(load.argmin())
        t = np.flatnonzero((second == hi) & (first != lo))[0]; second[t] = lo
    slot_token = np.empty(E * C, np.int64); pos = np.empty((2, T), np.int64); fill = np.zeros(E, np.int64)
    place = np.stack([np.random.permutation(C) for _ in range(E)])
    for r, deal in enumerate((first, second)):
        for t in np.random.permutation(T):
            e = deal[t]; j = e * C + place[e, fill[e]]; fill[e] += 1; slot_token[j] = t; pos[r, t] = j
    g = np.random.uniform(0.2, 0.8, T)
    w_slot = np.empty(E * C); w_slot[pos[0]] = g; w_slot[pos[1]] = 1.0 - g
    dy = pack_weight(n((N, T)) * s, "e5m2")
    return {
        "dy_words": dy[0],
        "dy_scales": dy[1],
        "w": (n((E + 1, N, K)) / np.sqrt(N) / s[None]).astype(np.float32),
        "gate": np.tile(w_slot, (K, 1)).astype(np.float32),
        "offs": striped(slot_token),
        "pos1": striped(pos[0]),
        "pos2": striped(pos[1]),
    }


def reference(dy_words, dy_scales, w, gate, offs, pos1, pos2):
    idx = unstriped(offs)
    gq = unpack_weight(dy_words, dy_scales, "e5m2")[:, idx]
    wq = mxq(f64(w), 1, "e4m3")
    ds = wq[E].T @ unpack_weight(dy_words, dy_scales, "e5m2")
    dx = f64(gate) * by_expert(wq, gq)
    return ds + dx[:, unstriped(pos1)] + dx[:, unstriped(pos2)]

@@ -1,0 +1,173 @@
+from contextlib import ExitStack
+
+import concourse.mybir as mybir
+
+K, T, E, C, N = 128, 1024, 4, 512, 1536
+FLOPS = 2 * N * K * (E * C + T)
+
+F32 = mybir.dt.float32
+BF16 = mybir.dt.bfloat16
+I32 = mybir.dt.int32
+U32 = mybir.dt.uint32
+U16 = mybir.dt.uint16
+U8 = mybir.dt.uint8
+E4M3 = mybir.dt.float8_e4m3fn_x4
+E5M2 = mybir.dt.float8_e5m2_x4
+ADD = mybir.AluOpType.add
+MULT = mybir.AluOpType.mult
+
+P = 128
+PASSES = N // 512
+S = E * C
+NE = E + 1
+CHUNKS = (256, 256, 256, 256)
+
+
+def tile_moe_bds_lin_none_kernel(tc, dy_words, dy_scales, w, gate, offs, pos1, pos2, out):
+    nc = tc.nc
+    with ExitStack() as ctx:
+        keep = ctx.enter_context(tc.tile_pool(name="keep", bufs=1))
+        psum = ctx.enter_context(tc.psum_pool(name="psum", bufs=1))
+
+        offs_t = keep.tile([P, S // 16], U16, name="offs_t")
+        pos1_t = keep.tile([P, T // 16], U16, name="pos1_t")
+        pos2_t = keep.tile([P, T // 16], U16, name="pos2_t")
+
+        packed = keep.tile([P, T], U8, name="packed", align_bytes=64)
+        shared_sc = keep.tile([P, 2 * T], U8, name="shared_sc", align_bytes=64)
+        moved = [keep.tile([P, S], U8, name=f"moved{a}", align_bytes=64) for a in (1, 2)]
+        nc.vector.memset(packed[:].bitcast(I32), 0)
+        nc.vector.memset(shared_sc[:].bitcast(I32), 0)
+        for m in moved:
+            nc.vector.memset(m[:].bitcast(I32), 0)
+
+        words = [keep.tile([P, T], I32, name=f"words{a}", align_bytes=64) for a in range(PASSES)]
+        raw = [keep.tile([P, NE * 512], F32, name=f"raw{a}", tag=f"raw{a}", align_bytes=64) for a in range(PASSES)]
+
+        def load_words(a):
+            nc.sync.dma_start(out=words[a][:], in_=dy_words[a].rearrange("p t d -> p (t d)").bitcast(I32))
+
+        def load_w(a):
+            nc.sync.dma_start(
+                out=raw[a][:].rearrange("p (e x) -> p e x", e=NE),
+                in_=w[:, 512 * a : 512 * (a + 1), :].rearrange("e (p j) k -> p e (j k)", j=4),
+            )
+
+        sc32 = dy_scales.bitcast(I32)
+        nc.sync.dma_start(offs_t[:], offs)
+        load_words(0)
+        for q in range(4):
+            nc.scalar.dma_start(out=packed[32 * q : 32 * q + 12, :].bitcast(I32), in_=sc32[:, 4 * q : 4 * q + 4, :])
+        load_w(0)
+        load_words(1)
+        load_w(1)
+        load_words(2)
+        load_w(2)
+        for q in range(4):
+            nc.scalar.dma_start(
+                out=shared_sc[32 * q : 32 * q + 4, :].bitcast(I32).rearrange("r (a t) -> r a t", a=2),
+                in_=sc32[1:3, 4 * q : 4 * q + 4, :].rearrange("a r t -> r a t"),
+            )
+
+        def gather_words(a, e, dst):
+            nc.vector.tensor_copy(dst, words[a][:].bitcast(U32).indirect(offs_t[:, 32 * e : 32 * (e + 1)]))
+
+        codes = [keep.tile([P, NE * K], U32, name=f"codes{a}", align_bytes=64) for a in range(PASSES)]
+        wsc = [keep.tile([P, NE * K], U8, name=f"wsc{a}", align_bytes=64) for a in range(PASSES)]
+
+        def quantise(a):
+            grouped = keep.tile([P, NE * 512], BF16, name=f"grouped{a}", tag=f"hold{a}", align_bytes=64)
+            for lo, hi in ((0, E), (E, NE)):
+                nc.scalar.copy(
+                    out=grouped[:, 512 * lo : 512 * hi].rearrange("p (e c i j) -> p e c j i", c=K // 4, i=4, j=4),
+                    in_=raw[a][:, 512 * lo : 512 * hi].rearrange("p (e j c i) -> p e c j i", j=4, c=K // 4, i=4),
+                )
+                nc.vector.quantize_mx(
+                    out=codes[a][:, K * lo : K * hi].bitcast(E4M3),
+                    scales=wsc[a][:, K * lo : K * hi],
+                    in_=grouped[:, 512 * lo : 512 * hi],
+                )
+
+        acc = [psum.tile([P, C], F32, name=f"acc{e}") for e in range(E)]
+        acc_sh = [psum.tile([P, 512], F32, name=f"acc_sh{h}") for h in range(T // 512)]
+
+        def multiply(a, e, dst, rhs, rhs_scale):
+            nc.tensor.matmul_mx(
+                out=dst,
+                lhsT=codes[a][:, K * e : K * (e + 1)].bitcast(E4M3),
+                lhsT_scale=wsc[a][:, K * e : K * (e + 1)],
+                rhs=rhs.bitcast(E5M2),
+                rhs_scale=rhs_scale,
+                start=(a == 0),
+                stop=(a == PASSES - 1),
+            )
+
+        def shared(a):
+            for h in range(T // 512):
+                plane = packed[:, 512 * h : 512 * (h + 1)] if a == 0 else shared_sc[:, T * (a - 1) + 512 * h : T * (a - 1) + 512 * (h + 1)]
+                multiply(a, E, acc_sh[h][:], words[a][:, 512 * h : 512 * (h + 1)], plane)
+
+        gw0 = keep.tile([P, S], U32, name="gw0", align_bytes=64)
+        for e in range(E):
+            gather_words(0, e, gw0[:, C * e : C * (e + 1)])
+        gb = keep.tile([P, S], U8, name="gb", align_bytes=64)
+        for e in range(E):
+            nc.vector.tensor_copy(gb[:, C * e : C * (e + 1)], packed[:].indirect(offs_t[:, 32 * e : 32 * (e + 1)]))
+        for a in (1, 2):
+            for q in range(4):
+                nc.sync.dma_start(
+                    out=moved[a - 1][32 * q : 32 * q + 4, :].bitcast(I32),
+                    in_=gb[32 * q + 4 * a : 32 * q + 4 * a + 4, :].bitcast(I32),
+                )
+        nc.sync.dma_start(pos1_t[:], pos1)
+        nc.sync.dma_start(pos2_t[:], pos2)
+        quantise(0)
+        for e in range(E):
+            multiply(0, e, acc[e][:], gw0[:, C * e : C * (e + 1)], gb[:, C * e : C * (e + 1)])
+        shared(0)
+        gate_t = keep.tile([P, S], F32, name="gate_t", tag="raw0", align_bytes=64)
+        nc.sync.dma_start(out=gate_t[:], in_=gate)
+
+        gw1 = keep.tile([P, S], U32, name="gw1", tag="hold0", align_bytes=64)
+        for e in range(E):
+            gather_words(1, e, gw1[:, C * e : C * (e + 1)])
+        quantise(1)
+        for e in range(E):
+            multiply(1, e, acc[e][:], gw1[:, C * e : C * (e + 1)], moved[0][:, C * e : C * (e + 1)])
+        shared(1)
+
+        gw2a = keep.tile([P, C], U32, name="gw2a", tag="hold1", align_bytes=64)
+        gather_words(2, 0, gw2a[:])
+        quantise(2)
+        shared(2)
+        ds = keep.tile([P, T], F32, name="ds")
+        for h in range(T // 512):
+            nc.scalar.copy(out=ds[:, 512 * h : 512 * (h + 1)], in_=acc_sh[h][:])
+        gw2b = keep.tile([P, S - C], U32, name="gw2b", tag="hold2", align_bytes=64)
+        multiply(2, 0, acc[0][:], gw2a[:], moved[1][:, 0:C])
+        for e in range(1, E):
+            gather_words(2, e, gw2b[:, C * (e - 1) : C * e])
+            multiply(2, e, acc[e][:], gw2b[:, C * (e - 1) : C * e], moved[1][:, C * e : C * (e + 1)])
+
+        dx = keep.tile([P, S], F32, name="dx")
+        for e in range(E):
+            nc.vector.tensor_tensor(dx[:, C * e : C * (e + 1)], acc[e][:], gate_t[:, C * e : C * (e + 1)], MULT)
+
+        starts = [sum(CHUNKS[:i]) for i in range(len(CHUNKS))]
+        part = [keep.tile([P, n], F32, name=f"part{i}") for i, n in enumerate(CHUNKS)]
+        full = [keep.tile([P, n], F32, name=f"full{i}") for i, n in enumerate(CHUNKS)]
+
+        def first(i):
+            t0, n = starts[i], CHUNKS[i]
+            nc.vector.tensor_tensor(part[i][:], dx[:].indirect(pos1_t[:, t0 // 16 : (t0 + n) // 16]), ds[:, t0 : t0 + n], ADD)
+
+        def second(i):
+            t0, n = starts[i], CHUNKS[i]
+            nc.vector.tensor_tensor(full[i][:], dx[:].indirect(pos2_t[:, t0 // 16 : (t0 + n) // 16]), part[i][:], ADD)
+            nc.sync.dma_start(out=out[:, t0 : t0 + n], in_=full[i][:])
+
+        first(0)
+        for i in range(1, len(CHUNKS)):
+            first(i)
+            second(i - 1)
+        second(len(CHUNKS) - 1)

@@ -20,6 +20,7 @@ P = 128
 PASSES = N // 512
 S = E * C
 NE = E + 1
+ROW0 = P - 16 * PASSES
 CHUNKS = (256, 256, 256, 256)
 
 
@@ -34,12 +35,13 @@ def tile_moe_bds_lin_none_kernel(tc, dy_words, dy_scales, w, gate, offs, pos1, p
         pos2_t = keep.tile([P, T // 16], U16, name="pos2_t")
 
         packed = keep.tile([P, T], U8, name="packed", align_bytes=64)
-        shared_sc = keep.tile([P, 2 * T], U8, name="shared_sc", align_bytes=64)
-        moved = [keep.tile([P, S], U8, name=f"moved{a}", align_bytes=64) for a in (1, 2)]
-        nc.vector.memset(packed[:].bitcast(I32), 0)
+        shared_sc = keep.tile([P, PASSES * T], U8, name="shared_sc", align_bytes=64)
+        moved = [keep.tile([P, S], U8, name=f"moved{a}", align_bytes=64) for a in range(PASSES)]
+        nc.vector.memset(packed[0:ROW0, :].bitcast(I32), 0)
         nc.vector.memset(shared_sc[:].bitcast(I32), 0)
-        for m in moved:
-            nc.vector.memset(m[:].bitcast(I32), 0)
+        nc.vector.memset(moved[0][:].bitcast(I32), 0)
+        for m in moved[1:]:
+            nc.gpsimd.memset(m[:].bitcast(I32), 0)
 
         words = [keep.tile([P, T], I32, name=f"words{a}", align_bytes=64) for a in range(PASSES)]
         raw = [keep.tile([P, NE * 512], F32, name=f"raw{a}", tag=f"raw{a}", align_bytes=64) for a in range(PASSES)]
@@ -55,19 +57,20 @@ def tile_moe_bds_lin_none_kernel(tc, dy_words, dy_scales, w, gate, offs, pos1, p
 
         sc32 = dy_scales.bitcast(I32)
         nc.sync.dma_start(offs_t[:], offs)
-        load_words(0)
+        rows = sc32.rearrange("a f t -> (a f) t")
+        nc.sync.dma_start(out=packed[ROW0 : ROW0 + 16, :].bitcast(I32), in_=rows[0:16, :])
+        nc.sync.dma_start(out=packed[ROW0 + 16 : P, :].bitcast(I32), in_=rows[16:48, :])
         for q in range(4):
-            nc.scalar.dma_start(out=packed[32 * q : 32 * q + 12, :].bitcast(I32), in_=sc32[:, 4 * q : 4 * q + 4, :])
+            nc.scalar.dma_start(
+                out=shared_sc[32 * q : 32 * q + 4, :].bitcast(I32).rearrange("r (a t) -> r a t", a=PASSES),
+                in_=sc32[:, 4 * q : 4 * q + 4, :].rearrange("a r t -> r a t"),
+            )
+        load_words(0)
         load_w(0)
         load_words(1)
         load_w(1)
         load_words(2)
         load_w(2)
-        for q in range(4):
-            nc.scalar.dma_start(
-                out=shared_sc[32 * q : 32 * q + 4, :].bitcast(I32).rearrange("r (a t) -> r a t", a=2),
-                in_=sc32[1:3, 4 * q : 4 * q + 4, :].rearrange("a r t -> r a t"),
-            )
 
         def gather_words(a, e, dst):
             nc.vector.tensor_copy(dst, words[a][:].bitcast(U32).indirect(offs_t[:, 32 * e : 32 * (e + 1)]))
@@ -104,26 +107,24 @@ def tile_moe_bds_lin_none_kernel(tc, dy_words, dy_scales, w, gate, offs, pos1, p
 
         def shared(a):
             for h in range(T // 512):
-                plane = packed[:, 512 * h : 512 * (h + 1)] if a == 0 else shared_sc[:, T * (a - 1) + 512 * h : T * (a - 1) + 512 * (h + 1)]
+                plane = shared_sc[:, T * a + 512 * h : T * a + 512 * (h + 1)]
                 multiply(a, E, acc_sh[h][:], words[a][:, 512 * h : 512 * (h + 1)], plane)
 
-        gw0 = keep.tile([P, S], U32, name="gw0", align_bytes=64)
-        for e in range(E):
-            gather_words(0, e, gw0[:, C * e : C * (e + 1)])
         gb = keep.tile([P, S], U8, name="gb", align_bytes=64)
         for e in range(E):
             nc.vector.tensor_copy(gb[:, C * e : C * (e + 1)], packed[:].indirect(offs_t[:, 32 * e : 32 * (e + 1)]))
-        for a in (1, 2):
+        for a in range(PASSES):
             for q in range(4):
-                nc.sync.dma_start(
-                    out=moved[a - 1][32 * q : 32 * q + 4, :].bitcast(I32),
-                    in_=gb[32 * q + 4 * a : 32 * q + 4 * a + 4, :].bitcast(I32),
-                )
+                r = ROW0 + 16 * a + 4 * q
+                nc.sync.dma_start(out=moved[a][32 * q : 32 * q + 4, :].bitcast(I32), in_=gb[r : r + 4, :].bitcast(I32))
+        gw0 = keep.tile([P, S], U32, name="gw0", align_bytes=64)
+        for e in range(E):
+            gather_words(0, e, gw0[:, C * e : C * (e + 1)])
         nc.sync.dma_start(pos1_t[:], pos1)
         nc.sync.dma_start(pos2_t[:], pos2)
         quantise(0)
         for e in range(E):
-            multiply(0, e, acc[e][:], gw0[:, C * e : C * (e + 1)], gb[:, C * e : C * (e + 1)])
+            multiply(0, e, acc[e][:], gw0[:, C * e : C * (e + 1)], moved[0][:, C * e : C * (e + 1)])
         shared(0)
         gate_t = keep.tile([P, S], F32, name="gate_t", tag="raw0", align_bytes=64)
         nc.sync.dma_start(out=gate_t[:], in_=gate)
@@ -133,7 +134,7 @@ def tile_moe_bds_lin_none_kernel(tc, dy_words, dy_scales, w, gate, offs, pos1, p
             gather_words(1, e, gw1[:, C * e : C * (e + 1)])
         quantise(1)
         for e in range(E):
-            multiply(1, e, acc[e][:], gw1[:, C * e : C * (e + 1)], moved[0][:, C * e : C * (e + 1)])
+            multiply(1, e, acc[e][:], gw1[:, C * e : C * (e + 1)], moved[1][:, C * e : C * (e + 1)])
         shared(1)
 
         gw2a = keep.tile([P, C], U32, name="gw2a", tag="hold1", align_bytes=64)
@@ -144,10 +145,10 @@ def tile_moe_bds_lin_none_kernel(tc, dy_words, dy_scales, w, gate, offs, pos1, p
         for h in range(T // 512):
             nc.scalar.copy(out=ds[:, 512 * h : 512 * (h + 1)], in_=acc_sh[h][:])
         gw2b = keep.tile([P, S - C], U32, name="gw2b", tag="hold2", align_bytes=64)
-        multiply(2, 0, acc[0][:], gw2a[:], moved[1][:, 0:C])
+        multiply(2, 0, acc[0][:], gw2a[:], moved[2][:, 0:C])
         for e in range(1, E):
             gather_words(2, e, gw2b[:, C * (e - 1) : C * e])
-            multiply(2, e, acc[e][:], gw2b[:, C * (e - 1) : C * e], moved[1][:, C * e : C * (e + 1)])
+            multiply(2, e, acc[e][:], gw2b[:, C * (e - 1) : C * e], moved[2][:, C * e : C * (e + 1)])
 
         dx = keep.tile([P, S], F32, name="dx")
         for e in range(E):

@@ -21,6 +21,7 @@ PASSES = N // 512
 S = E * C
 NE = E + 1
 ROW0 = P - 16 * PASSES
+EARLY = 2
 CHUNKS = (256, 256, 256, 256)
 
 
@@ -34,7 +35,7 @@ def tile_moe_bds_lin_none_kernel(tc, dy_words, dy_scales, w, gate, offs, pos1, p
         pos1_t = keep.tile([P, T // 16], U16, name="pos1_t")
         pos2_t = keep.tile([P, T // 16], U16, name="pos2_t")
 
-        packed = keep.tile([P, T], U8, name="packed", align_bytes=64)
+        packed = keep.tile([P, T], U8, name="packed", tag="packed", align_bytes=64)
         shared_sc = keep.tile([P, PASSES * T], U8, name="shared_sc", align_bytes=64)
         moved = [keep.tile([P, S], U8, name=f"moved{a}", align_bytes=64) for a in range(PASSES)]
         nc.vector.memset(packed[0:ROW0, :].bitcast(I32), 0)
@@ -44,20 +45,23 @@ def tile_moe_bds_lin_none_kernel(tc, dy_words, dy_scales, w, gate, offs, pos1, p
             nc.gpsimd.memset(m[:].bitcast(I32), 0)
 
         words = [keep.tile([P, T], I32, name=f"words{a}", align_bytes=64) for a in range(PASSES)]
-        raw = [keep.tile([P, NE * 512], F32, name=f"raw{a}", tag=f"raw{a}", align_bytes=64) for a in range(PASSES)]
 
         def load_words(a):
             nc.sync.dma_start(out=words[a][:], in_=dy_words[a].rearrange("p t d -> p (t d)").bitcast(I32))
 
-        def load_w(a):
+        raw = {}
+
+        def load_w(a, lo, hi, tile, col):
+            for e in range(lo, hi):
+                raw[a, e] = (tile, col + 512 * (e - lo))
             nc.sync.dma_start(
-                out=raw[a][:].rearrange("p (e x) -> p e x", e=NE),
-                in_=w[:, 512 * a : 512 * (a + 1), :].rearrange("e (p j) k -> p e (j k)", j=4),
+                out=tile[:, col : col + 512 * (hi - lo)].rearrange("p (e x) -> p e x", x=512),
+                in_=w[lo:hi, 512 * a : 512 * (a + 1), :].rearrange("e (p j) k -> p e (j k)", j=4),
             )
 
         sc32 = dy_scales.bitcast(I32)
-        nc.sync.dma_start(offs_t[:], offs)
         rows = sc32.rearrange("a f t -> (a f) t")
+        nc.sync.dma_start(offs_t[:], offs)
         nc.sync.dma_start(out=packed[ROW0 : ROW0 + 16, :].bitcast(I32), in_=rows[0:16, :])
         nc.sync.dma_start(out=packed[ROW0 + 16 : P, :].bitcast(I32), in_=rows[16:48, :])
         for q in range(4):
@@ -66,30 +70,34 @@ def tile_moe_bds_lin_none_kernel(tc, dy_words, dy_scales, w, gate, offs, pos1, p
                 in_=sc32[:, 4 * q : 4 * q + 4, :].rearrange("a r t -> r a t"),
             )
         load_words(0)
-        load_w(0)
+        raw0 = keep.tile([P, NE * 512], F32, name="raw0", tag="raw0", align_bytes=64)
+        load_w(0, 0, NE, raw0, 0)
         load_words(1)
-        load_w(1)
+        raw1 = keep.tile([P, 2 * EARLY * 512], F32, name="raw1", tag="raw1", align_bytes=64)
+        load_w(1, 0, EARLY, raw1, 0)
         load_words(2)
-        load_w(2)
+        load_w(2, 0, EARLY, raw1, EARLY * 512)
 
-        def gather_words(a, e, dst):
-            nc.vector.tensor_copy(dst, words[a][:].bitcast(U32).indirect(offs_t[:, 32 * e : 32 * (e + 1)]))
+        codes = {}
+        wsc = {}
 
-        codes = [keep.tile([P, NE * K], U32, name=f"codes{a}", align_bytes=64) for a in range(PASSES)]
-        wsc = [keep.tile([P, NE * K], U8, name=f"wsc{a}", align_bytes=64) for a in range(PASSES)]
-
-        def quantise(a):
-            grouped = keep.tile([P, NE * 512], BF16, name=f"grouped{a}", tag=f"hold{a}", align_bytes=64)
-            for lo, hi in ((0, E), (E, NE)):
+        def quantise(name, runs, tag):
+            n = sum(hi - lo for a, lo, hi in runs)
+            grouped = keep.tile([P, n * 512], BF16, name=f"grouped{name}", tag=tag, align_bytes=64)
+            code_t = keep.tile([P, n * K], U32, name=f"codes{name}", align_bytes=64)
+            scale_t = keep.tile([P, n * K], U8, name=f"wsc{name}", align_bytes=64)
+            u = 0
+            for a, lo, hi in runs:
+                tile, col = raw[a, lo]
                 nc.scalar.copy(
-                    out=grouped[:, 512 * lo : 512 * hi].rearrange("p (e c i j) -> p e c j i", c=K // 4, i=4, j=4),
-                    in_=raw[a][:, 512 * lo : 512 * hi].rearrange("p (e j c i) -> p e c j i", j=4, c=K // 4, i=4),
+                    out=grouped[:, 512 * u : 512 * (u + hi - lo)].rearrange("p (e c i j) -> p e c j i", c=K // 4, i=4, j=4),
+                    in_=tile[:, col : col + 512 * (hi - lo)].rearrange("p (e j c i) -> p e c j i", j=4, c=K // 4, i=4),
                 )
-                nc.vector.quantize_mx(
-                    out=codes[a][:, K * lo : K * hi].bitcast(E4M3),
-                    scales=wsc[a][:, K * lo : K * hi],
-                    in_=grouped[:, 512 * lo : 512 * hi],
-                )
+                for e in range(lo, hi):
+                    codes[a, e] = code_t[:, K * u : K * (u + 1)]
+                    wsc[a, e] = scale_t[:, K * u : K * (u + 1)]
+                    u = u + 1
+            nc.vector.quantize_mx(out=code_t[:].bitcast(E4M3), scales=scale_t[:], in_=grouped[:])
 
         acc = [psum.tile([P, C], F32, name=f"acc{e}") for e in range(E)]
         acc_sh = [psum.tile([P, 512], F32, name=f"acc_sh{h}") for h in range(T // 512)]
@@ -97,8 +105,8 @@ def tile_moe_bds_lin_none_kernel(tc, dy_words, dy_scales, w, gate, offs, pos1, p
         def multiply(a, e, dst, rhs, rhs_scale):
             nc.tensor.matmul_mx(
                 out=dst,
-                lhsT=codes[a][:, K * e : K * (e + 1)].bitcast(E4M3),
-                lhsT_scale=wsc[a][:, K * e : K * (e + 1)],
+                lhsT=codes[a, e].bitcast(E4M3),
+                lhsT_scale=wsc[a, e],
                 rhs=rhs.bitcast(E5M2),
                 rhs_scale=rhs_scale,
                 start=(a == 0),
@@ -107,51 +115,66 @@ def tile_moe_bds_lin_none_kernel(tc, dy_words, dy_scales, w, gate, offs, pos1, p
 
         def shared(a):
             for h in range(T // 512):
-                plane = shared_sc[:, T * a + 512 * h : T * a + 512 * (h + 1)]
-                multiply(a, E, acc_sh[h][:], words[a][:, 512 * h : 512 * (h + 1)], plane)
+                cols = slice(T * a + 512 * h, T * a + 512 * (h + 1))
+                multiply(a, E, acc_sh[h][:], words[a][:, 512 * h : 512 * (h + 1)], shared_sc[:, cols])
+
+        gw = {}
+
+        def gather_words(name, units, tag):
+            dst = keep.tile([P, C * len(units)], U32, name=f"gw{name}", tag=tag, align_bytes=64)
+            for u, (a, e) in enumerate(units):
+                gw[a, e] = dst[:, C * u : C * (u + 1)]
+                nc.vector.tensor_copy(gw[a, e], words[a][:].bitcast(U32).indirect(offs_t[:, 32 * e : 32 * (e + 1)]))
+
+        def routed(a, e):
+            multiply(a, e, acc[e][:], gw[a, e], moved[a][:, C * e : C * (e + 1)])
 
         gb = keep.tile([P, S], U8, name="gb", align_bytes=64)
         for e in range(E):
             nc.vector.tensor_copy(gb[:, C * e : C * (e + 1)], packed[:].indirect(offs_t[:, 32 * e : 32 * (e + 1)]))
+        raw2 = keep.tile([P, 2 * (NE - EARLY) * 512], F32, name="raw2", tag="packed", align_bytes=64)
         for a in range(PASSES):
             for q in range(4):
                 r = ROW0 + 16 * a + 4 * q
                 nc.sync.dma_start(out=moved[a][32 * q : 32 * q + 4, :].bitcast(I32), in_=gb[r : r + 4, :].bitcast(I32))
-        gw0 = keep.tile([P, S], U32, name="gw0", align_bytes=64)
-        for e in range(E):
-            gather_words(0, e, gw0[:, C * e : C * (e + 1)])
+            if a + 1 < PASSES:
+                load_w(a + 1, EARLY, NE, raw2, a * (NE - EARLY) * 512)
         nc.sync.dma_start(pos1_t[:], pos1)
         nc.sync.dma_start(pos2_t[:], pos2)
-        quantise(0)
+
+        gather_words("0", [(0, e) for e in range(E)], "gw0")
+        quantise("0a", [(0, 0, E)], "hold0a")
+        quantise("0b", [(0, E, NE)], "hold0")
         for e in range(E):
-            multiply(0, e, acc[e][:], gw0[:, C * e : C * (e + 1)], moved[0][:, C * e : C * (e + 1)])
+            routed(0, e)
         shared(0)
-        gate_t = keep.tile([P, S], F32, name="gate_t", tag="raw0", align_bytes=64)
+        gate_t = keep.tile([P, S], F32, name="gate_t", tag="hold0a", align_bytes=64)
         nc.sync.dma_start(out=gate_t[:], in_=gate)
 
-        gw1 = keep.tile([P, S], U32, name="gw1", tag="hold0", align_bytes=64)
-        for e in range(E):
-            gather_words(1, e, gw1[:, C * e : C * (e + 1)])
-        quantise(1)
-        for e in range(E):
-            multiply(1, e, acc[e][:], gw1[:, C * e : C * (e + 1)], moved[1][:, C * e : C * (e + 1)])
+        gather_words("1", [(1, e) for e in range(EARLY)], "raw0")
+        quantise("1", [(1, 0, EARLY), (2, 0, EARLY)], "hold1")
+        gather_words("2", [(2, e) for e in range(EARLY)], "raw1")
+        for a in (1, 2):
+            for e in range(EARLY):
+                routed(a, e)
+        quantise("2a", [(1, EARLY, NE), (2, EARLY, EARLY + 1)], "hold2a")
+        quantise("2b", [(2, EARLY + 1, NE)], "hold2")
+        gather_words("3", [(a, e) for a in (1, 2) for e in range(EARLY, E)], "packed")
         shared(1)
-
-        gw2a = keep.tile([P, C], U32, name="gw2a", tag="hold1", align_bytes=64)
-        gather_words(2, 0, gw2a[:])
-        quantise(2)
         shared(2)
+        for a in (1, 2):
+            for e in range(EARLY, E):
+                routed(a, e)
+
+        dx = keep.tile([P, S], F32, name="dx")
+        sums = keep.tile([P, EARLY * C], F32, name="sums", tag="hold2", align_bytes=64)
+        for e in range(EARLY):
+            nc.scalar.copy(out=sums[:, C * e : C * (e + 1)], in_=acc[e][:])
+            nc.gpsimd.tensor_tensor(dx[:, C * e : C * (e + 1)], sums[:, C * e : C * (e + 1)], gate_t[:, C * e : C * (e + 1)], MULT)
         ds = keep.tile([P, T], F32, name="ds")
         for h in range(T // 512):
             nc.scalar.copy(out=ds[:, 512 * h : 512 * (h + 1)], in_=acc_sh[h][:])
-        gw2b = keep.tile([P, S - C], U32, name="gw2b", tag="hold2", align_bytes=64)
-        multiply(2, 0, acc[0][:], gw2a[:], moved[2][:, 0:C])
-        for e in range(1, E):
-            gather_words(2, e, gw2b[:, C * (e - 1) : C * e])
-            multiply(2, e, acc[e][:], gw2b[:, C * (e - 1) : C * e], moved[2][:, C * e : C * (e + 1)])
-
-        dx = keep.tile([P, S], F32, name="dx")
-        for e in range(E):
+        for e in range(EARLY, E):
             nc.vector.tensor_tensor(dx[:, C * e : C * (e + 1)], acc[e][:], gate_t[:, C * e : C * (e + 1)], MULT)
 
         starts = [sum(CHUNKS[:i]) for i in range(len(CHUNKS))]

@@ -22,6 +22,7 @@ S = E * C
 NE = E + 1
 ROW0 = P - 16 * PASSES
 EARLY = 2
+WINDOW = 1408
 CHUNKS = (256, 256, 256, 256)
 
 
@@ -35,19 +36,22 @@ def tile_moe_bds_lin_none_kernel(tc, dy_words, dy_scales, w, gate, offs, pos1, p
         pos1_t = keep.tile([P, T // 16], U16, name="pos1_t")
         pos2_t = keep.tile([P, T // 16], U16, name="pos2_t")
 
-        packed = keep.tile([P, T], U8, name="packed", tag="packed", align_bytes=64)
+        packed = keep.tile([P, WINDOW], U8, name="packed", tag="packed", align_bytes=64)
         shared_sc = keep.tile([P, PASSES * T], U8, name="shared_sc", align_bytes=64)
         moved = [keep.tile([P, S], U8, name=f"moved{a}", align_bytes=64) for a in range(PASSES)]
-        nc.vector.memset(packed[0:ROW0, :].bitcast(I32), 0)
+        nc.vector.memset(packed[0:ROW0, 0:T].bitcast(I32), 0)
+        nc.vector.memset(packed[:, T:WINDOW].bitcast(I32), 0)
         nc.vector.memset(shared_sc[:].bitcast(I32), 0)
         nc.vector.memset(moved[0][:].bitcast(I32), 0)
         for m in moved[1:]:
             nc.gpsimd.memset(m[:].bitcast(I32), 0)
 
-        words = [keep.tile([P, T], I32, name=f"words{a}", align_bytes=64) for a in range(PASSES)]
+        words_t = keep.tile([P, (PASSES - 1) * T + WINDOW], I32, name="words_t", align_bytes=64)
+        nc.vector.memset(words_t[:, PASSES * T :], 0)
+        first_col = [(PASSES - 1 - a) * T for a in range(PASSES)]
 
         def load_words(a):
-            nc.sync.dma_start(out=words[a][:], in_=dy_words[a].rearrange("p t d -> p (t d)").bitcast(I32))
+            nc.sync.dma_start(out=words_t[:, first_col[a] : first_col[a] + T], in_=dy_words[a].rearrange("p t d -> p (t d)").bitcast(I32))
 
         raw = {}
 
@@ -62,8 +66,8 @@ def tile_moe_bds_lin_none_kernel(tc, dy_words, dy_scales, w, gate, offs, pos1, p
         sc32 = dy_scales.bitcast(I32)
         rows = sc32.rearrange("a f t -> (a f) t")
         nc.sync.dma_start(offs_t[:], offs)
-        nc.sync.dma_start(out=packed[ROW0 : ROW0 + 16, :].bitcast(I32), in_=rows[0:16, :])
-        nc.sync.dma_start(out=packed[ROW0 + 16 : P, :].bitcast(I32), in_=rows[16:48, :])
+        nc.sync.dma_start(out=packed[ROW0 : ROW0 + 16, 0:T].bitcast(I32), in_=rows[0:16, :])
+        nc.sync.dma_start(out=packed[ROW0 + 16 : P, 0:T].bitcast(I32), in_=rows[16:48, :])
         for q in range(4):
             nc.scalar.dma_start(
                 out=shared_sc[32 * q : 32 * q + 4, :].bitcast(I32).rearrange("r (a t) -> r a t", a=PASSES),
@@ -116,22 +120,26 @@ def tile_moe_bds_lin_none_kernel(tc, dy_words, dy_scales, w, gate, offs, pos1, p
         def shared(a):
             for h in range(T // 512):
                 cols = slice(T * a + 512 * h, T * a + 512 * (h + 1))
-                multiply(a, E, acc_sh[h][:], words[a][:, 512 * h : 512 * (h + 1)], shared_sc[:, cols])
+                multiply(a, E, acc_sh[h][:], words_t[:, first_col[a] + 512 * h : first_col[a] + 512 * (h + 1)], shared_sc[:, cols])
 
         gw = {}
 
         def gather_words(name, units, tag):
-            dst = keep.tile([P, C * len(units)], U32, name=f"gw{name}", tag=tag, align_bytes=64)
-            for u, (a, e) in enumerate(units):
-                gw[a, e] = dst[:, C * u : C * (u + 1)]
-                nc.vector.tensor_copy(gw[a, e], words[a][:].bitcast(U32).indirect(offs_t[:, 32 * e : 32 * (e + 1)]))
+            dst = keep.tile([P, C * sum(hi - lo for a, lo, hi in units)], U32, name=f"gw{name}", tag=tag, align_bytes=64)
+            u = 0
+            for a, lo, hi in units:
+                window = words_t[:, first_col[a] : first_col[a] + WINDOW].bitcast(U32)
+                nc.vector.tensor_copy(dst[:, C * u : C * (u + hi - lo)], window.indirect(offs_t[:, 32 * lo : 32 * hi]))
+                for e in range(lo, hi):
+                    gw[a, e] = dst[:, C * u : C * (u + 1)]
+                    u = u + 1
 
         def routed(a, e):
             multiply(a, e, acc[e][:], gw[a, e], moved[a][:, C * e : C * (e + 1)])
 
         gb = keep.tile([P, S], U8, name="gb", align_bytes=64)
-        for e in range(E):
-            nc.vector.tensor_copy(gb[:, C * e : C * (e + 1)], packed[:].indirect(offs_t[:, 32 * e : 32 * (e + 1)]))
+        for e in range(0, E, 2):
+            nc.vector.tensor_copy(gb[:, C * e : C * (e + 2)], packed[:].indirect(offs_t[:, 32 * e : 32 * (e + 2)]))
         raw2 = keep.tile([P, 2 * (NE - EARLY) * 512], F32, name="raw2", tag="packed", align_bytes=64)
         for a in range(PASSES):
             for q in range(4):
@@ -142,24 +150,24 @@ def tile_moe_bds_lin_none_kernel(tc, dy_words, dy_scales, w, gate, offs, pos1, p
         nc.sync.dma_start(pos1_t[:], pos1)
         nc.sync.dma_start(pos2_t[:], pos2)
 
-        gather_words("0", [(0, e) for e in range(E)], "gw0")
+        gather_words("0", [(0, 0, EARLY), (0, EARLY, E)], "gw0")
         quantise("0a", [(0, 0, E)], "hold0a")
         quantise("0b", [(0, E, NE)], "hold0")
         for e in range(E):
             routed(0, e)
         shared(0)
-        gate_t = keep.tile([P, S], F32, name="gate_t", tag="hold0a", align_bytes=64)
-        nc.sync.dma_start(out=gate_t[:], in_=gate)
 
-        gather_words("1", [(1, e) for e in range(EARLY)], "raw0")
+        gather_words("1", [(1, 0, EARLY)], "raw0")
         quantise("1", [(1, 0, EARLY), (2, 0, EARLY)], "hold1")
-        gather_words("2", [(2, e) for e in range(EARLY)], "raw1")
+        gather_words("2", [(2, 0, EARLY)], "raw1")
         for a in (1, 2):
             for e in range(EARLY):
                 routed(a, e)
         quantise("2a", [(1, EARLY, NE), (2, EARLY, EARLY + 1)], "hold2a")
         quantise("2b", [(2, EARLY + 1, NE)], "hold2")
-        gather_words("3", [(a, e) for a in (1, 2) for e in range(EARLY, E)], "packed")
+        gate_t = keep.tile([P, S], F32, name="gate_t", tag="hold2a", align_bytes=64)
+        nc.sync.dma_start(out=gate_t[:], in_=gate)
+        gather_words("3", [(1, EARLY, E), (2, EARLY, E - 1), (2, E - 1, E)], "packed")
         shared(1)
         shared(2)
         for a in (1, 2):
@@ -167,14 +175,10 @@ def tile_moe_bds_lin_none_kernel(tc, dy_words, dy_scales, w, gate, offs, pos1, p
                 routed(a, e)
 
         dx = keep.tile([P, S], F32, name="dx")
-        sums = keep.tile([P, EARLY * C], F32, name="sums", tag="hold2", align_bytes=64)
-        for e in range(EARLY):
-            nc.scalar.copy(out=sums[:, C * e : C * (e + 1)], in_=acc[e][:])
-            nc.gpsimd.tensor_tensor(dx[:, C * e : C * (e + 1)], sums[:, C * e : C * (e + 1)], gate_t[:, C * e : C * (e + 1)], MULT)
         ds = keep.tile([P, T], F32, name="ds")
         for h in range(T // 512):
             nc.scalar.copy(out=ds[:, 512 * h : 512 * (h + 1)], in_=acc_sh[h][:])
-        for e in range(EARLY, E):
+        for e in range(E):
             nc.vector.tensor_tensor(dx[:, C * e : C * (e + 1)], acc[e][:], gate_t[:, C * e : C * (e + 1)], MULT)
 
         starts = [sum(CHUNKS[:i]) for i in range(len(CHUNKS))]

@@ -21,9 +21,9 @@ PASSES = N // 512
 S = E * C
 NE = E + 1
 ROW0 = P - 16 * PASSES
-EARLY = 2
+LATE = 2
 WINDOW = 1408
-CHUNKS = (256, 256, 256, 256)
+CHUNKS = (512, 256, 128, 128)
 
 
 def tile_moe_bds_lin_none_kernel(tc, dy_words, dy_scales, w, gate, offs, pos1, pos2, out):
@@ -36,7 +36,7 @@ def tile_moe_bds_lin_none_kernel(tc, dy_words, dy_scales, w, gate, offs, pos1, p
         pos1_t = keep.tile([P, T // 16], U16, name="pos1_t")
         pos2_t = keep.tile([P, T // 16], U16, name="pos2_t")
 
-        packed = keep.tile([P, WINDOW], U8, name="packed", tag="packed", align_bytes=64)
+        packed = keep.tile([P, WINDOW], U8, name="packed", align_bytes=64)
         shared_sc = keep.tile([P, PASSES * T], U8, name="shared_sc", align_bytes=64)
         moved = [keep.tile([P, S], U8, name=f"moved{a}", align_bytes=64) for a in range(PASSES)]
         nc.vector.memset(packed[0:ROW0, 0:T].bitcast(I32), 0)
@@ -55,11 +55,12 @@ def tile_moe_bds_lin_none_kernel(tc, dy_words, dy_scales, w, gate, offs, pos1, p
 
         raw = {}
 
-        def load_w(a, lo, hi, tile, col):
+        def load_w(a, lo, hi):
+            tile = keep.tile([P, (hi - lo) * 512], F32, name=f"raw{a}_{lo}", tag=f"raw{a}_{lo}", align_bytes=64)
             for e in range(lo, hi):
-                raw[a, e] = (tile, col + 512 * (e - lo))
+                raw[a, e] = (tile, 512 * (e - lo))
             nc.sync.dma_start(
-                out=tile[:, col : col + 512 * (hi - lo)].rearrange("p (e x) -> p e x", x=512),
+                out=tile[:].rearrange("p (e x) -> p e x", x=512),
                 in_=w[lo:hi, 512 * a : 512 * (a + 1), :].rearrange("e (p j) k -> p e (j k)", j=4),
             )
 
@@ -73,14 +74,12 @@ def tile_moe_bds_lin_none_kernel(tc, dy_words, dy_scales, w, gate, offs, pos1, p
                 out=shared_sc[32 * q : 32 * q + 4, :].bitcast(I32).rearrange("r (a t) -> r a t", a=PASSES),
                 in_=sc32[:, 4 * q : 4 * q + 4, :].rearrange("a r t -> r a t"),
             )
+        load_w(0, 0, LATE)
         load_words(0)
-        raw0 = keep.tile([P, NE * 512], F32, name="raw0", tag="raw0", align_bytes=64)
-        load_w(0, 0, NE, raw0, 0)
+        load_w(0, LATE, NE)
         load_words(1)
-        raw1 = keep.tile([P, 2 * EARLY * 512], F32, name="raw1", tag="raw1", align_bytes=64)
-        load_w(1, 0, EARLY, raw1, 0)
+        load_w(1, LATE, NE)
         load_words(2)
-        load_w(2, 0, EARLY, raw1, EARLY * 512)
 
         codes = {}
         wsc = {}
@@ -126,6 +125,9 @@ def tile_moe_bds_lin_none_kernel(tc, dy_words, dy_scales, w, gate, offs, pos1, p
 
         def gather_words(name, units, tag):
             dst = keep.tile([P, C * sum(hi - lo for a, lo, hi in units)], U32, name=f"gw{name}", tag=tag, align_bytes=64)
+            gather_into(dst[:], units)
+
+        def gather_into(dst, units):
             u = 0
             for a, lo, hi in units:
                 window = words_t[:, first_col[a] : first_col[a] + WINDOW].bitcast(U32)
@@ -140,62 +142,73 @@ def tile_moe_bds_lin_none_kernel(tc, dy_words, dy_scales, w, gate, offs, pos1, p
         gb = keep.tile([P, S], U8, name="gb", align_bytes=64)
         for e in range(0, E, 2):
             nc.vector.tensor_copy(gb[:, C * e : C * (e + 2)], packed[:].indirect(offs_t[:, 32 * e : 32 * (e + 2)]))
-        raw2 = keep.tile([P, 2 * (NE - EARLY) * 512], F32, name="raw2", tag="packed", align_bytes=64)
-        for a in range(PASSES):
+
+        def move_scales(a):
             for q in range(4):
                 r = ROW0 + 16 * a + 4 * q
                 nc.sync.dma_start(out=moved[a][32 * q : 32 * q + 4, :].bitcast(I32), in_=gb[r : r + 4, :].bitcast(I32))
-            if a + 1 < PASSES:
-                load_w(a + 1, EARLY, NE, raw2, a * (NE - EARLY) * 512)
+
+        move_scales(0)
+        load_w(2, LATE, E)
+        move_scales(1)
+        load_w(1, 0, LATE)
+        move_scales(2)
+        load_w(2, 0, LATE)
+        load_w(2, E, NE)
         nc.sync.dma_start(pos1_t[:], pos1)
         nc.sync.dma_start(pos2_t[:], pos2)
+        gate_t = keep.tile([P, S], F32, name="gate_t", align_bytes=64)
+        nc.sync.dma_start(out=gate_t[:], in_=gate)
 
-        gather_words("0", [(0, 0, EARLY), (0, EARLY, E)], "gw0")
-        quantise("0a", [(0, 0, E)], "hold0a")
-        quantise("0b", [(0, E, NE)], "hold0")
+        gather_words("0", [(0, LATE, E), (0, 0, LATE)], "gw0")
+        quantise("0a", [(0, 0, LATE), (0, LATE, E)], "g0a")
+        quantise("0b", [(0, E, NE)], "g0b")
         for e in range(E):
             routed(0, e)
         shared(0)
 
-        gather_words("1", [(1, 0, EARLY)], "raw0")
-        quantise("1", [(1, 0, EARLY), (2, 0, EARLY)], "hold1")
-        gather_words("2", [(2, 0, EARLY)], "raw1")
-        for a in (1, 2):
-            for e in range(EARLY):
-                routed(a, e)
-        quantise("2a", [(1, EARLY, NE), (2, EARLY, EARLY + 1)], "hold2a")
-        quantise("2b", [(2, EARLY + 1, NE)], "hold2")
-        gate_t = keep.tile([P, S], F32, name="gate_t", tag="hold2a", align_bytes=64)
-        nc.sync.dma_start(out=gate_t[:], in_=gate)
-        gather_words("3", [(1, EARLY, E), (2, EARLY, E - 1), (2, E - 1, E)], "packed")
+        gather_words("1a", [(1, LATE, E)], "raw1_2")
+        quantise("1a", [(1, LATE, E)], "g1a")
+        quantise("1b", [(1, E, NE)], "g1b")
+        for e in range(LATE, E):
+            routed(1, e)
         shared(1)
+        ahead = keep.tile([P, (E - LATE) * C], U32, name="ahead", tag="raw2_2", align_bytes=64)
+        gather_into(ahead[:, 0:C], [(2, LATE, LATE + 1)])
+        quantise("2a", [(2, LATE, E)], "g2a")
+        gather_into(ahead[:, C:], [(2, LATE + 1, E)])
+        routed(2, LATE)
+        routed(2, LATE + 1)
+        quantise("3", [(1, 0, LATE), (2, 0, LATE)], "g3")
+        quantise("2b", [(2, E, NE)], "g2b")
+        last = keep.tile([P, 2 * LATE * C], U32, name="last", tag="raw2_4", align_bytes=64)
+        gather_into(last[:], [(a, e, e + 1) for a in (1, 2) for e in range(LATE)])
+        routed(1, 0)
         shared(2)
-        for a in (1, 2):
-            for e in range(EARLY, E):
-                routed(a, e)
+        routed(1, 1)
+        for e in range(LATE):
+            routed(2, e)
 
         dx = keep.tile([P, S], F32, name="dx")
-        ds = keep.tile([P, T], F32, name="ds")
+        copied = keep.tile([P, (E - LATE) * C + T], F32, name="copied", tag="g2b", align_bytes=64)
+        sums = copied[:, T:]
+        for e in range(LATE, E):
+            cols = slice(C * (e - LATE), C * (e - LATE + 1))
+            nc.scalar.copy(out=sums[:, cols], in_=acc[e][:])
+            nc.gpsimd.tensor_tensor(dx[:, C * e : C * (e + 1)], sums[:, cols], gate_t[:, C * e : C * (e + 1)], MULT)
+        ds = copied[:, 0:T]
         for h in range(T // 512):
             nc.scalar.copy(out=ds[:, 512 * h : 512 * (h + 1)], in_=acc_sh[h][:])
-        for e in range(E):
+        for e in range(LATE):
             nc.vector.tensor_tensor(dx[:, C * e : C * (e + 1)], acc[e][:], gate_t[:, C * e : C * (e + 1)], MULT)
 
-        starts = [sum(CHUNKS[:i]) for i in range(len(CHUNKS))]
-        part = [keep.tile([P, n], F32, name=f"part{i}") for i, n in enumerate(CHUNKS)]
-        full = [keep.tile([P, n], F32, name=f"full{i}") for i, n in enumerate(CHUNKS)]
-
-        def first(i):
-            t0, n = starts[i], CHUNKS[i]
-            nc.vector.tensor_tensor(part[i][:], dx[:].indirect(pos1_t[:, t0 // 16 : (t0 + n) // 16]), ds[:, t0 : t0 + n], ADD)
-
-        def second(i):
-            t0, n = starts[i], CHUNKS[i]
-            nc.vector.tensor_tensor(full[i][:], dx[:].indirect(pos2_t[:, t0 // 16 : (t0 + n) // 16]), part[i][:], ADD)
-            nc.sync.dma_start(out=out[:, t0 : t0 + n], in_=full[i][:])
-
-        first(0)
-        for i in range(1, len(CHUNKS)):
-            first(i)
-            second(i - 1)
-        second(len(CHUNKS) - 1)
+        part = keep.tile([P, T], F32, name="part")
+        for h in range(T // 512):
+            cols = slice(512 * h, 512 * (h + 1))
+            nc.vector.tensor_tensor(part[:, cols], dx[:].indirect(pos1_t[:, 32 * h : 32 * (h + 1)]), ds[:, cols], ADD)
+        t0 = 0
+        for i, n in enumerate(CHUNKS):
+            full = keep.tile([P, n], F32, name=f"full{i}")
+            nc.vector.tensor_tensor(full[:], dx[:].indirect(pos2_t[:, t0 // 16 : (t0 + n) // 16]), part[:, t0 : t0 + n], ADD)
+            nc.sync.dma_start(out=out[:, t0 : t0 + n], in_=full[:])
+            t0 = t0 + n

@@ -23,6 +23,8 @@ NE = E + 1
 ROW0 = P - 16 * PASSES
 LATE = 2
 WINDOW = 1408
+WIDE = 2048
+TAIL = 192
 CHUNKS = (512, 256, 128, 128)
 
 
@@ -41,13 +43,12 @@ def tile_moe_bds_lin_none_kernel(tc, dy_words, dy_scales, w, gate, offs, pos1, p
         moved = [keep.tile([P, S], U8, name=f"moved{a}", align_bytes=64) for a in range(PASSES)]
         nc.vector.memset(packed[0:ROW0, 0:T].bitcast(I32), 0)
         nc.vector.memset(packed[:, T:WINDOW].bitcast(I32), 0)
-        nc.vector.memset(shared_sc[:].bitcast(I32), 0)
-        nc.vector.memset(moved[0][:].bitcast(I32), 0)
-        for m in moved[1:]:
+        nc.gpsimd.memset(shared_sc[:].bitcast(I32), 0)
+        for m in moved:
             nc.gpsimd.memset(m[:].bitcast(I32), 0)
 
-        words_t = keep.tile([P, (PASSES - 1) * T + WINDOW], I32, name="words_t", align_bytes=64)
-        nc.vector.memset(words_t[:, PASSES * T :], 0)
+        words_t = keep.tile([P, (PASSES - 1) * T + WIDE], I32, name="words_t", align_bytes=64)
+        nc.gpsimd.memset(words_t[:, PASSES * T :], 0)
         first_col = [(PASSES - 1 - a) * T for a in range(PASSES)]
 
         def load_words(a):
@@ -123,18 +124,15 @@ def tile_moe_bds_lin_none_kernel(tc, dy_words, dy_scales, w, gate, offs, pos1, p
 
         gw = {}
 
-        def gather_words(name, units, tag):
-            dst = keep.tile([P, C * sum(hi - lo for a, lo, hi in units)], U32, name=f"gw{name}", tag=tag, align_bytes=64)
-            gather_into(dst[:], units)
+        def gather(dst, a, lo, hi, width):
+            window = words_t[:, first_col[a] : first_col[a] + width].bitcast(U32)
+            nc.vector.tensor_copy(dst, window.indirect(offs_t[:, lo // 16 : hi // 16]))
 
-        def gather_into(dst, units):
-            u = 0
-            for a, lo, hi in units:
-                window = words_t[:, first_col[a] : first_col[a] + WINDOW].bitcast(U32)
-                nc.vector.tensor_copy(dst[:, C * u : C * (u + hi - lo)], window.indirect(offs_t[:, 32 * lo : 32 * hi]))
-                for e in range(lo, hi):
-                    gw[a, e] = dst[:, C * u : C * (u + 1)]
-                    u = u + 1
+        def gather_words(a, lo, hi, tag):
+            dst = keep.tile([P, C * (hi - lo)], U32, name=f"gw{a}_{lo}", tag=tag, align_bytes=64)
+            gather(dst[:], a, C * lo, C * hi, WIDE)
+            for e in range(lo, hi):
+                gw[a, e] = dst[:, C * (e - lo) : C * (e - lo + 1)]
 
         def routed(a, e):
             multiply(a, e, acc[e][:], gw[a, e], moved[a][:, C * e : C * (e + 1)])
@@ -160,47 +158,54 @@ def tile_moe_bds_lin_none_kernel(tc, dy_words, dy_scales, w, gate, offs, pos1, p
         gate_t = keep.tile([P, S], F32, name="gate_t", align_bytes=64)
         nc.sync.dma_start(out=gate_t[:], in_=gate)
 
-        gather_words("0", [(0, LATE, E), (0, 0, LATE)], "gw0")
-        quantise("0a", [(0, 0, LATE), (0, LATE, E)], "g0a")
-        quantise("0b", [(0, E, NE)], "g0b")
-        for e in range(E):
+        gather_words(0, 1, E, "gw0")
+        quantise("0", [(0, 0, LATE), (0, LATE, E)], "g0")
+        for e in range(1, E):
             routed(0, e)
-        shared(0)
 
-        gather_words("1a", [(1, LATE, E)], "raw1_2")
-        quantise("1a", [(1, LATE, E)], "g1a")
-        quantise("1b", [(1, E, NE)], "g1b")
+        gather_words(1, 1, E, "gw1")
+        quantise("1", [(0, E, NE), (1, LATE, NE)], "g1")
         for e in range(LATE, E):
             routed(1, e)
+        shared(0)
         shared(1)
-        ahead = keep.tile([P, (E - LATE) * C], U32, name="ahead", tag="raw2_2", align_bytes=64)
-        gather_into(ahead[:, 0:C], [(2, LATE, LATE + 1)])
-        quantise("2a", [(2, LATE, E)], "g2a")
-        gather_into(ahead[:, C:], [(2, LATE + 1, E)])
-        routed(2, LATE)
-        routed(2, LATE + 1)
-        quantise("3", [(1, 0, LATE), (2, 0, LATE)], "g3")
-        quantise("2b", [(2, E, NE)], "g2b")
-        last = keep.tile([P, 2 * LATE * C], U32, name="last", tag="raw2_4", align_bytes=64)
-        gather_into(last[:], [(a, e, e + 1) for a in (1, 2) for e in range(LATE)])
-        routed(1, 0)
-        shared(2)
-        routed(1, 1)
-        for e in range(LATE):
-            routed(2, e)
-
-        dx = keep.tile([P, S], F32, name="dx")
-        copied = keep.tile([P, (E - LATE) * C + T], F32, name="copied", tag="g2b", align_bytes=64)
-        sums = copied[:, T:]
+        gather_words(2, LATE, E, "raw2_2")
+        quantise("2", [(2, LATE, E)], "g2")
         for e in range(LATE, E):
-            cols = slice(C * (e - LATE), C * (e - LATE + 1))
-            nc.scalar.copy(out=sums[:, cols], in_=acc[e][:])
-            nc.gpsimd.tensor_tensor(dx[:, C * e : C * (e + 1)], sums[:, cols], gate_t[:, C * e : C * (e + 1)], MULT)
-        ds = copied[:, 0:T]
+            routed(2, e)
+        quantise("3", [(1, 0, LATE), (2, 0, LATE)], "g3")
+        routed(1, 1)
+        quantise("4", [(2, E, NE)], "g4")
+        last = keep.tile([P, 4 * C], U32, name="last", tag="raw2_4", align_bytes=64)
+        head = C - TAIL
+        gw[2, 1] = last[:, 0:C]
+        gather(gw[2, 1], 2, C, 2 * C, T)
+        shared(2)
+        routed(2, 1)
+        pass0 = last[:, C : 2 * C]
+        pass1 = last[:, 2 * C + head : 3 * C + head]
+        gather(pass0, 0, 0, C, T)
+        gather(pass1, 1, 0, C, T)
+        gather(last[:, 2 * C : 2 * C + head], 2, 0, head, T)
+        gather(last[:, 3 * C + head : 4 * C], 2, head, C, T)
+        acc_tail = psum.tile([P, C], F32, name="acc_tail")
+        for a, rhs in enumerate((pass0, pass1)):
+            multiply(a, 0, acc[0][:], rhs, moved[a][:, 0:C])
+            multiply(a, 0, acc_tail[:], rhs, moved[a][:, 0:C])
+        multiply(2, 0, acc[0][:], last[:, 2 * C : 3 * C], moved[2][:, 0:C])
+        multiply(2, 0, acc_tail[:], last[:, 3 * C : 4 * C], moved[2][:, 0:C])
+
+        dx = keep.tile([P, S], F32, name="dx", tag="g4", align_bytes=64)
+        copied = keep.tile([P, S + T], F32, name="copied", tag="g3", align_bytes=64)
+        ds = copied[:, S:]
+        for e in (2, 3, 1):
+            cols = slice(C * e, C * (e + 1))
+            nc.scalar.copy(out=copied[:, cols], in_=acc[e][:])
+            nc.gpsimd.tensor_tensor(dx[:, cols], copied[:, cols], gate_t[:, cols], MULT)
         for h in range(T // 512):
             nc.scalar.copy(out=ds[:, 512 * h : 512 * (h + 1)], in_=acc_sh[h][:])
-        for e in range(LATE):
-            nc.vector.tensor_tensor(dx[:, C * e : C * (e + 1)], acc[e][:], gate_t[:, C * e : C * (e + 1)], MULT)
+        nc.vector.tensor_tensor(dx[:, 0:head], acc[0][:, 0:head], gate_t[:, 0:head], MULT)
+        nc.vector.tensor_tensor(dx[:, head:C], acc_tail[:, head:C], gate_t[:, head:C], MULT)
 
         part = keep.tile([P, T], F32, name="part")
         for h in range(T // 512):

@@ -25,6 +25,7 @@ LATE = 2
 WINDOW = 1408
 WIDE = 2048
 TAIL = 192
+FILL = 256
 CHUNKS = (512, 256, 128, 128)
 
 
@@ -43,12 +44,12 @@ def tile_moe_bds_lin_none_kernel(tc, dy_words, dy_scales, w, gate, offs, pos1, p
         moved = [keep.tile([P, S], U8, name=f"moved{a}", align_bytes=64) for a in range(PASSES)]
         nc.vector.memset(packed[0:ROW0, 0:T].bitcast(I32), 0)
         nc.vector.memset(packed[:, T:WINDOW].bitcast(I32), 0)
-        nc.gpsimd.memset(shared_sc[:].bitcast(I32), 0)
+        nc.vector.memset(shared_sc[:].bitcast(I32), 0)
         for m in moved:
-            nc.gpsimd.memset(m[:].bitcast(I32), 0)
+            nc.vector.memset(m[:].bitcast(I32), 0)
 
-        words_t = keep.tile([P, (PASSES - 1) * T + WIDE], I32, name="words_t", align_bytes=64)
-        nc.gpsimd.memset(words_t[:, PASSES * T :], 0)
+        words_t = keep.tile([P, (PASSES - 1) * T + WINDOW], I32, name="words_t", align_bytes=64)
+        nc.vector.memset(words_t[:, PASSES * T :], 0)
         first_col = [(PASSES - 1 - a) * T for a in range(PASSES)]
 
         def load_words(a):
@@ -75,10 +76,10 @@ def tile_moe_bds_lin_none_kernel(tc, dy_words, dy_scales, w, gate, offs, pos1, p
                 out=shared_sc[32 * q : 32 * q + 4, :].bitcast(I32).rearrange("r (a t) -> r a t", a=PASSES),
                 in_=sc32[:, 4 * q : 4 * q + 4, :].rearrange("a r t -> r a t"),
             )
-        load_w(0, 0, LATE)
+        load_w(0, 1, NE)
         load_words(0)
-        load_w(0, LATE, NE)
         load_words(1)
+        load_w(0, 0, 1)
         load_w(1, LATE, NE)
         load_words(2)
 
@@ -128,9 +129,11 @@ def tile_moe_bds_lin_none_kernel(tc, dy_words, dy_scales, w, gate, offs, pos1, p
             window = words_t[:, first_col[a] : first_col[a] + width].bitcast(U32)
             nc.vector.tensor_copy(dst, window.indirect(offs_t[:, lo // 16 : hi // 16]))
 
-        def gather_words(a, lo, hi, tag):
+        def gather_words(a, cuts, width, tag):
+            lo, hi = cuts[0], cuts[-1]
             dst = keep.tile([P, C * (hi - lo)], U32, name=f"gw{a}_{lo}", tag=tag, align_bytes=64)
-            gather(dst[:], a, C * lo, C * hi, WIDE)
+            for x, y in zip(cuts, cuts[1:]):
+                gather(dst[:, C * (x - lo) : C * (y - lo)], a, C * x, C * y, width)
             for e in range(lo, hi):
                 gw[a, e] = dst[:, C * (e - lo) : C * (e - lo + 1)]
 
@@ -158,18 +161,18 @@ def tile_moe_bds_lin_none_kernel(tc, dy_words, dy_scales, w, gate, offs, pos1, p
         gate_t = keep.tile([P, S], F32, name="gate_t", align_bytes=64)
         nc.sync.dma_start(out=gate_t[:], in_=gate)
 
-        gather_words(0, 1, E, "gw0")
-        quantise("0", [(0, 0, LATE), (0, LATE, E)], "g0")
+        gather_words(0, (1, LATE, E), WINDOW, "gw0")
+        quantise("0", [(0, 1, NE)], "g0")
         for e in range(1, E):
             routed(0, e)
+        shared(0)
 
-        gather_words(1, 1, E, "gw1")
-        quantise("1", [(0, E, NE), (1, LATE, NE)], "g1")
+        gather_words(1, (1, E), WIDE, "raw0_0")
+        quantise("1", [(0, 0, 1), (1, LATE, NE)], "g1")
         for e in range(LATE, E):
             routed(1, e)
-        shared(0)
         shared(1)
-        gather_words(2, LATE, E, "raw2_2")
+        gather_words(2, (LATE, E), WINDOW, "raw2_2")
         quantise("2", [(2, LATE, E)], "g2")
         for e in range(LATE, E):
             routed(2, e)
@@ -198,12 +201,14 @@ def tile_moe_bds_lin_none_kernel(tc, dy_words, dy_scales, w, gate, offs, pos1, p
         dx = keep.tile([P, S], F32, name="dx", tag="g4", align_bytes=64)
         copied = keep.tile([P, S + T], F32, name="copied", tag="g3", align_bytes=64)
         ds = copied[:, S:]
-        for e in (2, 3, 1):
-            cols = slice(C * e, C * (e + 1))
-            nc.scalar.copy(out=copied[:, cols], in_=acc[e][:])
+        for lo, hi in ((2 * C, 3 * C), (3 * C, 4 * C), (C + FILL, 2 * C)):
+            cols = slice(lo, hi)
+            e = lo // C
+            nc.scalar.copy(out=copied[:, cols], in_=acc[e][:, lo - C * e : hi - C * e])
             nc.gpsimd.tensor_tensor(dx[:, cols], copied[:, cols], gate_t[:, cols], MULT)
         for h in range(T // 512):
             nc.scalar.copy(out=ds[:, 512 * h : 512 * (h + 1)], in_=acc_sh[h][:])
+        nc.vector.tensor_tensor(dx[:, C : C + FILL], acc[1][:, 0:FILL], gate_t[:, C : C + FILL], MULT)
         nc.vector.tensor_tensor(dx[:, 0:head], acc[0][:, 0:head], gate_t[:, 0:head], MULT)
         nc.vector.tensor_tensor(dx[:, head:C], acc_tail[:, head:C], gate_t[:, head:C], MULT)
 

@@ -1,6 +1,7 @@
 from contextlib import ExitStack
 
 import concourse.mybir as mybir
+from concourse.masks import make_identity
 
 K, T, E, C, N = 128, 1024, 4, 512, 1536
 FLOPS = 2 * N * K * (E * C + T)
@@ -15,17 +16,15 @@ E4M3 = mybir.dt.float8_e4m3fn_x4
 E5M2 = mybir.dt.float8_e5m2_x4
 ADD = mybir.AluOpType.add
 MULT = mybir.AluOpType.mult
+COPY = mybir.ActivationFunctionType.Copy
 
 P = 128
 PASSES = N // 512
 S = E * C
-NE = E + 1
+SHARED = E
 ROW0 = P - 16 * PASSES
-LATE = 2
 WINDOW = 1408
-WIDE = 2048
 TAIL = 192
-FILL = 256
 CHUNKS = (512, 256, 128, 128)
 
 
@@ -39,73 +38,95 @@ def tile_moe_bds_lin_none_kernel(tc, dy_words, dy_scales, w, gate, offs, pos1, p
         pos1_t = keep.tile([P, T // 16], U16, name="pos1_t")
         pos2_t = keep.tile([P, T // 16], U16, name="pos2_t")
 
-        packed = keep.tile([P, WINDOW], U8, name="packed", align_bytes=64)
-        shared_sc = keep.tile([P, PASSES * T], U8, name="shared_sc", align_bytes=64)
-        moved = [keep.tile([P, S], U8, name=f"moved{a}", align_bytes=64) for a in range(PASSES)]
-        nc.vector.memset(packed[0:ROW0, 0:T].bitcast(I32), 0)
-        nc.vector.memset(packed[:, T:WINDOW].bitcast(I32), 0)
-        nc.vector.memset(shared_sc[:].bitcast(I32), 0)
-        for m in moved:
-            nc.vector.memset(m[:].bitcast(I32), 0)
-
+        scales_t = keep.tile([P, WINDOW + PASSES * T], U8, name="scales_t", align_bytes=64)
+        moved_t = keep.tile([P, PASSES * S], U8, name="moved_t", align_bytes=64)
         words_t = keep.tile([P, (PASSES - 1) * T + WINDOW], I32, name="words_t", align_bytes=64)
+        nc.vector.memset(scales_t[0:ROW0, 0:T].bitcast(I32), 0)
+        nc.vector.memset(scales_t[:, T:].bitcast(I32), 0)
+        nc.vector.memset(moved_t[:].bitcast(I32), 0)
         nc.vector.memset(words_t[:, PASSES * T :], 0)
         first_col = [(PASSES - 1 - a) * T for a in range(PASSES)]
+        ident = keep.tile([P, P], F32, name="ident")
+        make_identity(nc, ident[:])
 
         def load_words(a):
             nc.sync.dma_start(out=words_t[:, first_col[a] : first_col[a] + T], in_=dy_words[a].rearrange("p t d -> p (t d)").bitcast(I32))
 
         raw = {}
 
-        def load_w(a, lo, hi):
-            tile = keep.tile([P, (hi - lo) * 512], F32, name=f"raw{a}_{lo}", tag=f"raw{a}_{lo}", align_bytes=64)
-            for e in range(lo, hi):
-                raw[a, e] = (tile, 512 * (e - lo))
-            nc.sync.dma_start(
-                out=tile[:].rearrange("p (e x) -> p e x", x=512),
-                in_=w[lo:hi, 512 * a : 512 * (a + 1), :].rearrange("e (p j) k -> p e (j k)", j=4),
-            )
+        def load_w(name, units, source):
+            tile = keep.tile([P, len(units) * 512], F32, name=f"raw{name}", tag=f"raw{name}", align_bytes=64)
+            for u, unit in enumerate(units):
+                raw[unit] = (tile, u)
+            nc.sync.dma_start(out=tile[:].rearrange("p (u x) -> p u x", x=512), in_=source)
+
+        def load_pair(a):
+            load_w(f"pair{a}", [(a, 2), (a, 3)], w[2:4, 512 * a : 512 * (a + 1), :].rearrange("e (p j) k -> p e (j k)", j=4))
+
+        def load_expert(e):
+            load_w(f"expert{e}", [(a, e) for a in range(PASSES)], w[e].rearrange("(a p j) k -> p a (j k)", a=PASSES, j=4))
 
         sc32 = dy_scales.bitcast(I32)
         rows = sc32.rearrange("a f t -> (a f) t")
         nc.sync.dma_start(offs_t[:], offs)
-        nc.sync.dma_start(out=packed[ROW0 : ROW0 + 16, 0:T].bitcast(I32), in_=rows[0:16, :])
-        nc.sync.dma_start(out=packed[ROW0 + 16 : P, 0:T].bitcast(I32), in_=rows[16:48, :])
+        nc.sync.dma_start(out=scales_t[ROW0 : ROW0 + 16, 0:T].bitcast(I32), in_=rows[0:16, :])
+        nc.sync.dma_start(out=scales_t[ROW0 + 16 : P, 0:T].bitcast(I32), in_=rows[16:48, :])
         for q in range(4):
             nc.scalar.dma_start(
-                out=shared_sc[32 * q : 32 * q + 4, :].bitcast(I32).rearrange("r (a t) -> r a t", a=PASSES),
+                out=scales_t[32 * q : 32 * q + 4, WINDOW:].bitcast(I32).rearrange("r (a t) -> r a t", a=PASSES),
                 in_=sc32[:, 4 * q : 4 * q + 4, :].rearrange("a r t -> r a t"),
             )
-        load_w(0, 1, NE)
+        load_pair(0)
         load_words(0)
         load_words(1)
-        load_w(0, 0, 1)
-        load_w(1, LATE, NE)
+        load_pair(1)
         load_words(2)
+        load_pair(2)
+        load_expert(1)
+
+        gb = keep.tile([P, S], U8, name="gb", align_bytes=64)
+        for lo in range(0, S, 2 * C):
+            nc.vector.tensor_copy(gb[:, lo : lo + 2 * C], scales_t[:, 0:WINDOW].indirect(offs_t[:, lo // 16 : (lo + 2 * C) // 16]))
+
+        def move_scales(a):
+            for q in range(4):
+                r = ROW0 + 16 * a + 4 * q
+                nc.sync.dma_start(out=moved_t[32 * q : 32 * q + 4, S * a : S * (a + 1)].bitcast(I32), in_=gb[r : r + 4, :].bitcast(I32))
+
+        move_scales(0)
+        load_expert(SHARED)
+        move_scales(1)
+        load_expert(0)
+        move_scales(2)
+        gate_rows = keep.tile([P, P], F32, name="gate_rows")
+        nc.sync.dma_start(out=gate_rows[:], in_=gate.rearrange("r (b j) -> (r b) j", j=P)[0:P, :])
+        gate_t = keep.tile([P, 2 * C], F32, name="gate_t")
+        nc.sync.dma_start(out=gate_t[:], in_=gate[:, 0 : 2 * C])
+        nc.sync.dma_start(pos1_t[:], pos1)
+        nc.sync.dma_start(pos2_t[:], pos2)
 
         codes = {}
         wsc = {}
 
-        def quantise(name, runs, tag):
-            n = sum(hi - lo for a, lo, hi in runs)
-            grouped = keep.tile([P, n * 512], BF16, name=f"grouped{name}", tag=tag, align_bytes=64)
+        def quantise(name, runs):
+            n = sum(len(run) for run in runs)
+            grouped = keep.tile([P, n * 512], BF16, name=f"grouped{name}", tag=f"grouped{name}", align_bytes=64)
             code_t = keep.tile([P, n * K], U32, name=f"codes{name}", align_bytes=64)
             scale_t = keep.tile([P, n * K], U8, name=f"wsc{name}", align_bytes=64)
             u = 0
-            for a, lo, hi in runs:
-                tile, col = raw[a, lo]
+            for run in runs:
+                tile, at = raw[run[0]]
                 nc.scalar.copy(
-                    out=grouped[:, 512 * u : 512 * (u + hi - lo)].rearrange("p (e c i j) -> p e c j i", c=K // 4, i=4, j=4),
-                    in_=tile[:, col : col + 512 * (hi - lo)].rearrange("p (e j c i) -> p e c j i", j=4, c=K // 4, i=4),
+                    out=grouped[:, 512 * u : 512 * (u + len(run))].rearrange("p (e c i j) -> p e c j i", c=K // 4, i=4, j=4),
+                    in_=tile[:, 512 * at : 512 * (at + len(run))].rearrange("p (e j c i) -> p e c j i", j=4, c=K // 4, i=4),
                 )
-                for e in range(lo, hi):
-                    codes[a, e] = code_t[:, K * u : K * (u + 1)]
-                    wsc[a, e] = scale_t[:, K * u : K * (u + 1)]
+                for unit in run:
+                    codes[unit] = code_t[:, K * u : K * (u + 1)]
+                    wsc[unit] = scale_t[:, K * u : K * (u + 1)]
                     u = u + 1
             nc.vector.quantize_mx(out=code_t[:].bitcast(E4M3), scales=scale_t[:], in_=grouped[:])
 
-        acc = [psum.tile([P, C], F32, name=f"acc{e}") for e in range(E)]
-        acc_sh = [psum.tile([P, 512], F32, name=f"acc_sh{h}") for h in range(T // 512)]
+        acc = {e: psum.tile([P, C], F32, name=f"acc{e}", tag=f"acc{e}") for e in (2, 3)}
 
         def multiply(a, e, dst, rhs, rhs_scale):
             nc.tensor.matmul_mx(
@@ -118,97 +139,88 @@ def tile_moe_bds_lin_none_kernel(tc, dy_words, dy_scales, w, gate, offs, pos1, p
                 stop=(a == PASSES - 1),
             )
 
-        def shared(a):
-            for h in range(T // 512):
-                cols = slice(T * a + 512 * h, T * a + 512 * (h + 1))
-                multiply(a, E, acc_sh[h][:], words_t[:, first_col[a] + 512 * h : first_col[a] + 512 * (h + 1)], shared_sc[:, cols])
-
-        gw = {}
+        def routed(a, e, dst, rhs):
+            multiply(a, e, dst[:], rhs, moved_t[:, S * a + C * e : S * a + C * (e + 1)])
 
         def gather(dst, a, lo, hi, width):
             window = words_t[:, first_col[a] : first_col[a] + width].bitcast(U32)
             nc.vector.tensor_copy(dst, window.indirect(offs_t[:, lo // 16 : hi // 16]))
 
-        def gather_words(a, cuts, width, tag):
-            lo, hi = cuts[0], cuts[-1]
-            dst = keep.tile([P, C * (hi - lo)], U32, name=f"gw{a}_{lo}", tag=tag, align_bytes=64)
-            for x, y in zip(cuts, cuts[1:]):
-                gather(dst[:, C * (x - lo) : C * (y - lo)], a, C * x, C * y, width)
-            for e in range(lo, hi):
-                gw[a, e] = dst[:, C * (e - lo) : C * (e - lo + 1)]
+        def gather_pair(a, e, tag):
+            dst = keep.tile([P, 2 * C], U32, name=f"gw{a}_{e}", tag=tag, align_bytes=64)
+            gather(dst[:], a, C * e, C * (e + 2), WINDOW)
+            return dst
 
-        def routed(a, e):
-            multiply(a, e, acc[e][:], gw[a, e], moved[a][:, C * e : C * (e + 1)])
+        early = [gather_pair(0, 2, "gw0"), gather_pair(1, 2, "gw1")]
+        quantise("a", [[(0, 2), (0, 3)], [(1, 2), (1, 3)]])
+        for a in (0, 1):
+            for e in (2, 3):
+                routed(a, e, acc[e], early[a][:, C * (e - 2) : C * (e - 1)])
+        third = gather_pair(2, 2, "rawpair2")
+        quantise("b", [[(2, 2), (2, 3)], [(0, 1), (1, 1)]])
+        for e in (2, 3):
+            routed(2, e, acc[e], third[:, C * (e - 2) : C * (e - 1)])
+        late0 = gather_pair(0, 0, "rawexpert1")
+        quantise("c", [[(2, 1)], [(a, SHARED) for a in range(PASSES)]])
+        quantise("d", [[(0, 0), (1, 0)]])
+        quantise("e", [[(2, 0)]])
+        turned = psum.tile([P, P], F32, name="turned", tag="turn")
+        nc.tensor.transpose(turned[:], gate_rows[:], ident[:])
+        gate_cols = keep.tile([P, S // P], F32, name="gate_cols")
+        nc.scalar.copy(out=gate_cols[:], in_=turned[:, 0 : S // P])
 
-        gb = keep.tile([P, S], U8, name="gb", align_bytes=64)
-        for e in range(0, E, 2):
-            nc.vector.tensor_copy(gb[:, C * e : C * (e + 2)], packed[:].indirect(offs_t[:, 32 * e : 32 * (e + 2)]))
-
-        def move_scales(a):
-            for q in range(4):
-                r = ROW0 + 16 * a + 4 * q
-                nc.sync.dma_start(out=moved[a][32 * q : 32 * q + 4, :].bitcast(I32), in_=gb[r : r + 4, :].bitcast(I32))
-
-        move_scales(0)
-        load_w(2, LATE, E)
-        move_scales(1)
-        load_w(1, 0, LATE)
-        move_scales(2)
-        load_w(2, 0, LATE)
-        load_w(2, E, NE)
-        nc.sync.dma_start(pos1_t[:], pos1)
-        nc.sync.dma_start(pos2_t[:], pos2)
-        gate_t = keep.tile([P, S], F32, name="gate_t", align_bytes=64)
-        nc.sync.dma_start(out=gate_t[:], in_=gate)
-
-        gather_words(0, (1, LATE, E), WINDOW, "gw0")
-        quantise("0", [(0, 1, NE)], "g0")
-        for e in range(1, E):
-            routed(0, e)
-        shared(0)
-
-        gather_words(1, (1, E), WIDE, "raw0_0")
-        quantise("1", [(0, 0, 1), (1, LATE, NE)], "g1")
-        for e in range(LATE, E):
-            routed(1, e)
-        shared(1)
-        gather_words(2, (LATE, E), WINDOW, "raw2_2")
-        quantise("2", [(2, LATE, E)], "g2")
-        for e in range(LATE, E):
-            routed(2, e)
-        quantise("3", [(1, 0, LATE), (2, 0, LATE)], "g3")
-        routed(1, 1)
-        quantise("4", [(2, E, NE)], "g4")
-        last = keep.tile([P, 4 * C], U32, name="last", tag="raw2_4", align_bytes=64)
+        dx = keep.tile([P, S], F32, name="dx")
+        blocks = [slice(P * b, P * (b + 1)) for b in range(C // P)]
+        sums, gated = {}, {}
+        for e in (2, 3):
+            sums[e] = keep.tile([P, C], F32, name=f"sums{e}")
+            nc.scalar.copy(out=sums[e][:], in_=acc[e][:])
+        for e in (2, 3):
+            by_slot = psum.tile([P, C], F32, name=f"by_slot{e}", tag=f"slot{e}")
+            gated[e] = keep.tile([P, C], F32, name=f"gated{e}", tag=f"gated{e}")
+            for cols in blocks:
+                nc.tensor.transpose(by_slot[:, cols], sums[e][:, cols], ident[:])
+            for b, cols in enumerate(blocks):
+                column = e * C // P + b
+                nc.scalar.activation(gated[e][:, cols], by_slot[:, cols], COPY, scale=gate_cols[:, column : column + 1])
+        acc_sh = [psum.tile([P, 512], F32, name=f"acc_sh{h}", tag=f"acc{2 + h}") for h in range(T // 512)]
+        for a in range(PASSES):
+            for h in range(T // 512):
+                multiply(
+                    a,
+                    SHARED,
+                    acc_sh[h][:],
+                    words_t[:, first_col[a] + 512 * h : first_col[a] + 512 * (h + 1)],
+                    scales_t[:, WINDOW + T * a + 512 * h : WINDOW + T * a + 512 * (h + 1)],
+                )
+        for e, tag in ((2, "turn"), (3, "slot2")):
+            back = psum.tile([P, C], F32, name=f"back{e}", tag=tag)
+            for cols in blocks:
+                nc.tensor.transpose(back[:, cols], gated[e][:, cols], ident[:])
+            nc.scalar.copy(out=dx[:, C * e : C * (e + 1)], in_=back[:])
+        acc[1] = psum.tile([P, C], F32, name="acc1", tag="slot3")
+        acc[0] = psum.tile([P, C], F32, name="acc0", tag="turn")
+        acc_tail = psum.tile([P, C], F32, name="acc_tail", tag="slot2")
+        routed(0, 1, acc[1], late0[:, C:])
+        routed(0, 0, acc[0], late0[:, 0:C])
+        routed(0, 0, acc_tail, late0[:, 0:C])
+        last = keep.tile([P, 4 * C], U32, name="last", tag="rawexpert0", align_bytes=64)
         head = C - TAIL
-        gw[2, 1] = last[:, 0:C]
-        gather(gw[2, 1], 2, C, 2 * C, T)
-        shared(2)
-        routed(2, 1)
-        pass0 = last[:, C : 2 * C]
-        pass1 = last[:, 2 * C + head : 3 * C + head]
-        gather(pass0, 0, 0, C, T)
-        gather(pass1, 1, 0, C, T)
+        gather(last[:, 0 : 2 * C], 1, 0, 2 * C, WINDOW)
+        gather(last[:, 2 * C + head : 3 * C + head], 2, C, 2 * C, T)
         gather(last[:, 2 * C : 2 * C + head], 2, 0, head, T)
         gather(last[:, 3 * C + head : 4 * C], 2, head, C, T)
-        acc_tail = psum.tile([P, C], F32, name="acc_tail")
-        for a, rhs in enumerate((pass0, pass1)):
-            multiply(a, 0, acc[0][:], rhs, moved[a][:, 0:C])
-            multiply(a, 0, acc_tail[:], rhs, moved[a][:, 0:C])
-        multiply(2, 0, acc[0][:], last[:, 2 * C : 3 * C], moved[2][:, 0:C])
-        multiply(2, 0, acc_tail[:], last[:, 3 * C : 4 * C], moved[2][:, 0:C])
+        routed(1, 1, acc[1], last[:, C : 2 * C])
+        routed(1, 0, acc[0], last[:, 0:C])
+        routed(1, 0, acc_tail, last[:, 0:C])
+        routed(2, 1, acc[1], last[:, 2 * C + head : 3 * C + head])
+        routed(2, 0, acc[0], last[:, 2 * C : 3 * C])
+        routed(2, 0, acc_tail, last[:, 3 * C : 4 * C])
 
-        dx = keep.tile([P, S], F32, name="dx", tag="g4", align_bytes=64)
-        copied = keep.tile([P, S + T], F32, name="copied", tag="g3", align_bytes=64)
-        ds = copied[:, S:]
-        for lo, hi in ((2 * C, 3 * C), (3 * C, 4 * C), (C + FILL, 2 * C)):
-            cols = slice(lo, hi)
-            e = lo // C
-            nc.scalar.copy(out=copied[:, cols], in_=acc[e][:, lo - C * e : hi - C * e])
-            nc.gpsimd.tensor_tensor(dx[:, cols], copied[:, cols], gate_t[:, cols], MULT)
+        ds = keep.tile([P, T], F32, name="ds", tag="gated3")
         for h in range(T // 512):
             nc.scalar.copy(out=ds[:, 512 * h : 512 * (h + 1)], in_=acc_sh[h][:])
-        nc.vector.tensor_tensor(dx[:, C : C + FILL], acc[1][:, 0:FILL], gate_t[:, C : C + FILL], MULT)
+        nc.vector.tensor_tensor(dx[:, C : 2 * C], acc[1][:], gate_t[:, C : 2 * C], MULT)
         nc.vector.tensor_tensor(dx[:, 0:head], acc[0][:, 0:head], gate_t[:, 0:head], MULT)
         nc.vector.tensor_tensor(dx[:, head:C], acc_tail[:, head:C], gate_t[:, head:C], MULT)
 

@@ -1,7 +1,6 @@
 from contextlib import ExitStack
 
 import concourse.mybir as mybir
-from concourse.masks import make_identity
 
 K, T, E, C, N = 128, 1024, 4, 512, 1536
 FLOPS = 2 * N * K * (E * C + T)
@@ -16,7 +15,6 @@ E4M3 = mybir.dt.float8_e4m3fn_x4
 E5M2 = mybir.dt.float8_e5m2_x4
 ADD = mybir.AluOpType.add
 MULT = mybir.AluOpType.mult
-COPY = mybir.ActivationFunctionType.Copy
 
 P = 128
 PASSES = N // 512
@@ -46,8 +44,6 @@ def tile_moe_bds_lin_none_kernel(tc, dy_words, dy_scales, w, gate, offs, pos1, p
         nc.vector.memset(moved_t[:].bitcast(I32), 0)
         nc.vector.memset(words_t[:, PASSES * T :], 0)
         first_col = [(PASSES - 1 - a) * T for a in range(PASSES)]
-        ident = keep.tile([P, P], F32, name="ident")
-        make_identity(nc, ident[:])
 
         def load_words(a):
             nc.sync.dma_start(out=words_t[:, first_col[a] : first_col[a] + T], in_=dy_words[a].rearrange("p t d -> p (t d)").bitcast(I32))
@@ -82,26 +78,27 @@ def tile_moe_bds_lin_none_kernel(tc, dy_words, dy_scales, w, gate, offs, pos1, p
         load_pair(1)
         load_words(2)
         load_pair(2)
-        load_expert(1)
+        load_expert(SHARED)
 
         gb = keep.tile([P, S], U8, name="gb", align_bytes=64)
         for lo in range(0, S, 2 * C):
             nc.vector.tensor_copy(gb[:, lo : lo + 2 * C], scales_t[:, 0:WINDOW].indirect(offs_t[:, lo // 16 : (lo + 2 * C) // 16]))
 
-        def move_scales(a):
-            for q in range(4):
+        def move_scales(a, quadrants):
+            for q in quadrants:
                 r = ROW0 + 16 * a + 4 * q
                 nc.sync.dma_start(out=moved_t[32 * q : 32 * q + 4, S * a : S * (a + 1)].bitcast(I32), in_=gb[r : r + 4, :].bitcast(I32))
 
-        move_scales(0)
-        load_expert(SHARED)
-        move_scales(1)
-        load_expert(0)
-        move_scales(2)
-        gate_rows = keep.tile([P, P], F32, name="gate_rows")
-        nc.sync.dma_start(out=gate_rows[:], in_=gate.rearrange("r (b j) -> (r b) j", j=P)[0:P, :])
-        gate_t = keep.tile([P, 2 * C], F32, name="gate_t")
-        nc.sync.dma_start(out=gate_t[:], in_=gate[:, 0 : 2 * C])
+        move_scales(0, range(4))
+        move_scales(1, range(2))
+        load_expert(1)
+        move_scales(1, range(2, 4))
+        move_scales(2, range(4))
+        expert0 = w[0].rearrange("(a p j) k -> p a (j k)", a=PASSES, j=4)
+        load_w("first0", [(0, 0), (1, 0)], expert0[:, 0:2, :])
+        load_w("third0", [(2, 0)], expert0[:, 2:3, :])
+        gate_t = keep.tile([P, S], F32, name="gate_t")
+        nc.sync.dma_start(out=gate_t[:], in_=gate)
         nc.sync.dma_start(pos1_t[:], pos1)
         nc.sync.dma_start(pos2_t[:], pos2)
 
@@ -128,19 +125,19 @@ def tile_moe_bds_lin_none_kernel(tc, dy_words, dy_scales, w, gate, offs, pos1, p
 
         acc = {e: psum.tile([P, C], F32, name=f"acc{e}", tag=f"acc{e}") for e in (2, 3)}
 
-        def multiply(a, e, dst, rhs, rhs_scale):
+        def multiply(a, e, dst, rhs, rhs_scale, order):
             nc.tensor.matmul_mx(
                 out=dst,
                 lhsT=codes[a, e].bitcast(E4M3),
                 lhsT_scale=wsc[a, e],
                 rhs=rhs.bitcast(E5M2),
                 rhs_scale=rhs_scale,
-                start=(a == 0),
-                stop=(a == PASSES - 1),
+                start=(a == order[0]),
+                stop=(a == order[-1]),
             )
 
-        def routed(a, e, dst, rhs):
-            multiply(a, e, dst[:], rhs, moved_t[:, S * a + C * e : S * a + C * (e + 1)])
+        def routed(a, e, dst, rhs, slot, order):
+            multiply(a, e, dst[:], rhs, moved_t[:, S * a + slot : S * a + slot + C], order)
 
         def gather(dst, a, lo, hi, width):
             window = words_t[:, first_col[a] : first_col[a] + width].bitcast(U32)
@@ -155,74 +152,58 @@ def tile_moe_bds_lin_none_kernel(tc, dy_words, dy_scales, w, gate, offs, pos1, p
         quantise("a", [[(0, 2), (0, 3)], [(1, 2), (1, 3)]])
         for a in (0, 1):
             for e in (2, 3):
-                routed(a, e, acc[e], early[a][:, C * (e - 2) : C * (e - 1)])
+                routed(a, e, acc[e], early[a][:, C * (e - 2) : C * (e - 1)], C * e, (0, 1, 2))
         third = gather_pair(2, 2, "rawpair2")
-        quantise("b", [[(2, 2), (2, 3)], [(0, 1), (1, 1)]])
+        quantise("b", [[(2, 2), (2, 3)], [(0, SHARED), (1, SHARED)]])
         for e in (2, 3):
-            routed(2, e, acc[e], third[:, C * (e - 2) : C * (e - 1)])
-        late0 = gather_pair(0, 0, "rawexpert1")
-        quantise("c", [[(2, 1)], [(a, SHARED) for a in range(PASSES)]])
+            routed(2, e, acc[e], third[:, C * (e - 2) : C * (e - 1)], C * e, (0, 1, 2))
+        acc_sh = [psum.tile([P, 512], F32, name=f"acc_sh{h}") for h in range(T // 512)]
+
+        def shared(a):
+            for h in range(T // 512):
+                tokens = words_t[:, first_col[a] + 512 * h : first_col[a] + 512 * (h + 1)]
+                plane = scales_t[:, WINDOW + T * a + 512 * h : WINDOW + T * a + 512 * (h + 1)]
+                multiply(a, SHARED, acc_sh[h][:], tokens, plane, (0, 1, 2))
+
+        shared(0)
+        shared(1)
+        late0 = gather_pair(0, 0, f"rawexpert{SHARED}")
+        quantise("c", [[(2, SHARED)], [(a, 1) for a in range(PASSES)]])
+        shared(2)
+        late2 = keep.tile([P, 2 * C - TAIL], U32, name="late2", tag="rawexpert1", align_bytes=64)
+        gather(late2[:], 2, TAIL, 2 * C, WINDOW)
         quantise("d", [[(0, 0), (1, 0)]])
         quantise("e", [[(2, 0)]])
-        turned = psum.tile([P, P], F32, name="turned", tag="turn")
-        nc.tensor.transpose(turned[:], gate_rows[:], ident[:])
-        gate_cols = keep.tile([P, S // P], F32, name="gate_cols")
-        nc.scalar.copy(out=gate_cols[:], in_=turned[:, 0 : S // P])
-
-        dx = keep.tile([P, S], F32, name="dx")
-        blocks = [slice(P * b, P * (b + 1)) for b in range(C // P)]
-        sums, gated = {}, {}
+        dx = keep.tile([P, S], F32, name="dx", tag="groupede", align_bytes=64)
+        copied = keep.tile([P, S], F32, name="copied", tag="rawfirst0", align_bytes=64)
         for e in (2, 3):
-            sums[e] = keep.tile([P, C], F32, name=f"sums{e}")
-            nc.scalar.copy(out=sums[e][:], in_=acc[e][:])
-        for e in (2, 3):
-            by_slot = psum.tile([P, C], F32, name=f"by_slot{e}", tag=f"slot{e}")
-            gated[e] = keep.tile([P, C], F32, name=f"gated{e}", tag=f"gated{e}")
-            for cols in blocks:
-                nc.tensor.transpose(by_slot[:, cols], sums[e][:, cols], ident[:])
-            for b, cols in enumerate(blocks):
-                column = e * C // P + b
-                nc.scalar.activation(gated[e][:, cols], by_slot[:, cols], COPY, scale=gate_cols[:, column : column + 1])
-        acc_sh = [psum.tile([P, 512], F32, name=f"acc_sh{h}", tag=f"acc{2 + h}") for h in range(T // 512)]
-        for a in range(PASSES):
-            for h in range(T // 512):
-                multiply(
-                    a,
-                    SHARED,
-                    acc_sh[h][:],
-                    words_t[:, first_col[a] + 512 * h : first_col[a] + 512 * (h + 1)],
-                    scales_t[:, WINDOW + T * a + 512 * h : WINDOW + T * a + 512 * (h + 1)],
-                )
-        for e, tag in ((2, "turn"), (3, "slot2")):
-            back = psum.tile([P, C], F32, name=f"back{e}", tag=tag)
-            for cols in blocks:
-                nc.tensor.transpose(back[:, cols], gated[e][:, cols], ident[:])
-            nc.scalar.copy(out=dx[:, C * e : C * (e + 1)], in_=back[:])
-        acc[1] = psum.tile([P, C], F32, name="acc1", tag="slot3")
-        acc[0] = psum.tile([P, C], F32, name="acc0", tag="turn")
-        acc_tail = psum.tile([P, C], F32, name="acc_tail", tag="slot2")
-        routed(0, 1, acc[1], late0[:, C:])
-        routed(0, 0, acc[0], late0[:, 0:C])
-        routed(0, 0, acc_tail, late0[:, 0:C])
-        last = keep.tile([P, 4 * C], U32, name="last", tag="rawexpert0", align_bytes=64)
+            cols = slice(C * e, C * (e + 1))
+            nc.scalar.copy(out=copied[:, cols], in_=acc[e][:])
+            nc.gpsimd.tensor_tensor(dx[:, cols], copied[:, cols], gate_t[:, cols], MULT)
+        acc[1] = psum.tile([P, C], F32, name="acc1")
+        acc[0] = psum.tile([P, C], F32, name="acc0", tag="acc2")
+        acc_tail = psum.tile([P, C], F32, name="acc_tail", tag="acc3")
         head = C - TAIL
-        gather(last[:, 0 : 2 * C], 1, 0, 2 * C, WINDOW)
-        gather(last[:, 2 * C + head : 3 * C + head], 2, C, 2 * C, T)
-        gather(last[:, 2 * C : 2 * C + head], 2, 0, head, T)
-        gather(last[:, 3 * C + head : 4 * C], 2, head, C, T)
-        routed(1, 1, acc[1], last[:, C : 2 * C])
-        routed(1, 0, acc[0], last[:, 0:C])
-        routed(1, 0, acc_tail, last[:, 0:C])
-        routed(2, 1, acc[1], last[:, 2 * C + head : 3 * C + head])
-        routed(2, 0, acc[0], last[:, 2 * C : 3 * C])
-        routed(2, 0, acc_tail, last[:, 3 * C : 4 * C])
+        routed(2, 1, acc[1], late2[:, head:], C, (2, 0, 1))
+        routed(0, 1, acc[1], late0[:, C:], C, (2, 0, 1))
+        routed(0, 0, acc[0], late0[:, TAIL : TAIL + C], TAIL, (0, 2, 1))
+        routed(2, 0, acc[0], late2[:, 0:C], TAIL, (0, 2, 1))
+        routed(0, 0, acc_tail, late0[:, 0:C], 0, (0, 1, 2))
+        last = keep.tile([P, TAIL + 2 * C], U32, name="last", tag="rawthird0", align_bytes=64)
+        gather(last[:, 2 * TAIL :], 1, TAIL, 2 * C, WINDOW)
+        gather(last[:, TAIL : 2 * TAIL], 1, 0, TAIL, T)
+        gather(last[:, 0:TAIL], 2, 0, TAIL, T)
+        routed(1, 1, acc[1], last[:, TAIL + C :], C, (2, 0, 1))
+        routed(1, 0, acc[0], last[:, 2 * TAIL : 2 * TAIL + C], TAIL, (0, 2, 1))
+        routed(1, 0, acc_tail, last[:, TAIL : TAIL + C], 0, (0, 1, 2))
+        routed(2, 0, acc_tail, last[:, 0:C], 0, (0, 1, 2))
 
-        ds = keep.tile([P, T], F32, name="ds", tag="gated3")
+        ds = copied[:, 0:T]
         for h in range(T // 512):
             nc.scalar.copy(out=ds[:, 512 * h : 512 * (h + 1)], in_=acc_sh[h][:])
         nc.vector.tensor_tensor(dx[:, C : 2 * C], acc[1][:], gate_t[:, C : 2 * C], MULT)
-        nc.vector.tensor_tensor(dx[:, 0:head], acc[0][:, 0:head], gate_t[:, 0:head], MULT)
-        nc.vector.tensor_tensor(dx[:, head:C], acc_tail[:, head:C], gate_t[:, head:C], MULT)
+        nc.vector.tensor_tensor(dx[:, TAIL:C], acc[0][:, 0:head], gate_t[:, TAIL:C], MULT)
+        nc.vector.tensor_tensor(dx[:, 0:TAIL], acc_tail[:, 0:TAIL], gate_t[:, 0:TAIL], MULT)
 
         part = keep.tile([P, T], F32, name="part")
         for h in range(T // 512):

@@ -74,10 +74,10 @@ def tile_moe_bds_lin_none_kernel(tc, dy_words, dy_scales, w, gate, offs, pos1, p
             )
         load_pair(0)
         load_words(0)
-        load_words(1)
         load_pair(1)
-        load_words(2)
+        load_words(1)
         load_pair(2)
+        load_words(2)
         load_expert(SHARED)
 
         gb = keep.tile([P, S], U8, name="gb", align_bytes=64)
@@ -181,8 +181,8 @@ def tile_moe_bds_lin_none_kernel(tc, dy_words, dy_scales, w, gate, offs, pos1, p
             nc.scalar.copy(out=copied[:, cols], in_=acc[e][:])
             nc.gpsimd.tensor_tensor(dx[:, cols], copied[:, cols], gate_t[:, cols], MULT)
         acc[1] = psum.tile([P, C], F32, name="acc1")
-        acc[0] = psum.tile([P, C], F32, name="acc0", tag="acc2")
-        acc_tail = psum.tile([P, C], F32, name="acc_tail", tag="acc3")
+        acc[0] = psum.tile([P, C], F32, name="acc0")
+        acc_tail = psum.tile([P, C], F32, name="acc_tail")
         head = C - TAIL
         routed(2, 1, acc[1], late2[:, head:], C, (2, 0, 1))
         routed(0, 1, acc[1], late0[:, C:], C, (2, 0, 1))

@@ -23,7 +23,8 @@ SHARED = E
 ROW0 = P - 16 * PASSES
 WINDOW = 1408
 TAIL = 192
-CHUNKS = (512, 256, 128, 128)
+FIRST = 640
+CHUNKS = (640, 256, 128)
 
 
 def tile_moe_bds_lin_none_kernel(tc, dy_words, dy_scales, w, gate, offs, pos1, pos2, out):
@@ -36,11 +37,13 @@ def tile_moe_bds_lin_none_kernel(tc, dy_words, dy_scales, w, gate, offs, pos1, p
         pos1_t = keep.tile([P, T // 16], U16, name="pos1_t")
         pos2_t = keep.tile([P, T // 16], U16, name="pos2_t")
 
-        scales_t = keep.tile([P, WINDOW + PASSES * T], U8, name="scales_t", align_bytes=64)
+        scales_t = keep.tile([P, WINDOW], U8, name="scales_t", align_bytes=64)
+        shared_t = keep.tile([P, PASSES * T], U8, name="shared_t", align_bytes=64)
         moved_t = keep.tile([P, PASSES * S], U8, name="moved_t", align_bytes=64)
         words_t = keep.tile([P, (PASSES - 1) * T + WINDOW], I32, name="words_t", align_bytes=64)
         nc.vector.memset(scales_t[0:ROW0, 0:T].bitcast(I32), 0)
         nc.vector.memset(scales_t[:, T:].bitcast(I32), 0)
+        nc.vector.memset(shared_t[:].bitcast(I32), 0)
         nc.vector.memset(moved_t[:].bitcast(I32), 0)
         nc.vector.memset(words_t[:, PASSES * T :], 0)
         first_col = [(PASSES - 1 - a) * T for a in range(PASSES)]
@@ -59,18 +62,19 @@ def tile_moe_bds_lin_none_kernel(tc, dy_words, dy_scales, w, gate, offs, pos1, p
         def load_pair(a):
             load_w(f"pair{a}", [(a, 2), (a, 3)], w[2:4, 512 * a : 512 * (a + 1), :].rearrange("e (p j) k -> p e (j k)", j=4))
 
-        def load_expert(e):
-            load_w(f"expert{e}", [(a, e) for a in range(PASSES)], w[e].rearrange("(a p j) k -> p a (j k)", a=PASSES, j=4))
+        def load_expert(e, lo, hi):
+            source = w[e].rearrange("(a p j) k -> p a (j k)", a=PASSES, j=4)
+            load_w(f"expert{e}_{lo}", [(a, e) for a in range(lo, hi)], source[:, lo:hi, :])
 
         sc32 = dy_scales.bitcast(I32)
         rows = sc32.rearrange("a f t -> (a f) t")
         nc.sync.dma_start(offs_t[:], offs)
         nc.sync.dma_start(out=scales_t[ROW0 : ROW0 + 16, 0:T].bitcast(I32), in_=rows[0:16, :])
         nc.sync.dma_start(out=scales_t[ROW0 + 16 : P, 0:T].bitcast(I32), in_=rows[16:48, :])
-        for q in range(4):
+        for r in range(4):
             nc.scalar.dma_start(
-                out=scales_t[32 * q : 32 * q + 4, WINDOW:].bitcast(I32).rearrange("r (a t) -> r a t", a=PASSES),
-                in_=sc32[:, 4 * q : 4 * q + 4, :].rearrange("a r t -> r a t"),
+                out=shared_t[r:P:32, :].bitcast(I32).rearrange("q (a t) -> q a t", a=PASSES),
+                in_=sc32[:, r:16:4, :].rearrange("a q t -> q a t"),
             )
         load_pair(0)
         load_words(0)
@@ -78,27 +82,28 @@ def tile_moe_bds_lin_none_kernel(tc, dy_words, dy_scales, w, gate, offs, pos1, p
         load_words(1)
         load_pair(2)
         load_words(2)
-        load_expert(SHARED)
+        load_expert(SHARED, 0, 2)
 
         gb = keep.tile([P, S], U8, name="gb", align_bytes=64)
         for lo in range(0, S, 2 * C):
-            nc.vector.tensor_copy(gb[:, lo : lo + 2 * C], scales_t[:, 0:WINDOW].indirect(offs_t[:, lo // 16 : (lo + 2 * C) // 16]))
+            nc.vector.tensor_copy(gb[:, lo : lo + 2 * C], scales_t[:].indirect(offs_t[:, lo // 16 : (lo + 2 * C) // 16]))
 
-        def move_scales(a, quadrants):
-            for q in quadrants:
-                r = ROW0 + 16 * a + 4 * q
-                nc.sync.dma_start(out=moved_t[32 * q : 32 * q + 4, S * a : S * (a + 1)].bitcast(I32), in_=gb[r : r + 4, :].bitcast(I32))
+        def move_scales(a, rows_in_quadrant):
+            for r in rows_in_quadrant:
+                first = ROW0 + 16 * a + r
+                nc.sync.dma_start(out=moved_t[r:P:32, S * a : S * (a + 1)].bitcast(I32), in_=gb[first : first + 13 : 4, :].bitcast(I32))
 
         move_scales(0, range(4))
         move_scales(1, range(2))
-        load_expert(1)
+        load_expert(1, 0, 3)
         move_scales(1, range(2, 4))
         move_scales(2, range(4))
-        expert0 = w[0].rearrange("(a p j) k -> p a (j k)", a=PASSES, j=4)
-        load_w("first0", [(0, 0), (1, 0)], expert0[:, 0:2, :])
-        load_w("third0", [(2, 0)], expert0[:, 2:3, :])
+        load_expert(0, 0, 1)
+        load_expert(0, 1, 3)
+        load_expert(SHARED, 2, 3)
         gate_t = keep.tile([P, S], F32, name="gate_t")
-        nc.sync.dma_start(out=gate_t[:], in_=gate)
+        for lo in (2 * C, 0):
+            nc.sync.dma_start(out=gate_t[:, lo : lo + 2 * C], in_=gate[:, lo : lo + 2 * C])
         nc.sync.dma_start(pos1_t[:], pos1)
         nc.sync.dma_start(pos2_t[:], pos2)
 
@@ -148,34 +153,29 @@ def tile_moe_bds_lin_none_kernel(tc, dy_words, dy_scales, w, gate, offs, pos1, p
             gather(dst[:], a, C * e, C * (e + 2), WINDOW)
             return dst
 
-        early = [gather_pair(0, 2, "gw0"), gather_pair(1, 2, "gw1")]
-        quantise("a", [[(0, 2), (0, 3)], [(1, 2), (1, 3)]])
-        for a in (0, 1):
+        early = [gather_pair(a, 2, f"early{a}") for a in range(PASSES)]
+        quantise("a", [[(a, 2), (a, 3)] for a in range(PASSES)] + [[(0, SHARED), (1, SHARED)]])
+        for a in range(PASSES):
             for e in (2, 3):
                 routed(a, e, acc[e], early[a][:, C * (e - 2) : C * (e - 1)], C * e, (0, 1, 2))
-        third = gather_pair(2, 2, "rawpair2")
-        quantise("b", [[(2, 2), (2, 3)], [(0, SHARED), (1, SHARED)]])
-        for e in (2, 3):
-            routed(2, e, acc[e], third[:, C * (e - 2) : C * (e - 1)], C * e, (0, 1, 2))
         acc_sh = [psum.tile([P, 512], F32, name=f"acc_sh{h}") for h in range(T // 512)]
 
         def shared(a):
             for h in range(T // 512):
                 tokens = words_t[:, first_col[a] + 512 * h : first_col[a] + 512 * (h + 1)]
-                plane = scales_t[:, WINDOW + T * a + 512 * h : WINDOW + T * a + 512 * (h + 1)]
+                plane = shared_t[:, T * a + 512 * h : T * a + 512 * (h + 1)]
                 multiply(a, SHARED, acc_sh[h][:], tokens, plane, (0, 1, 2))
 
         shared(0)
         shared(1)
-        late0 = gather_pair(0, 0, f"rawexpert{SHARED}")
-        quantise("c", [[(2, SHARED)], [(a, 1) for a in range(PASSES)]])
-        shared(2)
-        late2 = keep.tile([P, 2 * C - TAIL], U32, name="late2", tag="rawexpert1", align_bytes=64)
+        late0 = gather_pair(0, 0, f"rawexpert{SHARED}_0")
+        quantise("c", [[(a, 1) for a in range(PASSES)], [(0, 0)]])
+        late2 = keep.tile([P, 2 * C - TAIL], U32, name="late2", tag="rawexpert0_0", align_bytes=64)
         gather(late2[:], 2, TAIL, 2 * C, WINDOW)
-        quantise("d", [[(0, 0), (1, 0)]])
-        quantise("e", [[(2, 0)]])
+        quantise("d", [[(1, 0), (2, 0)]])
+        quantise("e", [[(2, SHARED)]])
         dx = keep.tile([P, S], F32, name="dx", tag="groupede", align_bytes=64)
-        copied = keep.tile([P, S], F32, name="copied", tag="rawfirst0", align_bytes=64)
+        copied = keep.tile([P, S], F32, name="copied", tag="rawexpert0_1", align_bytes=64)
         for e in (2, 3):
             cols = slice(C * e, C * (e + 1))
             nc.scalar.copy(out=copied[:, cols], in_=acc[e][:])
@@ -189,7 +189,8 @@ def tile_moe_bds_lin_none_kernel(tc, dy_words, dy_scales, w, gate, offs, pos1, p
         routed(0, 0, acc[0], late0[:, TAIL : TAIL + C], TAIL, (0, 2, 1))
         routed(2, 0, acc[0], late2[:, 0:C], TAIL, (0, 2, 1))
         routed(0, 0, acc_tail, late0[:, 0:C], 0, (0, 1, 2))
-        last = keep.tile([P, TAIL + 2 * C], U32, name="last", tag="rawthird0", align_bytes=64)
+        shared(2)
+        last = keep.tile([P, TAIL + 2 * C], U32, name="last", tag=f"rawexpert{SHARED}_2", align_bytes=64)
         gather(last[:, 2 * TAIL :], 1, TAIL, 2 * C, WINDOW)
         gather(last[:, TAIL : 2 * TAIL], 1, 0, TAIL, T)
         gather(last[:, 0:TAIL], 2, 0, TAIL, T)
@@ -206,9 +207,8 @@ def tile_moe_bds_lin_none_kernel(tc, dy_words, dy_scales, w, gate, offs, pos1, p
         nc.vector.tensor_tensor(dx[:, 0:TAIL], acc_tail[:, 0:TAIL], gate_t[:, 0:TAIL], MULT)
 
         part = keep.tile([P, T], F32, name="part")
-        for h in range(T // 512):
-            cols = slice(512 * h, 512 * (h + 1))
-            nc.vector.tensor_tensor(part[:, cols], dx[:].indirect(pos1_t[:, 32 * h : 32 * (h + 1)]), ds[:, cols], ADD)
+        for lo, hi in ((0, FIRST), (FIRST, T)):
+            nc.vector.tensor_tensor(part[:, lo:hi], dx[:].indirect(pos1_t[:, lo // 16 : hi // 16]), ds[:, lo:hi], ADD)
         t0 = 0
         for i, n in enumerate(CHUNKS):
             full = keep.tile([P, n], F32, name=f"full{i}")

@@ -39,12 +39,10 @@ def tile_moe_bds_lin_none_kernel(tc, dy_words, dy_scales, w, gate, offs, pos1, p
 
         scales_t = keep.tile([P, WINDOW], U8, name="scales_t", align_bytes=64)
         shared_t = keep.tile([P, PASSES * T], U8, name="shared_t", align_bytes=64)
-        moved_t = keep.tile([P, PASSES * S], U8, name="moved_t", align_bytes=64)
         words_t = keep.tile([P, (PASSES - 1) * T + WINDOW], I32, name="words_t", align_bytes=64)
         nc.vector.memset(scales_t[0:ROW0, 0:T].bitcast(I32), 0)
         nc.vector.memset(scales_t[:, T:].bitcast(I32), 0)
         nc.vector.memset(shared_t[:].bitcast(I32), 0)
-        nc.vector.memset(moved_t[:].bitcast(I32), 0)
         nc.vector.memset(words_t[:, PASSES * T :], 0)
         first_col = [(PASSES - 1 - a) * T for a in range(PASSES)]
 
@@ -88,10 +86,14 @@ def tile_moe_bds_lin_none_kernel(tc, dy_words, dy_scales, w, gate, offs, pos1, p
         for lo in range(0, S, 2 * C):
             nc.vector.tensor_copy(gb[:, lo : lo + 2 * C], scales_t[:].indirect(offs_t[:, lo // 16 : (lo + 2 * C) // 16]))
 
+        planes01 = keep.tile([P, 2 * S], U8, name="planes01", tag="rawpair0", align_bytes=64)
+        plane2 = keep.tile([P, S], U8, name="plane2", tag="rawpair1", align_bytes=64)
+        moved = [planes01[:, 0:S], planes01[:, S : 2 * S], plane2[:]]
+
         def move_scales(a, rows_in_quadrant):
             for r in rows_in_quadrant:
                 first = ROW0 + 16 * a + r
-                nc.sync.dma_start(out=moved_t[r:P:32, S * a : S * (a + 1)].bitcast(I32), in_=gb[first : first + 13 : 4, :].bitcast(I32))
+                nc.sync.dma_start(out=moved[a][r:P:32, :].bitcast(I32), in_=gb[first : first + 13 : 4, :].bitcast(I32))
 
         move_scales(0, range(4))
         move_scales(1, range(2))
@@ -142,7 +144,7 @@ def tile_moe_bds_lin_none_kernel(tc, dy_words, dy_scales, w, gate, offs, pos1, p
             )
 
         def routed(a, e, dst, rhs, slot, order):
-            multiply(a, e, dst[:], rhs, moved_t[:, S * a + slot : S * a + slot + C], order)
+            multiply(a, e, dst[:], rhs, moved[a][:, slot : slot + C], order)
 
         def gather(dst, a, lo, hi, width):
             window = words_t[:, first_col[a] : first_col[a] + width].bitcast(U32)

@@ -95,13 +95,11 @@ def tile_moe_bds_lin_none_kernel(tc, dy_words, dy_scales, w, gate, offs, pos1, p
                 first = ROW0 + 16 * a + r
                 nc.sync.dma_start(out=moved[a][r:P:32, :].bitcast(I32), in_=gb[first : first + 13 : 4, :].bitcast(I32))
 
-        move_scales(0, range(4))
-        move_scales(1, range(2))
         load_expert(1, 0, 3)
-        move_scales(1, range(2, 4))
-        move_scales(2, range(4))
         load_expert(0, 0, 1)
         load_expert(0, 1, 3)
+        for a in (1, 2, 0):
+            move_scales(a, range(4))
         load_expert(SHARED, 2, 3)
         gate_t = keep.tile([P, S], F32, name="gate_t")
         for lo in (2 * C, 0):
@@ -157,9 +155,9 @@ def tile_moe_bds_lin_none_kernel(tc, dy_words, dy_scales, w, gate, offs, pos1, p
 
         early = [gather_pair(a, 2, f"early{a}") for a in range(PASSES)]
         quantise("a", [[(a, 2), (a, 3)] for a in range(PASSES)] + [[(0, SHARED), (1, SHARED)]])
-        for a in range(PASSES):
+        for a in (1, 2, 0):
             for e in (2, 3):
-                routed(a, e, acc[e], early[a][:, C * (e - 2) : C * (e - 1)], C * e, (0, 1, 2))
+                routed(a, e, acc[e], early[a][:, C * (e - 2) : C * (e - 1)], C * e, (1, 2, 0))
         acc_sh = [psum.tile([P, 512], F32, name=f"acc_sh{h}") for h in range(T // 512)]
 
         def shared(a):
@@ -186,17 +184,17 @@ def tile_moe_bds_lin_none_kernel(tc, dy_words, dy_scales, w, gate, offs, pos1, p
         acc[0] = psum.tile([P, C], F32, name="acc0")
         acc_tail = psum.tile([P, C], F32, name="acc_tail")
         head = C - TAIL
-        routed(2, 1, acc[1], late2[:, head:], C, (2, 0, 1))
-        routed(0, 1, acc[1], late0[:, C:], C, (2, 0, 1))
+        routed(0, 1, acc[1], late0[:, C:], C, (0, 2, 1))
         routed(0, 0, acc[0], late0[:, TAIL : TAIL + C], TAIL, (0, 2, 1))
-        routed(2, 0, acc[0], late2[:, 0:C], TAIL, (0, 2, 1))
         routed(0, 0, acc_tail, late0[:, 0:C], 0, (0, 1, 2))
+        routed(2, 1, acc[1], late2[:, head:], C, (0, 2, 1))
+        routed(2, 0, acc[0], late2[:, 0:C], TAIL, (0, 2, 1))
         shared(2)
         last = keep.tile([P, TAIL + 2 * C], U32, name="last", tag=f"rawexpert{SHARED}_2", align_bytes=64)
         gather(last[:, 2 * TAIL :], 1, TAIL, 2 * C, WINDOW)
         gather(last[:, TAIL : 2 * TAIL], 1, 0, TAIL, T)
         gather(last[:, 0:TAIL], 2, 0, TAIL, T)
-        routed(1, 1, acc[1], last[:, TAIL + C :], C, (2, 0, 1))
+        routed(1, 1, acc[1], last[:, TAIL + C :], C, (0, 2, 1))
         routed(1, 0, acc[0], last[:, 2 * TAIL : 2 * TAIL + C], TAIL, (0, 2, 1))
         routed(1, 0, acc_tail, last[:, TAIL : TAIL + C], 0, (0, 1, 2))
         routed(2, 0, acc_tail, last[:, 0:C], 0, (0, 1, 2))

@@ -20,7 +20,7 @@ P = 128
 PASSES = N // 512
 S = E * C
 SHARED = E
-ROW0 = P - 16 * PASSES
+ROW_OF_PASS = (32, 48, 112)
 WINDOW = 1408
 TAIL = 192
 FIRST = 640
@@ -40,7 +40,8 @@ def tile_moe_bds_lin_none_kernel(tc, dy_words, dy_scales, w, gate, offs, pos1, p
         scales_t = keep.tile([P, WINDOW], U8, name="scales_t", align_bytes=64)
         shared_t = keep.tile([P, PASSES * T], U8, name="shared_t", align_bytes=64)
         words_t = keep.tile([P, (PASSES - 1) * T + WINDOW], I32, name="words_t", align_bytes=64)
-        nc.vector.memset(scales_t[0:ROW0, 0:T].bitcast(I32), 0)
+        nc.vector.memset(scales_t[0:32, 0:T].bitcast(I32), 0)
+        nc.vector.memset(scales_t[64:112, 0:T].bitcast(I32), 0)
         nc.vector.memset(scales_t[:, T:].bitcast(I32), 0)
         nc.vector.memset(shared_t[:].bitcast(I32), 0)
         nc.vector.memset(words_t[:, PASSES * T :], 0)
@@ -67,15 +68,15 @@ def tile_moe_bds_lin_none_kernel(tc, dy_words, dy_scales, w, gate, offs, pos1, p
         sc32 = dy_scales.bitcast(I32)
         rows = sc32.rearrange("a f t -> (a f) t")
         nc.sync.dma_start(offs_t[:], offs)
-        nc.sync.dma_start(out=scales_t[ROW0 : ROW0 + 16, 0:T].bitcast(I32), in_=rows[0:16, :])
-        nc.sync.dma_start(out=scales_t[ROW0 + 16 : P, 0:T].bitcast(I32), in_=rows[16:48, :])
+        nc.sync.dma_start(out=scales_t[32:64, 0:T].bitcast(I32), in_=rows[0:32, :])
+        nc.sync.dma_start(out=scales_t[112:P, 0:T].bitcast(I32), in_=rows[32:48, :])
+        load_pair(0)
+        load_words(0)
         for r in range(4):
-            nc.scalar.dma_start(
+            nc.sync.dma_start(
                 out=shared_t[r:P:32, :].bitcast(I32).rearrange("q (a t) -> q a t", a=PASSES),
                 in_=sc32[:, r:16:4, :].rearrange("a q t -> q a t"),
             )
-        load_pair(0)
-        load_words(0)
         load_pair(1)
         load_words(1)
         load_pair(2)
@@ -92,7 +93,7 @@ def tile_moe_bds_lin_none_kernel(tc, dy_words, dy_scales, w, gate, offs, pos1, p
 
         def move_scales(a, rows_in_quadrant):
             for r in rows_in_quadrant:
-                first = ROW0 + 16 * a + r
+                first = ROW_OF_PASS[a] + r
                 nc.sync.dma_start(out=moved[a][r:P:32, :].bitcast(I32), in_=gb[first : first + 13 : 4, :].bitcast(I32))
 
         load_expert(1, 0, 3)

@@ -21,8 +21,7 @@ PASSES = N // 512
 S = E * C
 SHARED = E
 ROW_OF_PASS = (32, 48, 112)
-WINDOW = 1408
-TAIL = 192
+TAIL = 128
 FIRST = 640
 CHUNKS = (640, 256, 128)
 
@@ -31,77 +30,78 @@ def tile_moe_bds_lin_none_kernel(tc, dy_words, dy_scales, w, gate, offs, pos1, p
     nc = tc.nc
     with ExitStack() as ctx:
         keep = ctx.enter_context(tc.tile_pool(name="keep", bufs=1))
+        late = ctx.enter_context(tc.tile_pool(name="late", bufs=1))
         psum = ctx.enter_context(tc.psum_pool(name="psum", bufs=1))
 
         offs_t = keep.tile([P, S // 16], U16, name="offs_t")
         pos1_t = keep.tile([P, T // 16], U16, name="pos1_t")
         pos2_t = keep.tile([P, T // 16], U16, name="pos2_t")
 
-        scales_t = keep.tile([P, WINDOW], U8, name="scales_t", align_bytes=64)
-        shared_t = keep.tile([P, PASSES * T], U8, name="shared_t", align_bytes=64)
-        words_t = keep.tile([P, (PASSES - 1) * T + WINDOW], I32, name="words_t", align_bytes=64)
+        scales_t = keep.tile([P, 2 * S], U8, name="scales_t", tag="scales", align_bytes=64)
+        words_t = keep.tile([P, 2 * S], I32, name="words_t", align_bytes=64)
         nc.vector.memset(scales_t[0:32, 0:T].bitcast(I32), 0)
         nc.vector.memset(scales_t[64:112, 0:T].bitcast(I32), 0)
         nc.vector.memset(scales_t[:, T:].bitcast(I32), 0)
+        shared_t = keep.tile([P, PASSES * T], U8, name="shared_t", align_bytes=64)
         nc.vector.memset(shared_t[:].bitcast(I32), 0)
         nc.vector.memset(words_t[:, PASSES * T :], 0)
-        first_col = [(PASSES - 1 - a) * T for a in range(PASSES)]
-
-        def load_words(a):
-            nc.sync.dma_start(out=words_t[:, first_col[a] : first_col[a] + T], in_=dy_words[a].rearrange("p t d -> p (t d)").bitcast(I32))
-
-        raw = {}
-
-        def load_w(name, units, source):
-            tile = keep.tile([P, len(units) * 512], F32, name=f"raw{name}", tag=f"raw{name}", align_bytes=64)
-            for u, unit in enumerate(units):
-                raw[unit] = (tile, u)
-            nc.sync.dma_start(out=tile[:].rearrange("p (u x) -> p u x", x=512), in_=source)
-
-        def load_pair(a):
-            load_w(f"pair{a}", [(a, 2), (a, 3)], w[2:4, 512 * a : 512 * (a + 1), :].rearrange("e (p j) k -> p e (j k)", j=4))
-
-        def load_expert(e, lo, hi):
-            source = w[e].rearrange("(a p j) k -> p a (j k)", a=PASSES, j=4)
-            load_w(f"expert{e}_{lo}", [(a, e) for a in range(lo, hi)], source[:, lo:hi, :])
 
         sc32 = dy_scales.bitcast(I32)
         rows = sc32.rearrange("a f t -> (a f) t")
         nc.sync.dma_start(offs_t[:], offs)
         nc.sync.dma_start(out=scales_t[32:64, 0:T].bitcast(I32), in_=rows[0:32, :])
         nc.sync.dma_start(out=scales_t[112:P, 0:T].bitcast(I32), in_=rows[32:48, :])
-        load_pair(0)
-        load_words(0)
         for r in range(4):
-            nc.sync.dma_start(
+            nc.scalar.dma_start(
                 out=shared_t[r:P:32, :].bitcast(I32).rearrange("q (a t) -> q a t", a=PASSES),
                 in_=sc32[:, r:16:4, :].rearrange("a q t -> q a t"),
             )
-        load_pair(1)
-        load_words(1)
-        load_pair(2)
-        load_words(2)
-        load_expert(SHARED, 0, 2)
+
+        def load_words(a):
+            nc.sync.dma_start(out=words_t[:, T * a : T * (a + 1)], in_=dy_words[a].rearrange("p t d -> p (t d)").bitcast(I32))
+
+        raw = {}
+
+        def load_w(name, units, source):
+            if name == "pair2_0":
+                raw[name] = (late.tile([P, len(units) * 512], F32, name=name, offset=4 * 2 * C, align_bytes=64), units)
+            else:
+                raw[name] = (keep.tile([P, len(units) * 512], F32, name=name, tag=name, align_bytes=64), units)
+            nc.sync.dma_start(out=raw[name][0][:].rearrange("p (u x) -> p u x", x=512), in_=source)
+
+        def load_pair(a, e):
+            load_w(f"pair{a}_{e}", [(a, e), (a, e + 1)], w[e : e + 2, 512 * a : 512 * (a + 1), :].rearrange("e (p j) k -> p e (j k)", j=4))
+
+        def load_shared(lo, hi):
+            source = w[SHARED].rearrange("(a p j) k -> p a (j k)", a=PASSES, j=4)
+            load_w(f"shared{lo}", [(a, SHARED) for a in range(lo, hi)], source[:, lo:hi, :])
+
+        load_pair(0, 2)
+        for a in range(PASSES):
+            load_words(a)
+        load_pair(0, 0)
+        load_pair(1, 2)
+        load_pair(1, 0)
 
         gb = keep.tile([P, S], U8, name="gb", align_bytes=64)
-        for lo in range(0, S, 2 * C):
-            nc.vector.tensor_copy(gb[:, lo : lo + 2 * C], scales_t[:].indirect(offs_t[:, lo // 16 : (lo + 2 * C) // 16]))
+        nc.vector.tensor_copy(gb[:], scales_t[:].indirect(offs_t[:]))
 
-        planes01 = keep.tile([P, 2 * S], U8, name="planes01", tag="rawpair0", align_bytes=64)
-        plane2 = keep.tile([P, S], U8, name="plane2", tag="rawpair1", align_bytes=64)
+        planes01 = keep.tile([P, 2 * S], U8, name="planes01", tag="pair0_2", align_bytes=64)
+        plane2 = keep.tile([P, S], U8, name="plane2", tag="pair1_2", align_bytes=64)
         moved = [planes01[:, 0:S], planes01[:, S : 2 * S], plane2[:]]
 
-        def move_scales(a, rows_in_quadrant):
-            for r in rows_in_quadrant:
+        def move_scales(a):
+            for r in range(4):
                 first = ROW_OF_PASS[a] + r
                 nc.sync.dma_start(out=moved[a][r:P:32, :].bitcast(I32), in_=gb[first : first + 13 : 4, :].bitcast(I32))
 
-        load_expert(1, 0, 3)
-        load_expert(0, 0, 1)
-        load_expert(0, 1, 3)
-        for a in (1, 2, 0):
-            move_scales(a, range(4))
-        load_expert(SHARED, 2, 3)
+        load_pair(2, 2)
+        move_scales(0)
+        load_shared(0, 2)
+        move_scales(1)
+        load_shared(2, 3)
+        move_scales(2)
+        load_pair(2, 0)
         gate_t = keep.tile([P, S], F32, name="gate_t")
         for lo in (2 * C, 0):
             nc.sync.dma_start(out=gate_t[:, lo : lo + 2 * C], in_=gate[:, lo : lo + 2 * C])
@@ -111,101 +111,100 @@ def tile_moe_bds_lin_none_kernel(tc, dy_words, dy_scales, w, gate, offs, pos1, p
         codes = {}
         wsc = {}
 
-        def quantise(name, runs):
-            n = sum(len(run) for run in runs)
-            grouped = keep.tile([P, n * 512], BF16, name=f"grouped{name}", tag=f"grouped{name}", align_bytes=64)
-            code_t = keep.tile([P, n * K], U32, name=f"codes{name}", align_bytes=64)
-            scale_t = keep.tile([P, n * K], U8, name=f"wsc{name}", align_bytes=64)
+        def quantise(names):
+            n = sum(len(raw[name][1]) for name in names)
+            grouped = keep.tile([P, n * 512], BF16, name=f"grouped_{names[0]}", tag=f"grouped_{names[0]}", align_bytes=64)
+            code_t = keep.tile([P, n * K], U32, name=f"codes_{names[0]}", align_bytes=64)
+            scale_t = keep.tile([P, n * K], U8, name=f"wsc_{names[0]}", align_bytes=64)
             u = 0
-            for run in runs:
-                tile, at = raw[run[0]]
+            for name in names:
+                tile, units = raw[name]
                 nc.scalar.copy(
-                    out=grouped[:, 512 * u : 512 * (u + len(run))].rearrange("p (e c i j) -> p e c j i", c=K // 4, i=4, j=4),
-                    in_=tile[:, 512 * at : 512 * (at + len(run))].rearrange("p (e j c i) -> p e c j i", j=4, c=K // 4, i=4),
+                    out=grouped[:, 512 * u : 512 * (u + len(units))].rearrange("p (e c i j) -> p e c j i", c=K // 4, i=4, j=4),
+                    in_=tile[:].rearrange("p (e j c i) -> p e c j i", j=4, c=K // 4, i=4),
                 )
-                for unit in run:
+                for unit in units:
                     codes[unit] = code_t[:, K * u : K * (u + 1)]
                     wsc[unit] = scale_t[:, K * u : K * (u + 1)]
                     u = u + 1
             nc.vector.quantize_mx(out=code_t[:].bitcast(E4M3), scales=scale_t[:], in_=grouped[:])
 
-        acc = {e: psum.tile([P, C], F32, name=f"acc{e}", tag=f"acc{e}") for e in (2, 3)}
+        def gather(dst, a, lo, hi, width):
+            window = words_t[:, T * a : T * a + width].bitcast(U32)
+            nc.vector.tensor_copy(dst, window.indirect(offs_t[:, lo // 16 : hi // 16]))
 
-        def multiply(a, e, dst, rhs, rhs_scale, order):
+        def multiply(a, e, dst, rhs, rhs_scale, first, final):
             nc.tensor.matmul_mx(
                 out=dst,
                 lhsT=codes[a, e].bitcast(E4M3),
                 lhsT_scale=wsc[a, e],
                 rhs=rhs.bitcast(E5M2),
                 rhs_scale=rhs_scale,
-                start=(a == order[0]),
-                stop=(a == order[-1]),
+                start=first,
+                stop=final,
             )
 
-        def routed(a, e, dst, rhs, slot, order):
-            multiply(a, e, dst[:], rhs, moved[a][:, slot : slot + C], order)
-
-        def gather(dst, a, lo, hi, width):
-            window = words_t[:, first_col[a] : first_col[a] + width].bitcast(U32)
-            nc.vector.tensor_copy(dst, window.indirect(offs_t[:, lo // 16 : hi // 16]))
-
-        def gather_pair(a, e, tag):
-            dst = keep.tile([P, 2 * C], U32, name=f"gw{a}_{e}", tag=tag, align_bytes=64)
-            gather(dst[:], a, C * e, C * (e + 2), WINDOW)
-            return dst
-
-        early = [gather_pair(a, 2, f"early{a}") for a in range(PASSES)]
-        quantise("a", [[(a, 2), (a, 3)] for a in range(PASSES)] + [[(0, SHARED), (1, SHARED)]])
-        for a in (1, 2, 0):
-            for e in (2, 3):
-                routed(a, e, acc[e], early[a][:, C * (e - 2) : C * (e - 1)], C * e, (1, 2, 0))
+        first_slot = {"e3": 3 * C, "e2": 2 * C, "e1": C, "head": TAIL, "tail": 0}
+        expert_of = {"e3": 3, "e2": 2, "e1": 1, "head": 0, "tail": 0}
+        last_pass = {"e3": 2, "e2": 2, "e1": 2, "head": 1, "tail": 2}
+        acc = {name: psum.tile([P, C], F32, name=f"acc_{name}") for name in first_slot}
         acc_sh = [psum.tile([P, 512], F32, name=f"acc_sh{h}") for h in range(T // 512)]
+
+        def routed(a, name, rhs):
+            slot = first_slot[name]
+            multiply(a, expert_of[name], acc[name][:], rhs, moved[a][:, slot : slot + C], a == 0, a == last_pass[name])
 
         def shared(a):
             for h in range(T // 512):
-                tokens = words_t[:, first_col[a] + 512 * h : first_col[a] + 512 * (h + 1)]
-                plane = shared_t[:, T * a + 512 * h : T * a + 512 * (h + 1)]
-                multiply(a, SHARED, acc_sh[h][:], tokens, plane, (0, 1, 2))
+                cols = slice(T * a + 512 * h, T * a + 512 * (h + 1))
+                multiply(a, SHARED, acc_sh[h][:], words_t[:, cols], shared_t[:, cols], a == 0, a == PASSES - 1)
 
+        g0 = keep.tile([P, S], U32, name="g0", align_bytes=64)
+        gather(g0[:], 0, 0, S, 2 * S)
+        quantise(["pair0_2", "pair0_0"])
+        for name in ("e2", "e3", "e1", "head", "tail"):
+            routed(0, name, g0[:, first_slot[name] : first_slot[name] + C])
+
+        g1 = keep.tile([P, 3 * C], U32, name="g1", tag="pair0_0", align_bytes=64)
+        gather(g1[:], 1, C, S, S)
+        quantise(["pair1_2", "pair1_0", "pair2_2", "shared0"])
+        for name in ("e2", "e3", "e1"):
+            routed(1, name, g1[:, first_slot[name] - C : first_slot[name]])
         shared(0)
         shared(1)
-        late0 = gather_pair(0, 0, f"rawexpert{SHARED}_0")
-        quantise("c", [[(a, 1) for a in range(PASSES)], [(0, 0)]])
-        late2 = keep.tile([P, 2 * C - TAIL], U32, name="late2", tag="rawexpert0_0", align_bytes=64)
-        gather(late2[:], 2, TAIL, 2 * C, WINDOW)
-        quantise("d", [[(1, 0), (2, 0)]])
-        quantise("e", [[(2, SHARED)]])
-        dx = keep.tile([P, S], F32, name="dx", tag="groupede", align_bytes=64)
-        copied = keep.tile([P, S], F32, name="copied", tag="rawexpert0_1", align_bytes=64)
-        for e in (2, 3):
-            cols = slice(C * e, C * (e + 1))
-            nc.scalar.copy(out=copied[:, cols], in_=acc[e][:])
-            nc.gpsimd.tensor_tensor(dx[:, cols], copied[:, cols], gate_t[:, cols], MULT)
-        acc[1] = psum.tile([P, C], F32, name="acc1")
-        acc[0] = psum.tile([P, C], F32, name="acc0")
-        acc_tail = psum.tile([P, C], F32, name="acc_tail")
-        head = C - TAIL
-        routed(0, 1, acc[1], late0[:, C:], C, (0, 2, 1))
-        routed(0, 0, acc[0], late0[:, TAIL : TAIL + C], TAIL, (0, 2, 1))
-        routed(0, 0, acc_tail, late0[:, 0:C], 0, (0, 1, 2))
-        routed(2, 1, acc[1], late2[:, head:], C, (0, 2, 1))
-        routed(2, 0, acc[0], late2[:, 0:C], TAIL, (0, 2, 1))
+
+        g2 = keep.tile([P, 2 * C], U32, name="g2", tag="shared0", align_bytes=64)
+        gather(g2[:], 2, 2 * C, S, S)
+        for name in ("e2", "e3"):
+            routed(2, name, g2[:, first_slot[name] - 2 * C : first_slot[name] - C])
+        quantise(["shared2"])
+        quantise(["pair2_0"])
         shared(2)
-        last = keep.tile([P, TAIL + 2 * C], U32, name="last", tag=f"rawexpert{SHARED}_2", align_bytes=64)
-        gather(last[:, 2 * TAIL :], 1, TAIL, 2 * C, WINDOW)
+
+        dx = keep.tile([P, S], F32, name="dx", tag="grouped_pair2_0", align_bytes=64)
+        copied = late.tile([P, S], F32, name="copied", offset=4 * 3 * C, align_bytes=64)
+        for name in ("e2", "e3"):
+            cols = slice(first_slot[name], first_slot[name] + C)
+            nc.scalar.copy(out=copied[:, cols], in_=acc[name][:])
+            nc.gpsimd.tensor_tensor(dx[:, cols], copied[:, cols], gate_t[:, cols], MULT)
+
+        last = late.tile([P, 3 * C], U32, name="last", offset=0, align_bytes=64)
+        gather(last[:, TAIL + C :], 2, TAIL, 2 * C, S)
+        routed(2, "e1", last[:, 2 * C :])
+        routed(2, "head", last[:, TAIL + C : TAIL + 2 * C])
+        gather(last[:, 2 * TAIL : TAIL + C], 1, TAIL, C, T)
+        routed(1, "head", last[:, 2 * TAIL : 2 * TAIL + C])
         gather(last[:, TAIL : 2 * TAIL], 1, 0, TAIL, T)
+        routed(1, "tail", last[:, TAIL : TAIL + C])
         gather(last[:, 0:TAIL], 2, 0, TAIL, T)
-        routed(1, 1, acc[1], last[:, TAIL + C :], C, (0, 2, 1))
-        routed(1, 0, acc[0], last[:, 2 * TAIL : 2 * TAIL + C], TAIL, (0, 2, 1))
-        routed(1, 0, acc_tail, last[:, TAIL : TAIL + C], 0, (0, 1, 2))
-        routed(2, 0, acc_tail, last[:, 0:C], 0, (0, 1, 2))
+        routed(2, "tail", last[:, 0:C])
 
         ds = copied[:, 0:T]
         for h in range(T // 512):
             nc.scalar.copy(out=ds[:, 512 * h : 512 * (h + 1)], in_=acc_sh[h][:])
-        nc.vector.tensor_tensor(dx[:, C : 2 * C], acc[1][:], gate_t[:, C : 2 * C], MULT)
-        nc.vector.tensor_tensor(dx[:, TAIL:C], acc[0][:, 0:head], gate_t[:, TAIL:C], MULT)
-        nc.vector.tensor_tensor(dx[:, 0:TAIL], acc_tail[:, 0:TAIL], gate_t[:, 0:TAIL], MULT)
+        nc.vector.tensor_tensor(dx[:, C : 2 * C], acc["e1"][:], gate_t[:, C : 2 * C], MULT)
+        nc.vector.tensor_tensor(dx[:, TAIL:C], acc["head"][:, 0 : C - TAIL], gate_t[:, TAIL:C], MULT)
+        nc.vector.tensor_tensor(dx[:, 0:TAIL], acc["tail"][:, 0:TAIL], gate_t[:, 0:TAIL], MULT)
 
         part = keep.tile([P, T], F32, name="part")
         for lo, hi in ((0, FIRST), (FIRST, T)):

@@ -63,45 +63,41 @@ def tile_moe_bds_lin_none_kernel(tc, dy_words, dy_scales, w, gate, offs, pos1, p
         raw = {}
 
         def load_w(name, units, source):
-            if name == "pair2_0":
+            if name == "w2_0":
                 raw[name] = (late.tile([P, len(units) * 512], F32, name=name, offset=4 * 2 * C, align_bytes=64), units)
             else:
                 raw[name] = (keep.tile([P, len(units) * 512], F32, name=name, tag=name, align_bytes=64), units)
             nc.sync.dma_start(out=raw[name][0][:].rearrange("p (u x) -> p u x", x=512), in_=source)
 
-        def load_pair(a, e):
-            load_w(f"pair{a}_{e}", [(a, e), (a, e + 1)], w[e : e + 2, 512 * a : 512 * (a + 1), :].rearrange("e (p j) k -> p e (j k)", j=4))
+        def load_experts(a, lo, hi):
+            load_w(f"w{a}_{lo}", [(a, e) for e in range(lo, hi)], w[lo:hi, 512 * a : 512 * (a + 1), :].rearrange("e (p j) k -> p e (j k)", j=4))
 
-        def load_shared(lo, hi):
-            source = w[SHARED].rearrange("(a p j) k -> p a (j k)", a=PASSES, j=4)
-            load_w(f"shared{lo}", [(a, SHARED) for a in range(lo, hi)], source[:, lo:hi, :])
-
-        load_pair(0, 2)
-        for a in range(PASSES):
-            load_words(a)
-        load_pair(0, 0)
-        load_pair(1, 2)
-        load_pair(1, 0)
+        load_experts(2, 2, 4)
+        load_words(2)
+        load_experts(1, 1, 4)
+        load_words(1)
+        load_w("shared", [(a, SHARED) for a in range(PASSES)], w[SHARED].rearrange("(a p j) k -> p a (j k)", a=PASSES, j=4))
+        load_words(0)
 
         gb = keep.tile([P, S], U8, name="gb", align_bytes=64)
         nc.vector.tensor_copy(gb[:], scales_t[:].indirect(offs_t[:]))
 
-        planes01 = keep.tile([P, 2 * S], U8, name="planes01", tag="pair0_2", align_bytes=64)
-        plane2 = keep.tile([P, S], U8, name="plane2", tag="pair1_2", align_bytes=64)
-        moved = [planes01[:, 0:S], planes01[:, S : 2 * S], plane2[:]]
+        planes12 = keep.tile([P, 2 * S], U8, name="planes12", tag="w2_2", align_bytes=64)
+        plane0 = keep.tile([P, S], U8, name="plane0", tag="w1_1", align_bytes=64)
+        moved = [plane0[:], planes12[:, 0:S], planes12[:, S : 2 * S]]
 
         def move_scales(a):
             for r in range(4):
                 first = ROW_OF_PASS[a] + r
                 nc.sync.dma_start(out=moved[a][r:P:32, :].bitcast(I32), in_=gb[first : first + 13 : 4, :].bitcast(I32))
 
-        load_pair(2, 2)
-        move_scales(0)
-        load_shared(0, 2)
-        move_scales(1)
-        load_shared(2, 3)
+        load_experts(0, 2, 4)
         move_scales(2)
-        load_pair(2, 0)
+        load_experts(0, 0, 2)
+        move_scales(1)
+        load_experts(1, 0, 1)
+        load_experts(2, 0, 2)
+        move_scales(0)
         gate_t = keep.tile([P, S], F32, name="gate_t")
         for lo in (2 * C, 0):
             nc.sync.dma_start(out=gate_t[:, lo : lo + 2 * C], in_=gate[:, lo : lo + 2 * C])
@@ -146,42 +142,41 @@ def tile_moe_bds_lin_none_kernel(tc, dy_words, dy_scales, w, gate, offs, pos1, p
 
         first_slot = {"e3": 3 * C, "e2": 2 * C, "e1": C, "head": TAIL, "tail": 0}
         expert_of = {"e3": 3, "e2": 2, "e1": 1, "head": 0, "tail": 0}
-        last_pass = {"e3": 2, "e2": 2, "e1": 2, "head": 1, "tail": 2}
+        first_pass = {"e3": 2, "e2": 2, "e1": 1, "head": 0, "tail": 0}
+        last_pass = {"e3": 0, "e2": 0, "e1": 2, "head": 1, "tail": 2}
         acc = {name: psum.tile([P, C], F32, name=f"acc_{name}") for name in first_slot}
         acc_sh = [psum.tile([P, 512], F32, name=f"acc_sh{h}") for h in range(T // 512)]
 
         def routed(a, name, rhs):
             slot = first_slot[name]
-            multiply(a, expert_of[name], acc[name][:], rhs, moved[a][:, slot : slot + C], a == 0, a == last_pass[name])
+            multiply(a, expert_of[name], acc[name][:], rhs, moved[a][:, slot : slot + C], a == first_pass[name], a == last_pass[name])
 
         def shared(a):
             for h in range(T // 512):
                 cols = slice(T * a + 512 * h, T * a + 512 * (h + 1))
                 multiply(a, SHARED, acc_sh[h][:], words_t[:, cols], shared_t[:, cols], a == 0, a == PASSES - 1)
 
-        g0 = keep.tile([P, S], U32, name="g0", align_bytes=64)
-        gather(g0[:], 0, 0, S, 2 * S)
-        quantise(["pair0_2", "pair0_0"])
-        for name in ("e2", "e3", "e1", "head", "tail"):
-            routed(0, name, g0[:, first_slot[name] : first_slot[name] + C])
-
-        g1 = keep.tile([P, 3 * C], U32, name="g1", tag="pair0_0", align_bytes=64)
-        gather(g1[:], 1, C, S, S)
-        quantise(["pair1_2", "pair1_0", "pair2_2", "shared0"])
-        for name in ("e2", "e3", "e1"):
-            routed(1, name, g1[:, first_slot[name] - C : first_slot[name]])
-        shared(0)
-        shared(1)
-
-        g2 = keep.tile([P, 2 * C], U32, name="g2", tag="shared0", align_bytes=64)
+        g2 = keep.tile([P, 2 * C], U32, name="g2", align_bytes=64)
         gather(g2[:], 2, 2 * C, S, S)
+        g1 = keep.tile([P, 3 * C], U32, name="g1", align_bytes=64)
+        gather(g1[:], 1, C, S, S)
+        quantise(["w2_2", "w1_1", "shared"])
         for name in ("e2", "e3"):
             routed(2, name, g2[:, first_slot[name] - 2 * C : first_slot[name] - C])
-        quantise(["shared2"])
-        quantise(["pair2_0"])
-        shared(2)
+        for name in ("e2", "e3", "e1"):
+            routed(1, name, g1[:, first_slot[name] - C : first_slot[name]])
+        for a in range(PASSES):
+            shared(a)
 
-        dx = keep.tile([P, S], F32, name="dx", tag="grouped_pair2_0", align_bytes=64)
+        g0 = keep.tile([P, S], U32, name="g0", tag="shared", align_bytes=64)
+        gather(g0[:], 0, 0, S, 2 * S)
+        quantise(["w0_2", "w0_0"])
+        for name in ("e2", "e3", "e1", "head", "tail"):
+            routed(0, name, g0[:, first_slot[name] : first_slot[name] + C])
+        quantise(["w1_0"])
+        quantise(["w2_0"])
+
+        dx = keep.tile([P, S], F32, name="dx", tag="grouped_w2_0", align_bytes=64)
         copied = late.tile([P, S], F32, name="copied", offset=4 * 3 * C, align_bytes=64)
         for name in ("e2", "e3"):
             cols = slice(first_slot[name], first_slot[name] + C)

@@ -92,12 +92,11 @@ def tile_moe_bds_lin_none_kernel(tc, dy_words, dy_scales, w, gate, offs, pos1, p
                 nc.sync.dma_start(out=moved[a][r:P:32, :].bitcast(I32), in_=gb[first : first + 13 : 4, :].bitcast(I32))
 
         load_experts(0, 2, 4)
-        move_scales(2)
         load_experts(0, 0, 2)
-        move_scales(1)
         load_experts(1, 0, 1)
         load_experts(2, 0, 2)
-        move_scales(0)
+        for a in (2, 1, 0):
+            move_scales(a)
         gate_t = keep.tile([P, S], F32, name="gate_t")
         for lo in (2 * C, 0):
             nc.sync.dma_start(out=gate_t[:, lo : lo + 2 * C], in_=gate[:, lo : lo + 2 * C])

@@ -22,6 +22,7 @@ S = E * C
 SHARED = E
 ROW_OF_PASS = (32, 48, 112)
 TAIL = 128
+LENT = 256
 FIRST = 640
 CHUNKS = (640, 256, 128)
 
@@ -193,10 +194,13 @@ def tile_moe_bds_lin_none_kernel(tc, dy_words, dy_scales, w, gate, offs, pos1, p
         gather(last[:, 0:TAIL], 2, 0, TAIL, T)
         routed(2, "tail", last[:, 0:C])
 
+        lent = keep.tile([P, LENT], F32, name="lent", align_bytes=64)
+        nc.scalar.copy(out=lent[:], in_=acc["e1"][:, C - LENT : C])
+        nc.gpsimd.tensor_tensor(dx[:, 2 * C - LENT : 2 * C], lent[:], gate_t[:, 2 * C - LENT : 2 * C], MULT)
         ds = copied[:, 0:T]
         for h in range(T // 512):
             nc.scalar.copy(out=ds[:, 512 * h : 512 * (h + 1)], in_=acc_sh[h][:])
-        nc.vector.tensor_tensor(dx[:, C : 2 * C], acc["e1"][:], gate_t[:, C : 2 * C], MULT)
+        nc.vector.tensor_tensor(dx[:, C : 2 * C - LENT], acc["e1"][:, 0 : C - LENT], gate_t[:, C : 2 * C - LENT], MULT)
         nc.vector.tensor_tensor(dx[:, TAIL:C], acc["head"][:, 0 : C - TAIL], gate_t[:, TAIL:C], MULT)
         nc.vector.tensor_tensor(dx[:, 0:TAIL], acc["tail"][:, 0:TAIL], gate_t[:, 0:TAIL], MULT)
 

@@ -75,16 +75,17 @@ def tile_moe_bds_lin_none_kernel(tc, dy_words, dy_scales, w, gate, offs, pos1, p
 
         load_experts(2, 2, 4)
         load_words(2)
-        load_experts(1, 1, 4)
-        load_words(1)
         load_w("shared", [(a, SHARED) for a in range(PASSES)], w[SHARED].rearrange("(a p j) k -> p a (j k)", a=PASSES, j=4))
+        load_words(1)
+        load_experts(1, 2, 4)
+        load_experts(1, 1, 2)
         load_words(0)
 
         gb = keep.tile([P, S], U8, name="gb", align_bytes=64)
         nc.vector.tensor_copy(gb[:], scales_t[:].indirect(offs_t[:]))
 
         planes12 = keep.tile([P, 2 * S], U8, name="planes12", tag="w2_2", align_bytes=64)
-        plane0 = keep.tile([P, S], U8, name="plane0", tag="w1_1", align_bytes=64)
+        plane0 = keep.tile([P, S], U8, name="plane0", tag="shared", align_bytes=64)
         moved = [plane0[:], planes12[:, 0:S], planes12[:, S : 2 * S]]
 
         def move_scales(a):
@@ -160,7 +161,7 @@ def tile_moe_bds_lin_none_kernel(tc, dy_words, dy_scales, w, gate, offs, pos1, p
         gather(g2[:], 2, 2 * C, S, S)
         g1 = keep.tile([P, 3 * C], U32, name="g1", align_bytes=64)
         gather(g1[:], 1, C, S, S)
-        quantise(["w2_2", "w1_1", "shared"])
+        quantise(["w2_2", "shared", "w1_2", "w1_1"])
         for name in ("e2", "e3"):
             routed(2, name, g2[:, first_slot[name] - 2 * C : first_slot[name] - C])
         for name in ("e2", "e3", "e1"):
@@ -168,7 +169,7 @@ def tile_moe_bds_lin_none_kernel(tc, dy_words, dy_scales, w, gate, offs, pos1, p
         for a in range(PASSES):
             shared(a)
 
-        g0 = keep.tile([P, S], U32, name="g0", tag="shared", align_bytes=64)
+        g0 = keep.tile([P, S], U32, name="g0", tag="w1_1", align_bytes=64)
         gather(g0[:], 0, 0, S, 2 * S)
         quantise(["w0_2", "w0_0"])
         for name in ("e2", "e3", "e1", "head", "tail"):

@@ -64,8 +64,8 @@ def tile_moe_bds_lin_none_kernel(tc, dy_words, dy_scales, w, gate, offs, pos1, p
         raw = {}
 
         def load_w(name, units, source):
-            if name == "w2_0":
-                raw[name] = (late.tile([P, len(units) * 512], F32, name=name, offset=4 * 2 * C, align_bytes=64), units)
+            if name == "w1_0":
+                raw[name] = (late.tile([P, len(units) * 512], F32, name=name, offset=4 * 5 * C // 2, align_bytes=64), units)
             else:
                 raw[name] = (keep.tile([P, len(units) * 512], F32, name=name, tag=name, align_bytes=64), units)
             nc.sync.dma_start(out=raw[name][0][:].rearrange("p (u x) -> p u x", x=512), in_=source)
@@ -95,8 +95,8 @@ def tile_moe_bds_lin_none_kernel(tc, dy_words, dy_scales, w, gate, offs, pos1, p
 
         load_experts(0, 2, 4)
         load_experts(0, 0, 2)
-        load_experts(1, 0, 1)
         load_experts(2, 0, 2)
+        load_experts(1, 0, 1)
         for a in (2, 1, 0):
             move_scales(a)
         gate_t = keep.tile([P, S], F32, name="gate_t")
@@ -171,13 +171,15 @@ def tile_moe_bds_lin_none_kernel(tc, dy_words, dy_scales, w, gate, offs, pos1, p
 
         g0 = keep.tile([P, S], U32, name="g0", tag="w1_1", align_bytes=64)
         gather(g0[:], 0, 0, S, 2 * S)
-        quantise(["w0_2", "w0_0"])
-        for name in ("e2", "e3", "e1", "head", "tail"):
+        quantise(["w0_2"])
+        for name in ("e2", "e3"):
+            routed(0, name, g0[:, first_slot[name] : first_slot[name] + C])
+        quantise(["w0_0", "w2_0"])
+        for name in ("e1", "head", "tail"):
             routed(0, name, g0[:, first_slot[name] : first_slot[name] + C])
         quantise(["w1_0"])
-        quantise(["w2_0"])
 
-        dx = keep.tile([P, S], F32, name="dx", tag="grouped_w2_0", align_bytes=64)
+        dx = keep.tile([P, S], F32, name="dx", tag="grouped_w1_0", align_bytes=64)
         copied = late.tile([P, S], F32, name="copied", offset=4 * 3 * C, align_bytes=64)
         for name in ("e2", "e3"):
             cols = slice(first_slot[name], first_slot[name] + C)

@@ -15,16 +15,15 @@ E4M3 = mybir.dt.float8_e4m3fn_x4
 E5M2 = mybir.dt.float8_e5m2_x4
 ADD = mybir.AluOpType.add
 MULT = mybir.AluOpType.mult
+COPY = mybir.ActivationFunctionType.Copy
 
 P = 128
 PASSES = N // 512
 S = E * C
 SHARED = E
 ROW_OF_PASS = (32, 48, 112)
-TAIL = 128
-LENT = 256
-FIRST = 640
-CHUNKS = (640, 256, 128)
+HEAD = 384
+STORES = (0, 448, 704, 896, 1024)
 
 
 def tile_moe_bds_lin_none_kernel(tc, dy_words, dy_scales, w, gate, offs, pos1, pos2, out):
@@ -38,13 +37,11 @@ def tile_moe_bds_lin_none_kernel(tc, dy_words, dy_scales, w, gate, offs, pos1, p
         pos1_t = keep.tile([P, T // 16], U16, name="pos1_t")
         pos2_t = keep.tile([P, T // 16], U16, name="pos2_t")
 
-        scales_t = keep.tile([P, 2 * S], U8, name="scales_t", tag="scales", align_bytes=64)
-        words_t = keep.tile([P, 2 * S], I32, name="words_t", align_bytes=64)
+        scales_t = keep.tile([P, 2 * S], U8, name="scales_t", align_bytes=64)
+        words_t = keep.tile([P, (PASSES + 1) * T], I32, name="words_t", align_bytes=64)
         nc.vector.memset(scales_t[0:32, 0:T].bitcast(I32), 0)
         nc.vector.memset(scales_t[64:112, 0:T].bitcast(I32), 0)
         nc.vector.memset(scales_t[:, T:].bitcast(I32), 0)
-        shared_t = keep.tile([P, PASSES * T], U8, name="shared_t", align_bytes=64)
-        nc.vector.memset(shared_t[:].bitcast(I32), 0)
         nc.vector.memset(words_t[:, PASSES * T :], 0)
 
         sc32 = dy_scales.bitcast(I32)
@@ -52,11 +49,6 @@ def tile_moe_bds_lin_none_kernel(tc, dy_words, dy_scales, w, gate, offs, pos1, p
         nc.sync.dma_start(offs_t[:], offs)
         nc.sync.dma_start(out=scales_t[32:64, 0:T].bitcast(I32), in_=rows[0:32, :])
         nc.sync.dma_start(out=scales_t[112:P, 0:T].bitcast(I32), in_=rows[32:48, :])
-        for r in range(4):
-            nc.scalar.dma_start(
-                out=shared_t[r:P:32, :].bitcast(I32).rearrange("q (a t) -> q a t", a=PASSES),
-                in_=sc32[:, r:16:4, :].rearrange("a q t -> q a t"),
-            )
 
         def load_words(a):
             nc.sync.dma_start(out=words_t[:, T * a : T * (a + 1)], in_=dy_words[a].rearrange("p t d -> p (t d)").bitcast(I32))
@@ -64,49 +56,65 @@ def tile_moe_bds_lin_none_kernel(tc, dy_words, dy_scales, w, gate, offs, pos1, p
         raw = {}
 
         def load_w(name, units, source):
-            if name == "w1_0":
-                raw[name] = (late.tile([P, len(units) * 512], F32, name=name, offset=4 * 5 * C // 2, align_bytes=64), units)
+            if name == "last":
+                tile = late.tile([P, len(units) * 512], F32, name=name, offset=4 * S - 1024, align_bytes=64)
             else:
-                raw[name] = (keep.tile([P, len(units) * 512], F32, name=name, tag=name, align_bytes=64), units)
-            nc.sync.dma_start(out=raw[name][0][:].rearrange("p (u x) -> p u x", x=512), in_=source)
+                tile = keep.tile([P, len(units) * 512], F32, name=name, tag=name, align_bytes=64)
+            raw[name] = (tile, units)
+            nc.sync.dma_start(out=tile[:].rearrange("p (u x) -> p u x", x=512), in_=source)
 
-        def load_experts(a, lo, hi):
-            load_w(f"w{a}_{lo}", [(a, e) for e in range(lo, hi)], w[lo:hi, 512 * a : 512 * (a + 1), :].rearrange("e (p j) k -> p e (j k)", j=4))
+        def load_pass(name, a, lo, hi):
+            load_w(name, [(a, e) for e in range(lo, hi)], w[lo:hi, 512 * a : 512 * (a + 1), :].rearrange("e (p j) k -> p e (j k)", j=4))
 
-        load_experts(2, 2, 4)
+        def load_expert(name, e):
+            load_w(name, [(a, e) for a in range(PASSES)], w[e].rearrange("(a p j) k -> p a (j k)", a=PASSES, j=4))
+
         load_words(2)
-        load_w("shared", [(a, SHARED) for a in range(PASSES)], w[SHARED].rearrange("(a p j) k -> p a (j k)", a=PASSES, j=4))
+        load_pass("pass2", 2, 1, 4)
         load_words(1)
-        load_experts(1, 2, 4)
-        load_experts(1, 1, 2)
+        load_pass("pass1", 1, 1, 4)
+        load_pass("pass0", 0, 2, 4)
+        load_expert("shared", SHARED)
         load_words(0)
+        load_expert("expert0", 0)
+        load_pass("last", 0, 1, 2)
 
         gb = keep.tile([P, S], U8, name="gb", align_bytes=64)
         nc.vector.tensor_copy(gb[:], scales_t[:].indirect(offs_t[:]))
 
-        planes12 = keep.tile([P, 2 * S], U8, name="planes12", tag="w2_2", align_bytes=64)
-        plane0 = keep.tile([P, S], U8, name="plane0", tag="shared", align_bytes=64)
+        planes12 = keep.tile([P, 2 * S], U8, name="planes12", tag="pass2", align_bytes=64)
+        plane0 = keep.tile([P, S], U8, name="plane0", tag="pass1", align_bytes=64)
         moved = [plane0[:], planes12[:, 0:S], planes12[:, S : 2 * S]]
-
-        def move_scales(a):
+        for a in (2, 1, 0):
             for r in range(4):
                 first = ROW_OF_PASS[a] + r
                 nc.sync.dma_start(out=moved[a][r:P:32, :].bitcast(I32), in_=gb[first : first + 13 : 4, :].bitcast(I32))
 
-        load_experts(0, 2, 4)
-        load_experts(0, 0, 2)
-        load_experts(2, 0, 2)
-        load_experts(1, 0, 1)
-        for a in (2, 1, 0):
-            move_scales(a)
         gate_t = keep.tile([P, S], F32, name="gate_t")
-        for lo in (2 * C, 0):
-            nc.sync.dma_start(out=gate_t[:, lo : lo + 2 * C], in_=gate[:, lo : lo + 2 * C])
+        nc.sync.dma_start(out=gate_t[:, 2 * C :], in_=gate[:, 2 * C :])
+        shared_t = keep.tile([P, PASSES * T], U8, name="shared_t", tag="shared", align_bytes=64)
+        for r in range(4):
+            nc.sync.dma_start(
+                out=shared_t[r:P:32, :].bitcast(I32).rearrange("q (a t) -> q a t", a=PASSES),
+                in_=sc32[:, r:16:4, :].rearrange("a q t -> q a t"),
+            )
+        nc.sync.dma_start(out=gate_t[:, 0 : 2 * C], in_=gate[:, 0 : 2 * C])
         nc.sync.dma_start(pos1_t[:], pos1)
         nc.sync.dma_start(pos2_t[:], pos2)
 
         codes = {}
         wsc = {}
+
+        def interleave(dst, src, by_activation):
+            if by_activation:
+                nc.scalar.activation(
+                    dst.rearrange("p (c i j) -> p c j i", i=4, j=4), src.rearrange("p (j c i) -> p c j i", j=4, i=4), COPY
+                )
+            else:
+                nc.scalar.copy(
+                    out=dst.rearrange("p (e c i j) -> p e c j i", c=K // 4, i=4, j=4),
+                    in_=src.rearrange("p (e j c i) -> p e c j i", j=4, c=K // 4, i=4),
+                )
 
         def quantise(names):
             n = sum(len(raw[name][1]) for name in names)
@@ -116,10 +124,12 @@ def tile_moe_bds_lin_none_kernel(tc, dy_words, dy_scales, w, gate, offs, pos1, p
             u = 0
             for name in names:
                 tile, units = raw[name]
-                nc.scalar.copy(
-                    out=grouped[:, 512 * u : 512 * (u + len(units))].rearrange("p (e c i j) -> p e c j i", c=K // 4, i=4, j=4),
-                    in_=tile[:].rearrange("p (e j c i) -> p e c j i", j=4, c=K // 4, i=4),
-                )
+                lo, hi = 512 * u, 512 * (u + len(units))
+                if name == "pass2":
+                    interleave(grouped[:, lo : lo + 512], tile[:, 0:512], True)
+                    interleave(grouped[:, lo + 512 : hi], tile[:, 512:], False)
+                else:
+                    interleave(grouped[:, lo:hi], tile[:], False)
                 for unit in units:
                     codes[unit] = code_t[:, K * u : K * (u + 1)]
                     wsc[unit] = scale_t[:, K * u : K * (u + 1)]
@@ -141,78 +151,82 @@ def tile_moe_bds_lin_none_kernel(tc, dy_words, dy_scales, w, gate, offs, pos1, p
                 stop=final,
             )
 
-        first_slot = {"e3": 3 * C, "e2": 2 * C, "e1": C, "head": TAIL, "tail": 0}
-        expert_of = {"e3": 3, "e2": 2, "e1": 1, "head": 0, "tail": 0}
-        first_pass = {"e3": 2, "e2": 2, "e1": 1, "head": 0, "tail": 0}
-        last_pass = {"e3": 0, "e2": 0, "e1": 2, "head": 1, "tail": 2}
-        acc = {name: psum.tile([P, C], F32, name=f"acc_{name}") for name in first_slot}
-        acc_sh = [psum.tile([P, 512], F32, name=f"acc_sh{h}") for h in range(T // 512)]
+        acc = {e: psum.tile([P, C], F32, name=f"acc{e}") for e in (2, 3, 1)}
+        early = {}
+        for a in (2, 1):
+            early[a] = keep.tile([P, 3 * C], U32, name=f"early{a}", align_bytes=64)
+            gather(early[a][:], a, C, S, S)
+        quantise(["pass2", "pass1", "pass0"])
+        for a in (2, 1):
+            for e in (2, 3):
+                multiply(a, e, acc[e][:], early[a][:, C * (e - 1) : C * e], moved[a][:, C * e : C * (e + 1)], a == 2, False)
+        g0 = keep.tile([P, 2 * C], U32, name="g0", tag="pass0", align_bytes=64)
+        gather(g0[:], 0, 2 * C, S, S)
+        for e in (2, 3):
+            multiply(0, e, acc[e][:], g0[:, C * (e - 2) : C * (e - 1)], moved[0][:, C * e : C * (e + 1)], False, True)
+        quantise(["shared"])
+        quantise(["expert0", "last"])
 
-        def routed(a, name, rhs):
-            slot = first_slot[name]
-            multiply(a, expert_of[name], acc[name][:], rhs, moved[a][:, slot : slot + C], a == first_pass[name], a == last_pass[name])
+        dx = keep.tile([P, S], F32, name="dx", tag="grouped_expert0", align_bytes=64)
+        copied = late.tile([P, 3 * C + T], F32, name="copied", offset=4 * S, align_bytes=64)
+        last = late.tile([P, S], U32, name="last_words", offset=0, align_bytes=64)
 
-        def shared(a):
-            for h in range(T // 512):
-                cols = slice(T * a + 512 * h, T * a + 512 * (h + 1))
-                multiply(a, SHARED, acc_sh[h][:], words_t[:, cols], shared_t[:, cols], a == 0, a == PASSES - 1)
+        def lend(e):
+            cols = slice(C * e, C * (e + 1))
+            nc.scalar.copy(out=copied[:, C * (e - 1) : C * e], in_=acc[e][:])
+            nc.gpsimd.tensor_tensor(dx[:, cols], copied[:, C * (e - 1) : C * e], gate_t[:, cols], MULT)
 
-        g2 = keep.tile([P, 2 * C], U32, name="g2", align_bytes=64)
-        gather(g2[:], 2, 2 * C, S, S)
-        g1 = keep.tile([P, 3 * C], U32, name="g1", align_bytes=64)
-        gather(g1[:], 1, C, S, S)
-        quantise(["w2_2", "shared", "w1_2", "w1_1"])
-        for name in ("e2", "e3"):
-            routed(2, name, g2[:, first_slot[name] - 2 * C : first_slot[name] - C])
-        for name in ("e2", "e3", "e1"):
-            routed(1, name, g1[:, first_slot[name] - C : first_slot[name]])
-        for a in range(PASSES):
-            shared(a)
+        lend(2)
+        lend(3)
+        gather(last[:, 3 * C :], 0, C, 2 * C, T)
+        multiply(0, 1, acc[1][:], last[:, 3 * C :], moved[0][:, C : 2 * C], True, False)
+        for a in (2, 1):
+            multiply(a, 1, acc[1][:], early[a][:, 0:C], moved[a][:, C : 2 * C], False, a == 1)
+        lend(1)
 
-        g0 = keep.tile([P, S], U32, name="g0", tag="w1_1", align_bytes=64)
-        gather(g0[:], 0, 0, S, 2 * S)
-        quantise(["w0_2"])
-        for name in ("e2", "e3"):
-            routed(0, name, g0[:, first_slot[name] : first_slot[name] + C])
-        quantise(["w0_0", "w2_0"])
-        for name in ("e1", "head", "tail"):
-            routed(0, name, g0[:, first_slot[name] : first_slot[name] + C])
-        quantise(["w1_0"])
+        ds = copied[:, 3 * C :]
+        for h, (lo, hi) in enumerate(((0, 256), (256, 512), (512, T))):
+            acc_sh = psum.tile([P, 512], F32, name=f"acc_sh{h}", tag=f"twice{h}")
+            for a in range(PASSES):
+                cols = slice(T * a + lo, T * a + hi)
+                multiply(a, SHARED, acc_sh[:, 0 : hi - lo], words_t[:, cols], shared_t[:, cols], a == 0, a == PASSES - 1)
+            nc.scalar.copy(out=ds[:, lo:hi], in_=acc_sh[:, 0 : hi - lo])
 
-        dx = keep.tile([P, S], F32, name="dx", tag="grouped_w1_0", align_bytes=64)
-        copied = late.tile([P, S], F32, name="copied", offset=4 * 3 * C, align_bytes=64)
-        for name in ("e2", "e3"):
-            cols = slice(first_slot[name], first_slot[name] + C)
-            nc.scalar.copy(out=copied[:, cols], in_=acc[name][:])
-            nc.gpsimd.tensor_tensor(dx[:, cols], copied[:, cols], gate_t[:, cols], MULT)
+        head = psum.tile([P, C], F32, name="head", tag="twice0")
+        tail = psum.tile([P, C], F32, name="tail", tag="twice1")
+        for a in (0, 1):
+            gather(last[:, C * a : C * (a + 1)], a, 0, C, T)
+            multiply(a, 0, head[:], last[:, C * a : C * (a + 1)], moved[a][:, 0:C], a == 0, False)
+            multiply(a, 0, tail[:, HEAD:C], last[:, C * a + HEAD : C * (a + 1)], moved[a][:, HEAD:C], a == 0, False)
+        gather(last[:, 2 * C : 2 * C + HEAD], 2, 0, HEAD, T)
+        for lo, hi in ((0, 256), (256, HEAD)):
+            multiply(2, 0, head[:, lo:hi], last[:, 2 * C + lo : 2 * C + hi], moved[2][:, lo:hi], False, hi == HEAD)
+        gather(last[:, 2 * C + HEAD : 3 * C], 2, HEAD, C, T)
+        multiply(2, 0, tail[:, HEAD:C], last[:, 2 * C + HEAD : 3 * C], moved[2][:, HEAD:C], False, True)
+        nc.vector.tensor_tensor(dx[:, 0:HEAD], head[:, 0:HEAD], gate_t[:, 0:HEAD], MULT)
+        nc.vector.tensor_tensor(dx[:, HEAD:C], tail[:, HEAD:C], gate_t[:, HEAD:C], MULT)
 
-        last = late.tile([P, 3 * C], U32, name="last", offset=0, align_bytes=64)
-        gather(last[:, TAIL + C :], 2, TAIL, 2 * C, S)
-        routed(2, "e1", last[:, 2 * C :])
-        routed(2, "head", last[:, TAIL + C : TAIL + 2 * C])
-        gather(last[:, 2 * TAIL : TAIL + C], 1, TAIL, C, T)
-        routed(1, "head", last[:, 2 * TAIL : 2 * TAIL + C])
-        gather(last[:, TAIL : 2 * TAIL], 1, 0, TAIL, T)
-        routed(1, "tail", last[:, TAIL : TAIL + C])
-        gather(last[:, 0:TAIL], 2, 0, TAIL, T)
-        routed(2, "tail", last[:, 0:C])
+        def fetch(dst, pos_t, lo, hi):
+            nc.scalar.activation(dst, dx[:].indirect(pos_t[:, lo // 16 : hi // 16]), COPY)
 
-        lent = keep.tile([P, LENT], F32, name="lent", align_bytes=64)
-        nc.scalar.copy(out=lent[:], in_=acc["e1"][:, C - LENT : C])
-        nc.gpsimd.tensor_tensor(dx[:, 2 * C - LENT : 2 * C], lent[:], gate_t[:, 2 * C - LENT : 2 * C], MULT)
-        ds = copied[:, 0:T]
-        for h in range(T // 512):
-            nc.scalar.copy(out=ds[:, 512 * h : 512 * (h + 1)], in_=acc_sh[h][:])
-        nc.vector.tensor_tensor(dx[:, C : 2 * C - LENT], acc["e1"][:, 0 : C - LENT], gate_t[:, C : 2 * C - LENT], MULT)
-        nc.vector.tensor_tensor(dx[:, TAIL:C], acc["head"][:, 0 : C - TAIL], gate_t[:, TAIL:C], MULT)
-        nc.vector.tensor_tensor(dx[:, 0:TAIL], acc["tail"][:, 0:TAIL], gate_t[:, 0:TAIL], MULT)
-
+        t0, t1, t2, t3, t4 = STORES
+        second = keep.tile([P, T], F32, name="second")
+        first = keep.tile([P, t4 - t3], F32, name="first")
         part = keep.tile([P, T], F32, name="part")
-        for lo, hi in ((0, FIRST), (FIRST, T)):
+        full = keep.tile([P, T], F32, name="full")
+
+        def finish(lo, hi):
+            nc.vector.tensor_tensor(full[:, lo:hi], part[:, lo:hi], second[:, lo:hi], ADD)
+            nc.sync.dma_start(out=out[:, lo:hi], in_=full[:, lo:hi])
+
+        fetch(second[:, t0:t1], pos2_t, t0, t1)
+        fetch(first[:], pos1_t, t3, t4)
+        fetch(second[:, t1:t3], pos2_t, t1, t3)
+        fetch(second[:, t3:t4], pos2_t, t3, t4)
+        for lo, hi in ((t0, t1), (t1, t3)):
             nc.vector.tensor_tensor(part[:, lo:hi], dx[:].indirect(pos1_t[:, lo // 16 : hi // 16]), ds[:, lo:hi], ADD)
-        t0 = 0
-        for i, n in enumerate(CHUNKS):
-            full = keep.tile([P, n], F32, name=f"full{i}")
-            nc.vector.tensor_tensor(full[:], dx[:].indirect(pos2_t[:, t0 // 16 : (t0 + n) // 16]), part[:, t0 : t0 + n], ADD)
-            nc.sync.dma_start(out=out[:, t0 : t0 + n], in_=full[:])
-            t0 = t0 + n
+        finish(t0, t1)
+        nc.vector.tensor_tensor(part[:, t3:t4], first[:], ds[:, t3:t4], ADD)
+        finish(t1, t2)
+        finish(t2, t3)
+        finish(t3, t4)

@@ -22,8 +22,9 @@ PASSES = N // 512
 S = E * C
 SHARED = E
 ROW_OF_PASS = (32, 48, 112)
-HEAD = 384
-STORES = (0, 448, 704, 896, 1024)
+HEAD = 256
+STORES = (0, 384, 640, 896, 1024)
+BOTH = 128
 
 
 def tile_moe_bds_lin_none_kernel(tc, dy_words, dy_scales, w, gate, offs, pos1, pos2, out):
@@ -196,11 +197,10 @@ def tile_moe_bds_lin_none_kernel(tc, dy_words, dy_scales, w, gate, offs, pos1, p
         tail = psum.tile([P, C], F32, name="tail", tag="twice1")
         for a in (0, 1):
             gather(last[:, C * a : C * (a + 1)], a, 0, C, T)
-            multiply(a, 0, head[:], last[:, C * a : C * (a + 1)], moved[a][:, 0:C], a == 0, False)
+            multiply(a, 0, head[:, 0:HEAD], last[:, C * a : C * a + HEAD], moved[a][:, 0:HEAD], a == 0, False)
             multiply(a, 0, tail[:, HEAD:C], last[:, C * a + HEAD : C * (a + 1)], moved[a][:, HEAD:C], a == 0, False)
         gather(last[:, 2 * C : 2 * C + HEAD], 2, 0, HEAD, T)
-        for lo, hi in ((0, 256), (256, HEAD)):
-            multiply(2, 0, head[:, lo:hi], last[:, 2 * C + lo : 2 * C + hi], moved[2][:, lo:hi], False, hi == HEAD)
+        multiply(2, 0, head[:, 0:HEAD], last[:, 2 * C : 2 * C + HEAD], moved[2][:, 0:HEAD], False, True)
         gather(last[:, 2 * C + HEAD : 3 * C], 2, HEAD, C, T)
         multiply(2, 0, tail[:, HEAD:C], last[:, 2 * C + HEAD : 3 * C], moved[2][:, HEAD:C], False, True)
         nc.vector.tensor_tensor(dx[:, 0:HEAD], head[:, 0:HEAD], gate_t[:, 0:HEAD], MULT)
@@ -210,23 +210,27 @@ def tile_moe_bds_lin_none_kernel(tc, dy_words, dy_scales, w, gate, offs, pos1, p
             nc.scalar.activation(dst, dx[:].indirect(pos_t[:, lo // 16 : hi // 16]), COPY)
 
         t0, t1, t2, t3, t4 = STORES
-        second = keep.tile([P, T], F32, name="second")
-        first = keep.tile([P, t4 - t3], F32, name="first")
+        second = keep.tile([P, t3], F32, name="second")
+        first = keep.tile([P, BOTH], F32, name="first")
         part = keep.tile([P, T], F32, name="part")
         full = keep.tile([P, T], F32, name="full")
+
+        def start(lo, hi):
+            nc.vector.tensor_tensor(part[:, lo:hi], dx[:].indirect(pos1_t[:, lo // 16 : hi // 16]), ds[:, lo:hi], ADD)
 
         def finish(lo, hi):
             nc.vector.tensor_tensor(full[:, lo:hi], part[:, lo:hi], second[:, lo:hi], ADD)
             nc.sync.dma_start(out=out[:, lo:hi], in_=full[:, lo:hi])
 
         fetch(second[:, t0:t1], pos2_t, t0, t1)
-        fetch(first[:], pos1_t, t3, t4)
-        fetch(second[:, t1:t3], pos2_t, t1, t3)
-        fetch(second[:, t3:t4], pos2_t, t3, t4)
-        for lo, hi in ((t0, t1), (t1, t3)):
-            nc.vector.tensor_tensor(part[:, lo:hi], dx[:].indirect(pos1_t[:, lo // 16 : hi // 16]), ds[:, lo:hi], ADD)
+        fetch(first[:], pos1_t, t1, t1 + BOTH)
+        fetch(second[:, t2:t3], pos2_t, t2, t3)
+        fetch(second[:, t1:t2], pos2_t, t1, t2)
+        start(t0, t1)
+        start(t1 + BOTH, t4)
         finish(t0, t1)
-        nc.vector.tensor_tensor(part[:, t3:t4], first[:], ds[:, t3:t4], ADD)
-        finish(t1, t2)
+        nc.vector.tensor_tensor(part[:, t1 : t1 + BOTH], first[:], ds[:, t1 : t1 + BOTH], ADD)
         finish(t2, t3)
-        finish(t3, t4)
+        finish(t1, t2)
+        nc.vector.tensor_tensor(full[:, t3:t4], dx[:].indirect(pos2_t[:, t3 // 16 : t4 // 16]), part[:, t3:t4], ADD)
+        nc.sync.dma_start(out=out[:, t3:t4], in_=full[:, t3:t4])

@@ -21,7 +21,9 @@ P = 128
 PASSES = N // 512
 S = E * C
 SHARED = E
-ROW_OF_PASS = (32, 48, 112)
+ROW_OF_PASS = (80, 96, 112)
+COLUMN_OF_PASS = (2 * T, T, 0)
+SPARE = 384
 HEAD = 256
 STORES = (0, 384, 640, 896, 1024)
 BOTH = 128
@@ -39,20 +41,19 @@ def tile_moe_bds_lin_none_kernel(tc, dy_words, dy_scales, w, gate, offs, pos1, p
         pos2_t = keep.tile([P, T // 16], U16, name="pos2_t")
 
         scales_t = keep.tile([P, 2 * S], U8, name="scales_t", align_bytes=64)
-        words_t = keep.tile([P, (PASSES + 1) * T], I32, name="words_t", align_bytes=64)
-        nc.vector.memset(scales_t[0:32, 0:T].bitcast(I32), 0)
-        nc.vector.memset(scales_t[64:112, 0:T].bitcast(I32), 0)
+        words_t = keep.tile([P, PASSES * T + SPARE], I32, name="words_t", align_bytes=64)
+        nc.vector.memset(scales_t[0:80, 0:T].bitcast(I32), 0)
         nc.vector.memset(scales_t[:, T:].bitcast(I32), 0)
         nc.vector.memset(words_t[:, PASSES * T :], 0)
 
         sc32 = dy_scales.bitcast(I32)
         rows = sc32.rearrange("a f t -> (a f) t")
         nc.sync.dma_start(offs_t[:], offs)
-        nc.sync.dma_start(out=scales_t[32:64, 0:T].bitcast(I32), in_=rows[0:32, :])
+        nc.sync.dma_start(out=scales_t[80:112, 0:T].bitcast(I32), in_=rows[0:32, :])
         nc.sync.dma_start(out=scales_t[112:P, 0:T].bitcast(I32), in_=rows[32:48, :])
 
         def load_words(a):
-            nc.sync.dma_start(out=words_t[:, T * a : T * (a + 1)], in_=dy_words[a].rearrange("p t d -> p (t d)").bitcast(I32))
+            nc.sync.dma_start(out=words_t[:, COLUMN_OF_PASS[a] : COLUMN_OF_PASS[a] + T], in_=dy_words[a].rearrange("p t d -> p (t d)").bitcast(I32))
 
         raw = {}
 
@@ -71,12 +72,12 @@ def tile_moe_bds_lin_none_kernel(tc, dy_words, dy_scales, w, gate, offs, pos1, p
             load_w(name, [(a, e) for a in range(PASSES)], w[e].rearrange("(a p j) k -> p a (j k)", a=PASSES, j=4))
 
         load_words(2)
-        load_pass("pass2", 2, 1, 4)
         load_words(1)
+        load_pass("pass2", 2, 1, 4)
         load_pass("pass1", 1, 1, 4)
+        load_words(0)
         load_pass("pass0", 0, 2, 4)
         load_expert("shared", SHARED)
-        load_words(0)
         load_expert("expert0", 0)
         load_pass("last", 0, 1, 2)
 
@@ -138,7 +139,7 @@ def tile_moe_bds_lin_none_kernel(tc, dy_words, dy_scales, w, gate, offs, pos1, p
             nc.vector.quantize_mx(out=code_t[:].bitcast(E4M3), scales=scale_t[:], in_=grouped[:])
 
         def gather(dst, a, lo, hi, width):
-            window = words_t[:, T * a : T * a + width].bitcast(U32)
+            window = words_t[:, COLUMN_OF_PASS[a] : COLUMN_OF_PASS[a] + width].bitcast(U32)
             nc.vector.tensor_copy(dst, window.indirect(offs_t[:, lo // 16 : hi // 16]))
 
         def multiply(a, e, dst, rhs, rhs_scale, first, final):
@@ -162,7 +163,7 @@ def tile_moe_bds_lin_none_kernel(tc, dy_words, dy_scales, w, gate, offs, pos1, p
             for e in (2, 3):
                 multiply(a, e, acc[e][:], early[a][:, C * (e - 1) : C * e], moved[a][:, C * e : C * (e + 1)], a == 2, False)
         g0 = keep.tile([P, 2 * C], U32, name="g0", tag="pass0", align_bytes=64)
-        gather(g0[:], 0, 2 * C, S, S)
+        gather(g0[:], 0, 2 * C, S, T + SPARE)
         for e in (2, 3):
             multiply(0, e, acc[e][:], g0[:, C * (e - 2) : C * (e - 1)], moved[0][:, C * e : C * (e + 1)], False, True)
         quantise(["shared"])
@@ -189,8 +190,8 @@ def tile_moe_bds_lin_none_kernel(tc, dy_words, dy_scales, w, gate, offs, pos1, p
         for h, (lo, hi) in enumerate(((0, 256), (256, 512), (512, T))):
             acc_sh = psum.tile([P, 512], F32, name=f"acc_sh{h}", tag=f"twice{h}")
             for a in range(PASSES):
-                cols = slice(T * a + lo, T * a + hi)
-                multiply(a, SHARED, acc_sh[:, 0 : hi - lo], words_t[:, cols], shared_t[:, cols], a == 0, a == PASSES - 1)
+                words = words_t[:, COLUMN_OF_PASS[a] + lo : COLUMN_OF_PASS[a] + hi]
+                multiply(a, SHARED, acc_sh[:, 0 : hi - lo], words, shared_t[:, T * a + lo : T * a + hi], a == 0, a == PASSES - 1)
             nc.scalar.copy(out=ds[:, lo:hi], in_=acc_sh[:, 0 : hi - lo])
 
         head = psum.tile([P, C], F32, name="head", tag="twice0")

@@ -25,8 +25,7 @@ ROW_OF_PASS = (80, 96, 112)
 COLUMN_OF_PASS = (2 * T, T, 0)
 SPARE = 384
 HEAD = 256
-STORES = (0, 384, 640, 896, 1024)
-BOTH = 128
+STORES = (0, 448, 768, 1024)
 
 
 def tile_moe_bds_lin_none_kernel(tc, dy_words, dy_scales, w, gate, offs, pos1, pos2, out):
@@ -210,9 +209,9 @@ def tile_moe_bds_lin_none_kernel(tc, dy_words, dy_scales, w, gate, offs, pos1, p
         def fetch(dst, pos_t, lo, hi):
             nc.scalar.activation(dst, dx[:].indirect(pos_t[:, lo // 16 : hi // 16]), COPY)
 
-        t0, t1, t2, t3, t4 = STORES
-        second = keep.tile([P, t3], F32, name="second")
-        first = keep.tile([P, BOTH], F32, name="first")
+        t0, t1, t2, t3 = STORES
+        second = keep.tile([P, T], F32, name="second")
+        first = keep.tile([P, t3 - t2], F32, name="first")
         part = keep.tile([P, T], F32, name="part")
         full = keep.tile([P, T], F32, name="full")
 
@@ -224,14 +223,12 @@ def tile_moe_bds_lin_none_kernel(tc, dy_words, dy_scales, w, gate, offs, pos1, p
             nc.sync.dma_start(out=out[:, lo:hi], in_=full[:, lo:hi])
 
         fetch(second[:, t0:t1], pos2_t, t0, t1)
-        fetch(first[:], pos1_t, t1, t1 + BOTH)
-        fetch(second[:, t2:t3], pos2_t, t2, t3)
+        fetch(first[:], pos1_t, t2, t3)
         fetch(second[:, t1:t2], pos2_t, t1, t2)
+        fetch(second[:, t2:t3], pos2_t, t2, t3)
         start(t0, t1)
-        start(t1 + BOTH, t4)
+        start(t1, t2)
         finish(t0, t1)
-        nc.vector.tensor_tensor(part[:, t1 : t1 + BOTH], first[:], ds[:, t1 : t1 + BOTH], ADD)
-        finish(t2, t3)
+        nc.vector.tensor_tensor(part[:, t2:t3], first[:], ds[:, t2:t3], ADD)
         finish(t1, t2)
-        nc.vector.tensor_tensor(full[:, t3:t4], dx[:].indirect(pos2_t[:, t3 // 16 : t4 // 16]), part[:, t3:t4], ADD)
-        nc.sync.dma_start(out=out[:, t3:t4], in_=full[:, t3:t4])
+        finish(t2, t3)

@@ -67,17 +67,15 @@ def tile_moe_bds_lin_none_kernel(tc, dy_words, dy_scales, w, gate, offs, pos1, p
         def load_pass(name, a, lo, hi):
             load_w(name, [(a, e) for e in range(lo, hi)], w[lo:hi, 512 * a : 512 * (a + 1), :].rearrange("e (p j) k -> p e (j k)", j=4))
 
-        def load_expert(name, e):
-            load_w(name, [(a, e) for a in range(PASSES)], w[e].rearrange("(a p j) k -> p a (j k)", a=PASSES, j=4))
-
         load_words(2)
         load_words(1)
         load_pass("pass2", 2, 1, 4)
         load_pass("pass1", 1, 1, 4)
         load_words(0)
         load_pass("pass0", 0, 2, 4)
-        load_expert("shared", SHARED)
-        load_expert("expert0", 0)
+        for e in (SHARED, 0):
+            for a in range(PASSES):
+                load_pass(f"w{e}_{a}", a, e, e + 1)
         load_pass("last", 0, 1, 2)
 
         gb = keep.tile([P, S], U8, name="gb", align_bytes=64)
@@ -93,7 +91,7 @@ def tile_moe_bds_lin_none_kernel(tc, dy_words, dy_scales, w, gate, offs, pos1, p
 
         gate_t = keep.tile([P, S], F32, name="gate_t")
         nc.sync.dma_start(out=gate_t[:, 2 * C :], in_=gate[:, 2 * C :])
-        shared_t = keep.tile([P, PASSES * T], U8, name="shared_t", tag="shared", align_bytes=64)
+        shared_t = keep.tile([P, PASSES * T], U8, name="shared_t", tag="w4_0", align_bytes=64)
         for r in range(4):
             nc.sync.dma_start(
                 out=shared_t[r:P:32, :].bitcast(I32).rearrange("q (a t) -> q a t", a=PASSES),
@@ -165,10 +163,10 @@ def tile_moe_bds_lin_none_kernel(tc, dy_words, dy_scales, w, gate, offs, pos1, p
         gather(g0[:], 0, 2 * C, S, T + SPARE)
         for e in (2, 3):
             multiply(0, e, acc[e][:], g0[:, C * (e - 2) : C * (e - 1)], moved[0][:, C * e : C * (e + 1)], False, True)
-        quantise(["shared"])
-        quantise(["expert0", "last"])
+        quantise([f"w{SHARED}_{a}" for a in range(PASSES)])
+        quantise([f"w0_{a}" for a in range(PASSES)] + ["last"])
 
-        dx = keep.tile([P, S], F32, name="dx", tag="grouped_expert0", align_bytes=64)
+        dx = keep.tile([P, S], F32, name="dx", tag="grouped_w0_0", align_bytes=64)
         copied = late.tile([P, 3 * C + T], F32, name="copied", offset=4 * S, align_bytes=64)
         last = late.tile([P, S], U32, name="last_words", offset=0, align_bytes=64)
 

@@ -150,7 +150,7 @@ def tile_moe_bds_lin_none_kernel(tc, dy_words, dy_scales, w, gate, offs, pos1, p
                 stop=final,
             )
 
-        acc = {e: psum.tile([P, C], F32, name=f"acc{e}") for e in (2, 3, 1)}
+        acc = {e: psum.tile([P, C], F32, name=f"acc{e}", tag=f"acc{e}") for e in (2, 3)}
         early = {}
         for a in (2, 1):
             early[a] = keep.tile([P, 3 * C], U32, name=f"early{a}", align_bytes=64)
@@ -177,10 +177,11 @@ def tile_moe_bds_lin_none_kernel(tc, dy_words, dy_scales, w, gate, offs, pos1, p
 
         lend(2)
         lend(3)
-        gather(last[:, 3 * C :], 0, C, 2 * C, T)
-        multiply(0, 1, acc[1][:], last[:, 3 * C :], moved[0][:, C : 2 * C], True, False)
+        acc[1] = psum.tile([P, C], F32, name="acc1", tag="acc2")
         for a in (2, 1):
-            multiply(a, 1, acc[1][:], early[a][:, 0:C], moved[a][:, C : 2 * C], False, a == 1)
+            multiply(a, 1, acc[1][:], early[a][:, 0:C], moved[a][:, C : 2 * C], a == 2, False)
+        gather(last[:, 3 * C :], 0, C, 2 * C, T)
+        multiply(0, 1, acc[1][:], last[:, 3 * C :], moved[0][:, C : 2 * C], False, True)
         lend(1)
 
         ds = copied[:, 3 * C :]

@@ -24,7 +24,7 @@ SHARED = E
 ROW_OF_PASS = (80, 96, 112)
 COLUMN_OF_PASS = (2 * T, T, 0)
 SPARE = 384
-HEAD = 256
+HEAD = 384
 STORES = (0, 448, 768, 1024)
 
 
@@ -196,10 +196,11 @@ def tile_moe_bds_lin_none_kernel(tc, dy_words, dy_scales, w, gate, offs, pos1, p
         tail = psum.tile([P, C], F32, name="tail", tag="twice1")
         for a in (0, 1):
             gather(last[:, C * a : C * (a + 1)], a, 0, C, T)
-            multiply(a, 0, head[:, 0:HEAD], last[:, C * a : C * a + HEAD], moved[a][:, 0:HEAD], a == 0, False)
+            multiply(a, 0, head[:], last[:, C * a : C * (a + 1)], moved[a][:, 0:C], a == 0, False)
             multiply(a, 0, tail[:, HEAD:C], last[:, C * a + HEAD : C * (a + 1)], moved[a][:, HEAD:C], a == 0, False)
         gather(last[:, 2 * C : 2 * C + HEAD], 2, 0, HEAD, T)
-        multiply(2, 0, head[:, 0:HEAD], last[:, 2 * C : 2 * C + HEAD], moved[2][:, 0:HEAD], False, True)
+        for lo, hi in ((0, 256), (256, HEAD)):
+            multiply(2, 0, head[:, lo:hi], last[:, 2 * C + lo : 2 * C + hi], moved[2][:, lo:hi], False, hi == HEAD)
         gather(last[:, 2 * C + HEAD : 3 * C], 2, HEAD, C, T)
         multiply(2, 0, tail[:, HEAD:C], last[:, 2 * C + HEAD : 3 * C], moved[2][:, HEAD:C], False, True)
         nc.vector.tensor_tensor(dx[:, 0:HEAD], head[:, 0:HEAD], gate_t[:, 0:HEAD], MULT)

@@ -194,15 +194,16 @@ def tile_moe_bds_lin_none_kernel(tc, dy_words, dy_scales, w, gate, offs, pos1, p
 
         head = psum.tile([P, C], F32, name="head", tag="twice0")
         tail = psum.tile([P, C], F32, name="tail", tag="twice1")
-        for a in (0, 1):
-            gather(last[:, C * a : C * (a + 1)], a, 0, C, T)
-            multiply(a, 0, head[:], last[:, C * a : C * (a + 1)], moved[a][:, 0:C], a == 0, False)
-            multiply(a, 0, tail[:, HEAD:C], last[:, C * a + HEAD : C * (a + 1)], moved[a][:, HEAD:C], a == 0, False)
-        gather(last[:, 2 * C : 2 * C + HEAD], 2, 0, HEAD, T)
-        for lo, hi in ((0, 256), (256, HEAD)):
-            multiply(2, 0, head[:, lo:hi], last[:, 2 * C + lo : 2 * C + hi], moved[2][:, lo:hi], False, hi == HEAD)
-        gather(last[:, 2 * C + HEAD : 3 * C], 2, HEAD, C, T)
-        multiply(2, 0, tail[:, HEAD:C], last[:, 2 * C + HEAD : 3 * C], moved[2][:, HEAD:C], False, True)
+        gather(last[:, 0:C], 0, 0, C, T)
+        multiply(0, 0, head[:], last[:, 0:C], moved[0][:, 0:C], True, False)
+        multiply(0, 0, tail[:, HEAD:C], last[:, HEAD:C], moved[0][:, HEAD:C], True, False)
+        for a in (1, 2):
+            gather(last[:, C * a : C * a + HEAD], a, 0, HEAD, T)
+            for lo, hi in ((0, 256), (256, HEAD)):
+                multiply(a, 0, head[:, lo:hi], last[:, C * a + lo : C * a + hi], moved[a][:, lo:hi], False, (a, hi) == (2, HEAD))
+        for a in (1, 2):
+            gather(last[:, C * a + HEAD : C * (a + 1)], a, HEAD, C, T)
+            multiply(a, 0, tail[:, HEAD:C], last[:, C * a + HEAD : C * (a + 1)], moved[a][:, HEAD:C], False, a == 2)
         nc.vector.tensor_tensor(dx[:, 0:HEAD], head[:, 0:HEAD], gate_t[:, 0:HEAD], MULT)
         nc.vector.tensor_tensor(dx[:, HEAD:C], tail[:, HEAD:C], gate_t[:, HEAD:C], MULT)
 

@@ -21,7 +21,7 @@ P = 128
 PASSES = N // 512
 S = E * C
 SHARED = E
-ROW_OF_PASS = (80, 96, 112)
+ROW_OF_PASS = (48, 64, 80)
 COLUMN_OF_PASS = (2 * T, T, 0)
 SPARE = 384
 HEAD = 384
@@ -41,15 +41,16 @@ def tile_moe_bds_lin_none_kernel(tc, dy_words, dy_scales, w, gate, offs, pos1, p
 
         scales_t = keep.tile([P, 2 * S], U8, name="scales_t", align_bytes=64)
         words_t = keep.tile([P, PASSES * T + SPARE], I32, name="words_t", align_bytes=64)
-        nc.vector.memset(scales_t[0:80, 0:T].bitcast(I32), 0)
+        nc.vector.memset(scales_t[0:48, 0:T].bitcast(I32), 0)
+        nc.vector.memset(scales_t[96:P, 0:T].bitcast(I32), 0)
         nc.vector.memset(scales_t[:, T:].bitcast(I32), 0)
         nc.vector.memset(words_t[:, PASSES * T :], 0)
 
         sc32 = dy_scales.bitcast(I32)
         rows = sc32.rearrange("a f t -> (a f) t")
         nc.sync.dma_start(offs_t[:], offs)
-        nc.sync.dma_start(out=scales_t[80:112, 0:T].bitcast(I32), in_=rows[0:32, :])
-        nc.sync.dma_start(out=scales_t[112:P, 0:T].bitcast(I32), in_=rows[32:48, :])
+        nc.sync.dma_start(out=scales_t[48:80, 0:T].bitcast(I32), in_=rows[0:32, :])
+        nc.sync.dma_start(out=scales_t[80:96, 0:T].bitcast(I32), in_=rows[32:48, :])
 
         def load_words(a):
             nc.sync.dma_start(out=words_t[:, COLUMN_OF_PASS[a] : COLUMN_OF_PASS[a] + T], in_=dy_words[a].rearrange("p t d -> p (t d)").bitcast(I32))

@@ -196,7 +196,8 @@ def tile_moe_bds_lin_none_kernel(tc, dy_words, dy_scales, w, gate, offs, pos1, p
         head = psum.tile([P, C], F32, name="head", tag="twice0")
         tail = psum.tile([P, C], F32, name="tail", tag="twice1")
         gather(last[:, 0:C], 0, 0, C, T)
-        multiply(0, 0, head[:], last[:, 0:C], moved[0][:, 0:C], True, False)
+        for lo, hi in ((0, 256), (256, HEAD)):
+            multiply(0, 0, head[:, lo:hi], last[:, lo:hi], moved[0][:, lo:hi], lo == 0, False)
         multiply(0, 0, tail[:, HEAD:C], last[:, HEAD:C], moved[0][:, HEAD:C], True, False)
         for a in (1, 2):
             gather(last[:, C * a : C * a + HEAD], a, 0, HEAD, T)

@@ -41,10 +41,17 @@ def tile_moe_bds_lin_none_kernel(tc, dy_words, dy_scales, w, gate, offs, pos1, p
 
         scales_t = keep.tile([P, 2 * S], U8, name="scales_t", align_bytes=64)
         words_t = keep.tile([P, PASSES * T + SPARE], I32, name="words_t", align_bytes=64)
+        scratch = keep.tile([P, 16], F32, name="scratch", align_bytes=64)
+        nc.vector.memset(scratch[:], 0.0)
         nc.vector.memset(scales_t[0:48, 0:T].bitcast(I32), 0)
         nc.vector.memset(scales_t[96:P, 0:T].bitcast(I32), 0)
         nc.vector.memset(scales_t[:, T:].bitcast(I32), 0)
         nc.vector.memset(words_t[:, PASSES * T :], 0)
+
+        warm_copy = keep.tile([P, 64], U8, name="warm_copy", align_bytes=64)
+        warm_sum = keep.tile([P, 16], F32, name="warm_sum", align_bytes=64)
+        nc.vector.tensor_copy(warm_copy[:], scratch[:].bitcast(U8))
+        nc.vector.tensor_tensor(warm_sum[:], scratch[:], scratch[:], ADD)
 
         sc32 = dy_scales.bitcast(I32)
         rows = sc32.rearrange("a f t -> (a f) t")

@@ -23,7 +23,7 @@ S = E * C
 SHARED = E
 ROW_OF_PASS = (48, 64, 80)
 COLUMN_OF_PASS = (2 * T, T, 0)
-SPARE = 384
+SPARE = T
 HEAD = 384
 STORES = (0, 448, 768, 1024)
 
@@ -66,7 +66,7 @@ def tile_moe_bds_lin_none_kernel(tc, dy_words, dy_scales, w, gate, offs, pos1, p
 
         def load_w(name, units, source):
             if name == "last":
-                tile = late.tile([P, len(units) * 512], F32, name=name, offset=4 * S - 1024, align_bytes=64)
+                tile = late.tile([P, len(units) * 512], F32, name=name, offset=0, align_bytes=64)
             else:
                 tile = keep.tile([P, len(units) * 512], F32, name=name, tag=name, align_bytes=64)
             raw[name] = (tile, units)
@@ -158,42 +158,37 @@ def tile_moe_bds_lin_none_kernel(tc, dy_words, dy_scales, w, gate, offs, pos1, p
                 stop=final,
             )
 
-        acc = {e: psum.tile([P, C], F32, name=f"acc{e}", tag=f"acc{e}") for e in (2, 3)}
+        acc = {e: psum.tile([P, C], F32, name=f"acc{e}", tag=f"acc{e}") for e in (2, 3, 1)}
         early = {}
         for a in (2, 1):
             early[a] = keep.tile([P, 3 * C], U32, name=f"early{a}", align_bytes=64)
             gather(early[a][:], a, C, S, S)
         quantise(["pass2", "pass1", "pass0"])
+
+        def early_pass(a, e):
+            multiply(a, e, acc[e][:], early[a][:, C * (e - 1) : C * e], moved[a][:, C * e : C * (e + 1)], a == 2, a == 0)
+
         for a in (2, 1):
-            for e in (2, 3):
-                multiply(a, e, acc[e][:], early[a][:, C * (e - 1) : C * e], moved[a][:, C * e : C * (e + 1)], a == 2, False)
-        g0 = keep.tile([P, 2 * C], U32, name="g0", tag="pass0", align_bytes=64)
-        gather(g0[:], 0, 2 * C, S, T + SPARE)
-        for e in (2, 3):
-            multiply(0, e, acc[e][:], g0[:, C * (e - 2) : C * (e - 1)], moved[0][:, C * e : C * (e + 1)], False, True)
+            for e in (2, 3, 1):
+                early_pass(a, e)
+        early[0] = keep.tile([P, 3 * C], U32, name="early0", tag="pass0", align_bytes=64)
+        gather(early[0][:], 0, C, S, S)
         quantise([f"w{SHARED}_{a}" for a in range(PASSES)])
         quantise([f"w0_{a}" for a in range(PASSES)] + ["last"])
+        for e in (2, 3, 1):
+            early_pass(0, e)
 
         dx = keep.tile([P, S], F32, name="dx", tag="grouped_w0_0", align_bytes=64)
-        copied = late.tile([P, 3 * C + T], F32, name="copied", offset=4 * S, align_bytes=64)
-        last = late.tile([P, S], U32, name="last_words", offset=0, align_bytes=64)
+        copied = late.tile([P, 3 * C + STORES[2]], F32, name="copied", offset=4 * 3 * C, align_bytes=64)
+        last = late.tile([P, 3 * C], U32, name="last_words", offset=0, align_bytes=64)
 
-        def lend(e):
+        for e in (2, 3, 1):
             cols = slice(C * e, C * (e + 1))
             nc.scalar.copy(out=copied[:, C * (e - 1) : C * e], in_=acc[e][:])
             nc.gpsimd.tensor_tensor(dx[:, cols], copied[:, C * (e - 1) : C * e], gate_t[:, cols], MULT)
 
-        lend(2)
-        lend(3)
-        acc[1] = psum.tile([P, C], F32, name="acc1", tag="acc2")
-        for a in (2, 1):
-            multiply(a, 1, acc[1][:], early[a][:, 0:C], moved[a][:, C : 2 * C], a == 2, False)
-        gather(last[:, 3 * C :], 0, C, 2 * C, T)
-        multiply(0, 1, acc[1][:], last[:, 3 * C :], moved[0][:, C : 2 * C], False, True)
-        lend(1)
-
         ds = copied[:, 3 * C :]
-        for h, (lo, hi) in enumerate(((0, 256), (256, 512), (512, T))):
+        for h, (lo, hi) in enumerate(((0, 256), (256, 512), (512, STORES[2]))):
             acc_sh = psum.tile([P, 512], F32, name=f"acc_sh{h}", tag=f"twice{h}")
             for a in range(PASSES):
                 words = words_t[:, COLUMN_OF_PASS[a] + lo : COLUMN_OF_PASS[a] + hi]
@@ -206,6 +201,10 @@ def tile_moe_bds_lin_none_kernel(tc, dy_words, dy_scales, w, gate, offs, pos1, p
         for lo, hi in ((0, 256), (256, HEAD)):
             multiply(0, 0, head[:, lo:hi], last[:, lo:hi], moved[0][:, lo:hi], lo == 0, False)
         multiply(0, 0, tail[:, HEAD:C], last[:, HEAD:C], moved[0][:, HEAD:C], True, False)
+        ds_last = tail[:, 0 : T - STORES[2]]
+        for a in range(PASSES):
+            words = words_t[:, COLUMN_OF_PASS[a] + STORES[2] : COLUMN_OF_PASS[a] + T]
+            multiply(a, SHARED, ds_last, words, shared_t[:, T * a + STORES[2] : T * (a + 1)], False, False)
         for a in (1, 2):
             gather(last[:, C * a : C * a + HEAD], a, 0, HEAD, T)
             for lo, hi in ((0, 256), (256, HEAD)):
@@ -239,6 +238,6 @@ def tile_moe_bds_lin_none_kernel(tc, dy_words, dy_scales, w, gate, offs, pos1, p
         start(t0, t1)
         start(t1, t2)
         finish(t0, t1)
-        nc.vector.tensor_tensor(part[:, t2:t3], first[:], ds[:, t2:t3], ADD)
+        nc.vector.tensor_tensor(part[:, t2:t3], first[:], ds_last, ADD)
         finish(t1, t2)
         finish(t2, t3)

from contextlib import ExitStack

import concourse.mybir as mybir

K, T, E, C, N = 128, 1024, 4, 512, 1536
FLOPS = 2 * N * K * (E * C + T)

F32 = mybir.dt.float32
BF16 = mybir.dt.bfloat16
I32 = mybir.dt.int32
U32 = mybir.dt.uint32
U16 = mybir.dt.uint16
U8 = mybir.dt.uint8
E4M3 = mybir.dt.float8_e4m3fn_x4
E5M2 = mybir.dt.float8_e5m2_x4
ADD = mybir.AluOpType.add
MULT = mybir.AluOpType.mult
COPY = mybir.ActivationFunctionType.Copy

P = 128
PASSES = N // 512
S = E * C
SHARED = E
ROW_OF_PASS = (48, 64, 80)
COLUMN_OF_PASS = (2 * T, T, 0)
SPARE = T
HEAD = 384
STORES = (0, 448, 768, 1024)


def tile_moe_bds_lin_none_kernel(tc, dy_words, dy_scales, w, gate, offs, pos1, pos2, out):
    nc = tc.nc
    with ExitStack() as ctx:
        keep = ctx.enter_context(tc.tile_pool(name="keep", bufs=1))
        late = ctx.enter_context(tc.tile_pool(name="late", bufs=1))
        psum = ctx.enter_context(tc.psum_pool(name="psum", bufs=1))

        offs_t = keep.tile([P, S // 16], U16, name="offs_t")
        pos1_t = keep.tile([P, T // 16], U16, name="pos1_t")
        pos2_t = keep.tile([P, T // 16], U16, name="pos2_t")

        scales_t = keep.tile([P, 2 * S], U8, name="scales_t", align_bytes=64)
        words_t = keep.tile([P, PASSES * T + SPARE], I32, name="words_t", align_bytes=64)
        scratch = keep.tile([P, 16], F32, name="scratch", align_bytes=64)
        nc.vector.memset(scratch[:], 0.0)
        nc.vector.memset(scales_t[0:48, 0:T].bitcast(I32), 0)
        nc.vector.memset(scales_t[96:P, 0:T].bitcast(I32), 0)
        nc.vector.memset(scales_t[:, T:].bitcast(I32), 0)
        nc.vector.memset(words_t[:, PASSES * T :], 0)

        warm_copy = keep.tile([P, 64], U8, name="warm_copy", align_bytes=64)
        warm_sum = keep.tile([P, 16], F32, name="warm_sum", align_bytes=64)
        nc.vector.tensor_copy(warm_copy[:], scratch[:].bitcast(U8))
        nc.vector.tensor_tensor(warm_sum[:], scratch[:], scratch[:], ADD)

        sc32 = dy_scales.bitcast(I32)
        rows = sc32.rearrange("a f t -> (a f) t")
        nc.sync.dma_start(offs_t[:], offs)
        nc.sync.dma_start(out=scales_t[48:80, 0:T].bitcast(I32), in_=rows[0:32, :])
        nc.sync.dma_start(out=scales_t[80:96, 0:T].bitcast(I32), in_=rows[32:48, :])

        def load_words(a):
            nc.sync.dma_start(out=words_t[:, COLUMN_OF_PASS[a] : COLUMN_OF_PASS[a] + T], in_=dy_words[a].rearrange("p t d -> p (t d)").bitcast(I32))

        raw = {}

        def load_w(name, units, source):
            if name == "last":
                tile = late.tile([P, len(units) * 512], F32, name=name, offset=0, align_bytes=64)
            else:
                tile = keep.tile([P, len(units) * 512], F32, name=name, tag=name, align_bytes=64)
            raw[name] = (tile, units)
            nc.sync.dma_start(out=tile[:].rearrange("p (u x) -> p u x", x=512), in_=source)

        def load_pass(name, a, lo, hi):
            load_w(name, [(a, e) for e in range(lo, hi)], w[lo:hi, 512 * a : 512 * (a + 1), :].rearrange("e (p j) k -> p e (j k)", j=4))

        load_words(2)
        load_words(1)
        load_pass("pass2", 2, 1, 4)
        load_pass("pass1", 1, 1, 4)
        load_words(0)
        load_pass("pass0", 0, 2, 4)
        for e in (SHARED, 0):
            for a in range(PASSES):
                load_pass(f"w{e}_{a}", a, e, e + 1)
        load_pass("last", 0, 1, 2)

        gb = keep.tile([P, S], U8, name="gb", align_bytes=64)
        nc.vector.tensor_copy(gb[:], scales_t[:].indirect(offs_t[:]))

        planes12 = keep.tile([P, 2 * S], U8, name="planes12", tag="pass2", align_bytes=64)
        plane0 = keep.tile([P, S], U8, name="plane0", tag="pass1", align_bytes=64)
        moved = [plane0[:], planes12[:, 0:S], planes12[:, S : 2 * S]]
        for a in (2, 1, 0):
            for r in range(4):
                first = ROW_OF_PASS[a] + r
                nc.sync.dma_start(out=moved[a][r:P:32, :].bitcast(I32), in_=gb[first : first + 13 : 4, :].bitcast(I32))

        gate_t = keep.tile([P, S], F32, name="gate_t")
        nc.sync.dma_start(out=gate_t[:, 2 * C :], in_=gate[:, 2 * C :])
        shared_t = keep.tile([P, PASSES * T], U8, name="shared_t", tag="w4_0", align_bytes=64)
        for r in range(4):
            nc.sync.dma_start(
                out=shared_t[r:P:32, :].bitcast(I32).rearrange("q (a t) -> q a t", a=PASSES),
                in_=sc32[:, r:16:4, :].rearrange("a q t -> q a t"),
            )
        nc.sync.dma_start(out=gate_t[:, 0 : 2 * C], in_=gate[:, 0 : 2 * C])
        nc.sync.dma_start(pos1_t[:], pos1)
        nc.sync.dma_start(pos2_t[:], pos2)

        codes = {}
        wsc = {}

        def interleave(dst, src, by_activation):
            if by_activation:
                nc.scalar.activation(
                    dst.rearrange("p (c i j) -> p c j i", i=4, j=4), src.rearrange("p (j c i) -> p c j i", j=4, i=4), COPY
                )
            else:
                nc.scalar.copy(
                    out=dst.rearrange("p (e c i j) -> p e c j i", c=K // 4, i=4, j=4),
                    in_=src.rearrange("p (e j c i) -> p e c j i", j=4, c=K // 4, i=4),
                )

        def quantise(names):
            n = sum(len(raw[name][1]) for name in names)
            grouped = keep.tile([P, n * 512], BF16, name=f"grouped_{names[0]}", tag=f"grouped_{names[0]}", align_bytes=64)
            code_t = keep.tile([P, n * K], U32, name=f"codes_{names[0]}", align_bytes=64)
            scale_t = keep.tile([P, n * K], U8, name=f"wsc_{names[0]}", align_bytes=64)
            u = 0
            for name in names:
                tile, units = raw[name]
                lo, hi = 512 * u, 512 * (u + len(units))
                if name == "pass2":
                    interleave(grouped[:, lo : lo + 512], tile[:, 0:512], True)
                    interleave(grouped[:, lo + 512 : hi], tile[:, 512:], False)
                else:
                    interleave(grouped[:, lo:hi], tile[:], False)
                for unit in units:
                    codes[unit] = code_t[:, K * u : K * (u + 1)]
                    wsc[unit] = scale_t[:, K * u : K * (u + 1)]
                    u = u + 1
            nc.vector.quantize_mx(out=code_t[:].bitcast(E4M3), scales=scale_t[:], in_=grouped[:])

        def gather(dst, a, lo, hi, width):
            window = words_t[:, COLUMN_OF_PASS[a] : COLUMN_OF_PASS[a] + width].bitcast(U32)
            nc.vector.tensor_copy(dst, window.indirect(offs_t[:, lo // 16 : hi // 16]))

        def multiply(a, e, dst, rhs, rhs_scale, first, final):
            nc.tensor.matmul_mx(
                out=dst,
                lhsT=codes[a, e].bitcast(E4M3),
                lhsT_scale=wsc[a, e],
                rhs=rhs.bitcast(E5M2),
                rhs_scale=rhs_scale,
                start=first,
                stop=final,
            )

        acc = {e: psum.tile([P, C], F32, name=f"acc{e}", tag=f"acc{e}") for e in (2, 3, 1)}
        early = {}
        for a in (2, 1):
            early[a] = keep.tile([P, 3 * C], U32, name=f"early{a}", align_bytes=64)
            gather(early[a][:], a, C, S, S)
        quantise(["pass2", "pass1", "pass0"])

        def early_pass(a, e):
            multiply(a, e, acc[e][:], early[a][:, C * (e - 1) : C * e], moved[a][:, C * e : C * (e + 1)], a == 2, a == 0)

        for a in (2, 1):
            for e in (2, 3, 1):
                early_pass(a, e)
        early[0] = keep.tile([P, 3 * C], U32, name="early0", tag="pass0", align_bytes=64)
        gather(early[0][:], 0, C, S, S)
        quantise([f"w{SHARED}_{a}" for a in range(PASSES)])
        quantise([f"w0_{a}" for a in range(PASSES)] + ["last"])
        for e in (2, 3, 1):
            early_pass(0, e)

        dx = keep.tile([P, S], F32, name="dx", tag="grouped_w0_0", align_bytes=64)
        copied = late.tile([P, 3 * C + STORES[2]], F32, name="copied", offset=4 * 3 * C, align_bytes=64)
        last = late.tile([P, 3 * C], U32, name="last_words", offset=0, align_bytes=64)

        for e in (2, 3, 1):
            cols = slice(C * e, C * (e + 1))
            nc.scalar.copy(out=copied[:, C * (e - 1) : C * e], in_=acc[e][:])
            nc.gpsimd.tensor_tensor(dx[:, cols], copied[:, C * (e - 1) : C * e], gate_t[:, cols], MULT)

        ds = copied[:, 3 * C :]
        for h, (lo, hi) in enumerate(((0, 256), (256, 512), (512, STORES[2]))):
            acc_sh = psum.tile([P, 512], F32, name=f"acc_sh{h}", tag=f"twice{h}")
            for a in range(PASSES):
                words = words_t[:, COLUMN_OF_PASS[a] + lo : COLUMN_OF_PASS[a] + hi]
                multiply(a, SHARED, acc_sh[:, 0 : hi - lo], words, shared_t[:, T * a + lo : T * a + hi], a == 0, a == PASSES - 1)
            nc.scalar.copy(out=ds[:, lo:hi], in_=acc_sh[:, 0 : hi - lo])

        head = psum.tile([P, C], F32, name="head", tag="twice0")
        tail = psum.tile([P, C], F32, name="tail", tag="twice1")
        gather(last[:, 0:C], 0, 0, C, T)
        for lo, hi in ((0, 256), (256, HEAD)):
            multiply(0, 0, head[:, lo:hi], last[:, lo:hi], moved[0][:, lo:hi], lo == 0, False)
        multiply(0, 0, tail[:, HEAD:C], last[:, HEAD:C], moved[0][:, HEAD:C], True, False)
        ds_last = tail[:, 0 : T - STORES[2]]
        for a in range(PASSES):
            words = words_t[:, COLUMN_OF_PASS[a] + STORES[2] : COLUMN_OF_PASS[a] + T]
            multiply(a, SHARED, ds_last, words, shared_t[:, T * a + STORES[2] : T * (a + 1)], False, False)
        for a in (1, 2):
            gather(last[:, C * a : C * a + HEAD], a, 0, HEAD, T)
            for lo, hi in ((0, 256), (256, HEAD)):
                multiply(a, 0, head[:, lo:hi], last[:, C * a + lo : C * a + hi], moved[a][:, lo:hi], False, (a, hi) == (2, HEAD))
        for a in (1, 2):
            gather(last[:, C * a + HEAD : C * (a + 1)], a, HEAD, C, T)
            multiply(a, 0, tail[:, HEAD:C], last[:, C * a + HEAD : C * (a + 1)], moved[a][:, HEAD:C], False, a == 2)
        nc.vector.tensor_tensor(dx[:, 0:HEAD], head[:, 0:HEAD], gate_t[:, 0:HEAD], MULT)
        nc.vector.tensor_tensor(dx[:, HEAD:C], tail[:, HEAD:C], gate_t[:, HEAD:C], MULT)

        def fetch(dst, pos_t, lo, hi):
            nc.scalar.activation(dst, dx[:].indirect(pos_t[:, lo // 16 : hi // 16]), COPY)

        t0, t1, t2, t3 = STORES
        second = keep.tile([P, T], F32, name="second")
        first = keep.tile([P, t3 - t2], F32, name="first")
        part = keep.tile([P, T], F32, name="part")
        full = keep.tile([P, T], F32, name="full")

        def start(lo, hi):
            nc.vector.tensor_tensor(part[:, lo:hi], dx[:].indirect(pos1_t[:, lo // 16 : hi // 16]), ds[:, lo:hi], ADD)

        def finish(lo, hi):
            nc.vector.tensor_tensor(full[:, lo:hi], part[:, lo:hi], second[:, lo:hi], ADD)
            nc.sync.dma_start(out=out[:, lo:hi], in_=full[:, lo:hi])

        fetch(second[:, t0:t1], pos2_t, t0, t1)
        fetch(first[:], pos1_t, t2, t3)
        fetch(second[:, t1:t2], pos2_t, t1, t2)
        fetch(second[:, t2:t3], pos2_t, t2, t3)
        start(t0, t1)
        start(t1, t2)
        finish(t0, t1)
        nc.vector.tensor_tensor(part[:, t2:t3], first[:], ds_last, ADD)
        finish(t1, t2)
        finish(t2, t3)
